import numpy as np
import ml_dtypes


def mxq(x, axis, fmt="e4m3"):
    dtype, down = {"e4m3": (ml_dtypes.float8_e4m3fn, 7), "e5m2": (ml_dtypes.float8_e5m2, 14)}[fmt]
    v = np.moveaxis(np.asarray(x, np.float32).astype(ml_dtypes.bfloat16).astype(np.float64), axis, -1)
    blocks = v.reshape(v.shape[:-1] + (-1, 32))
    amax = np.abs(blocks).max(-1, keepdims=True)
    byte = np.maximum(np.where(amax > 0, np.frexp(amax)[1] - 1 + 127, 0) - down, 1)
    scale = np.exp2(byte - 127.0)
    codes = (blocks / scale).astype(np.float32).astype(dtype).astype(np.float64)
    return np.moveaxis((codes * scale).reshape(v.shape), -1, axis)


WIDE = False


def mx_kscale(k):
    if not WIDE:
        return np.ones(k)
    levels = np.array([10, -10, 5, -5, 0])
    if k % 512:
        return np.exp2(np.random.permutation(np.resize(levels, k // 32))).repeat(32)
    a = np.empty((k // 512, 16))
    for p in range(k // 512):
        a[p, :8] = np.random.permutation(np.resize(levels, 8))
        for g in range(8):
            far = levels[np.abs(levels - a[p, g]) >= 10]
            a[p, g + 8] = far[np.random.randint(len(far))]
    return np.exp2(a.ravel()).repeat(32)


def f64(x):
    return np.asarray(x).astype(np.float64)


def striped(idx):
    return np.tile(idx.reshape(-1, 16).T, (8, 1)).astype(np.uint16)


def unstriped(offs):
    return offs[:16].T.reshape(-1).astype(np.int64)


def pack_weight(w):
    k, n = w.shape
    w = f64(np.asarray(w, np.float32).astype(ml_dtypes.bfloat16)).reshape(k // 32, 32, n)
    amax = np.abs(w).max(1)
    byte = np.clip(np.where(amax > 0, np.frexp(amax)[1] - 1 + 127 - 7, 1), 1, 254)
    scaled = (w * np.exp2(127.0 - byte)[:, None, :]).reshape(k, n).astype(np.float32)
    words = np.ascontiguousarray(scaled.reshape(k // 512, 128, 4, n).transpose(0, 1, 3, 2)).astype(ml_dtypes.float8_e4m3fn).view(np.uint8)
    return words, np.ascontiguousarray(byte.astype(np.uint8).reshape(k // 512, 16, n))


def unpack_weight(words, scales):
    g, p, n, _ = words.shape
    vals = np.ascontiguousarray(words).view(ml_dtypes.float8_e4m3fn).astype(np.float64) * np.repeat(np.exp2(scales.astype(np.float64) - 127.0), 8, axis=1)[..., None]
    return vals.transpose(0, 1, 3, 2).reshape(g * 512, n)


def silu(v):
    return v / (1.0 + np.exp(-np.maximum(v, -700.0)))


K, T, S, H, N, R = 512, 4096, 1024, 512, 128, 512


def setup_inputs():
    n = np.random.standard_normal
    s = mx_kscale(K)[:, None]
    u = mx_kscale(H)
    packed_xT = pack_weight(n((K, T)) * s)
    return {
        "x_words": packed_xT[0],
        "x_scales": packed_xT[1],
        "w1": (n((K, H)) / np.sqrt(K) / s * u).astype(np.float32),
        "w2": (n((H, N)) / np.sqrt(H) / u[:, None]).astype(np.float32),
        "w3": (n((K, N)) / np.sqrt(K) / s).astype(np.float32),
        "ld": (np.random.uniform(0.2, 1.5, (H, R))).astype(np.float32),
        "lb": (np.random.uniform(0.2, 1.5, (N, R))).astype(np.float32),
        "offs": striped(np.random.permutation(T)[:S]),
        "ad": striped(np.random.permutation(np.concatenate([np.arange(R), np.random.randint(0, R, S - R)]))),
    }


def reference(x_words, x_scales, w1, w2, w3, ld, lb, offs, ad):
    xq = unpack_weight(x_words, x_scales)[:, unstriped(offs)]
    ee = mxq(f64(w3), 0, "e4m3").T @ xq
    y = mxq(f64(w1), 0, "e4m3").T @ xq
    h = f64(ld)[:, unstriped(ad)] * y
    rr = mxq(f64(w2), 0, "e4m3").T @ mxq(h, 0, "e4m3")
    return silu(ee + f64(lb)[:, unstriped(ad)] * rr)

@@ -1,0 +1,237 @@
+from contextlib import ExitStack
+
+import concourse.mybir as mybir
+
+K, T, S, H, N, R = 512, 4096, 1024, 512, 128, 512
+FLOPS = 2 * S * (K * N + K * H + H * N)
+
+F32 = mybir.dt.float32
+BF16 = mybir.dt.bfloat16
+I32 = mybir.dt.int32
+U32 = mybir.dt.uint32
+U16 = mybir.dt.uint16
+U8 = mybir.dt.uint8
+FP8X4 = mybir.dt.float8_e4m3fn_x4
+MULT = mybir.AluOpType.mult
+ADD = mybir.AluOpType.add
+SILU = mybir.ActivationFunctionType.Silu
+
+P = 128
+PACK = 4
+LIST = 16
+HALF = 512
+CHUNK = 128
+SPARE = 32
+RUN = 4
+W1_PIECES = 4
+FUSED_GROUP = 256
+GROUPS = (256, 256, 256, 128, 128)
+
+
+def tile_picked_yvera_silu_p_kernel(
+    tc, x_words, x_scales, w1, w2, w3, ld, lb, offs, ad, out
+):
+    nc = tc.nc
+    with ExitStack() as ctx:
+        lists = ctx.enter_context(tc.tile_pool(name="lists", bufs=1))
+        keep = ctx.enter_context(tc.tile_pool(name="keep", bufs=1))
+        psum = ctx.enter_context(tc.psum_pool(name="psum", bufs=1))
+
+        ad_list = lists.tile([P, S // LIST], U16, name="ad_list")
+        token_list = lists.tile([P, S // LIST], U16, name="token_list")
+        ld_tables = [keep.tile([P, R + SPARE], F32, name=f"ld_table{t}") for t in range(PACK)]
+        lb_table = keep.tile([P, R + SPARE], F32, name="lb_table")
+        word_table = keep.tile([P, T], I32, name="word_table")
+        scale_table = keep.tile([P, T], U8, name="scale_table")
+        piece = H // W1_PIECES
+        w1_raw = [keep.tile([P, PACK, piece], F32, name=f"w1_raw{i}") for i in range(W1_PIECES)]
+        w2_raw = keep.tile([P, PACK, N], F32, name="w2_raw")
+        w3_raw = keep.tile([P, PACK, N], F32, name="w3_raw")
+
+        def entries(index_list, first, count):
+            return index_list[:, first // LIST : (first + count) // LIST]
+
+        warm_in = keep.tile([P, 1], F32, name="warm_in")
+        warm_out = keep.tile([P, 1], F32, name="warm_out")
+        nc.gpsimd.memset(warm_in[:], 0.0)
+        nc.scalar.activation(warm_out[:], warm_in[:], SILU)
+
+        for table in ld_tables + [lb_table]:
+            nc.vector.memset(table[:, R:], 0.0)
+        nc.vector.memset(scale_table[:].bitcast(I32), 0)
+
+        ld_rows = ld.rearrange("(p t) r -> p t r", t=PACK)
+        w1_rows = w1.rearrange("(p j) c -> p j c", j=PACK)
+        nc.sync.dma_start(ad_list[:], ad)
+        for t in range(PACK):
+            nc.sync.dma_start(ld_tables[t][:, :R], ld_rows[:, t, :])
+        nc.sync.dma_start(lb_table[:, :R], lb)
+        nc.sync.dma_start(token_list[:], offs)
+        for q in range(4):
+            nc.sync.dma_start(
+                scale_table[32 * q : 32 * q + 4, :].bitcast(I32),
+                x_scales[0, 4 * q : 4 * q + 4, :].bitcast(I32),
+            )
+        nc.sync.dma_start(word_table[:], x_words[0].rearrange("p c t -> p (c t)").bitcast(I32))
+        for i in range(W1_PIECES):
+            nc.sync.dma_start(w1_raw[i][:], w1_rows[:, :, i * piece : (i + 1) * piece])
+        nc.sync.dma_start(w3_raw[:], w3.rearrange("(p j) c -> p j c", j=PACK))
+        nc.sync.dma_start(w2_raw[:], w2.rearrange("(p j) c -> p j c", j=PACK))
+
+        ld_picked = keep.tile([P, PACK, HALF], F32, name="ld_picked")
+        for t in range(PACK):
+            nc.vector.tensor_copy(
+                ld_picked[:, t, :], ld_tables[t][:].indirect(entries(ad_list, HALF, HALF))
+            )
+        lb_picked = [keep.tile([P, HALF], F32, name="lb_picked0")]
+        nc.vector.tensor_copy(lb_picked[0][:], lb_table[:].indirect(entries(ad_list, 0, HALF)))
+        ld_woven = keep.tile([P, HALF, PACK], F32, name="ld_woven")
+        nc.scalar.copy(
+            ld_woven[:].rearrange("p (c i) t -> p c t i", i=RUN),
+            ld_picked[:].rearrange("p t (c i) -> p c t i", i=RUN),
+        )
+
+        x_codes = []
+        x_bytes = []
+        for half in range(S // HALF):
+            picked = entries(token_list, half * HALF, HALF)
+            codes = keep.tile([P, HALF], U32, name=f"x_codes{half}", align_bytes=64)
+            scale_bytes = keep.tile([P, HALF], U8, name=f"x_bytes{half}", align_bytes=64)
+            nc.vector.tensor_copy(codes[:], word_table[:].bitcast(U32).indirect(picked))
+            nc.vector.tensor_copy(scale_bytes[:], scale_table[:].indirect(picked))
+            x_codes.append(codes)
+            x_bytes.append(scale_bytes)
+
+        w1_bf = keep.tile([P, PACK * H], BF16, name="w1_bf", tag="w1_then_lb", align_bytes=64)
+        w1_dealt = w1_bf[:].rearrange("p (t m j) -> p m t j", t=PACK, j=PACK)
+        for i in range(W1_PIECES):
+            nc.scalar.copy(
+                w1_dealt[:, i * piece // PACK : (i + 1) * piece // PACK],
+                w1_raw[i][:].rearrange("p j (m t) -> p m t j", t=PACK),
+            )
+        w1_codes = keep.tile([P, H], U32, name="w1_codes", align_bytes=64)
+        w1_scales = keep.tile([P, H], U8, name="w1_scales", align_bytes=64)
+        nc.vector.quantize_mx(w1_codes[:].bitcast(FP8X4), w1_scales[:], w1_bf[:])
+
+        lb_picked.append(
+            keep.tile([P, HALF], F32, name="lb_picked1", tag="w1_then_lb", align_bytes=64)
+        )
+        nc.vector.tensor_copy(lb_picked[1][:], lb_table[:].indirect(entries(ad_list, HALF, HALF)))
+
+        w32_bf = keep.tile([P, 2, N, PACK], BF16, name="w32_bf", align_bytes=64)
+        for slot, raw in enumerate((w3_raw, w2_raw)):
+            nc.scalar.copy(
+                w32_bf[:, slot].rearrange("p (c i) j -> p c j i", i=RUN),
+                raw[:].rearrange("p j (c i) -> p c j i", i=RUN),
+            )
+        w32_codes = keep.tile([P, 2 * N], U32, name="w32_codes", align_bytes=64)
+        w32_scales = keep.tile([P, 2 * N], U8, name="w32_scales", align_bytes=64)
+        nc.vector.quantize_mx(
+            w32_codes[:].bitcast(FP8X4), w32_scales[:], w32_bf[:].rearrange("p w c j -> p (w c j)")
+        )
+
+        def first_product(target, t, half, cols):
+            nc.tensor.matmul_mx(
+                target,
+                lhsT=w1_codes[:, t * P : (t + 1) * P].bitcast(FP8X4),
+                lhsT_scale=w1_scales[:, t * P : (t + 1) * P],
+                rhs=x_codes[half][:, cols].bitcast(FP8X4),
+                rhs_scale=x_bytes[half][:, cols],
+                start=True,
+                stop=True,
+            )
+
+        y_sb = keep.tile([P, PACK, HALF], F32, name="y_sb", tag="y_then_h", align_bytes=64)
+        for t in range(PACK):
+            y = psum.tile([P, HALF], F32, name="y_wide", tag="y", bufs=4)
+            first_product(y[:], t, 0, slice(0, HALF))
+            nc.scalar.copy(y_sb[:, t, :], y[:])
+
+        frozen = []
+        for half in range(S // HALF):
+            ee = psum.tile([P, HALF], F32, name=f"ee{half}")
+            nc.tensor.matmul_mx(
+                ee[:],
+                lhsT=w32_codes[:, :N].bitcast(FP8X4),
+                lhsT_scale=w32_scales[:, :N],
+                rhs=x_codes[half][:].bitcast(FP8X4),
+                rhs_scale=x_bytes[half][:],
+                start=True,
+                stop=True,
+            )
+            frozen.append(ee)
+
+        h_first = keep.tile([P, HALF, PACK], BF16, name="h_first", align_bytes=64)
+        for first in range(0, HALF, FUSED_GROUP):
+            cols = slice(first, first + FUSED_GROUP)
+            h_planes = keep.tile([P, PACK, FUSED_GROUP], F32, name=f"h_planes{first}")
+            for t in range(PACK):
+                nc.vector.tensor_tensor(
+                    h_planes[:, t, :],
+                    ld_tables[t][:].indirect(entries(ad_list, first, FUSED_GROUP)),
+                    y_sb[:, t, cols],
+                    MULT,
+                )
+            nc.scalar.copy(
+                h_first[:, cols, :].rearrange("p (c i) t -> p c t i", i=RUN),
+                h_planes[:].rearrange("p t (c i) -> p c t i", i=RUN),
+            )
+
+        h_second = keep.tile([P, HALF, PACK], BF16, name="h_second", tag="y_then_h", align_bytes=64)
+
+        def hidden(first):
+            cols = slice(first, first + CHUNK)
+            y = psum.tile([P, PACK, CHUNK], F32, name="y_chunk", tag="y", bufs=4)
+            for t in range(PACK):
+                first_product(y[:, t, :], t, 1, cols)
+            nc.vector.tensor_tensor(
+                h_second[:, cols, :], y[:].rearrange("p t n -> p n t"), ld_woven[:, cols, :], MULT
+            )
+
+        def second(first, width):
+            half, col = divmod(first, HALF)
+            h_bf = (h_first, h_second)[half][:, col : col + width, :]
+            h_codes = keep.tile([P, width], U32, name=f"h_codes{first}", align_bytes=64)
+            h_scales = keep.tile([P, width], U8, name=f"h_scales{first}", align_bytes=64)
+            nc.vector.quantize_mx(
+                h_codes[:].bitcast(FP8X4), h_scales[:], h_bf.rearrange("p n t -> p (n t)")
+            )
+            rr = psum.tile([P, width], F32, name="rr", tag="rr", bufs=2)
+            nc.tensor.matmul_mx(
+                rr[:],
+                lhsT=w32_codes[:, N:].bitcast(FP8X4),
+                lhsT_scale=w32_scales[:, N:],
+                rhs=h_codes[:].bitcast(FP8X4),
+                rhs_scale=h_scales[:],
+                start=True,
+                stop=True,
+            )
+            return rr
+
+        def scaled(first, width, rr):
+            half, col = divmod(first, HALF)
+            term = keep.tile([P, width], F32, name=f"term{first}")
+            nc.vector.tensor_tensor(term[:], rr[:], lb_picked[half][:, col : col + width], MULT)
+            return term
+
+        def finish(first, width, term):
+            half, col = divmod(first, HALF)
+            total = keep.tile([P, width], F32, name=f"total{first}")
+            nc.vector.tensor_tensor(total[:], frozen[half][:, col : col + width], term[:], ADD)
+            result = keep.tile([P, width], F32, name=f"result{first}")
+            nc.scalar.activation(result[:], total[:], SILU)
+            nc.sync.dma_start(out[:, first : first + width], result[:])
+
+        starts = [sum(GROUPS[:g]) for g in range(len(GROUPS))]
+        chunks = list(range(0, HALF, CHUNK))
+        rr_tiles = {}
+        terms = {}
+        for step in range(len(GROUPS) + 2):
+            if step < len(chunks):
+                hidden(chunks[step])
+            if 0 <= step - 2:
+                finish(starts[step - 2], GROUPS[step - 2], terms[step - 2])
+            if 0 <= step - 1 < len(GROUPS):
+                terms[step - 1] = scaled(starts[step - 1], GROUPS[step - 1], rr_tiles[step - 1])
+            if step < len(GROUPS):
+                rr_tiles[step] = second(starts[step], GROUPS[step])

@@ -1,6 +1,7 @@
 from contextlib import ExitStack
 
 import concourse.mybir as mybir
+from concourse.masks import make_identity
 
 K, T, S, H, N, R = 512, 4096, 1024, 512, 128, 512
 FLOPS = 2 * S * (K * N + K * H + H * N)
@@ -21,11 +22,12 @@ PACK = 4
 LIST = 16
 HALF = 512
 CHUNK = 128
-SPARE = 32
 RUN = 4
-W1_PIECES = 4
-FUSED_GROUP = 256
-GROUPS = (256, 256, 256, 128, 128)
+FUSED_GROUPS = (256, 128)
+EARLY_GROUPS = (256, 256, 128)
+FUSED = sum(FUSED_GROUPS)
+EARLY = sum(EARLY_GROUPS)
+SPARE = EARLY - R + 32
 
 
 def tile_picked_yvera_silu_p_kernel(
@@ -43,8 +45,7 @@ def tile_picked_yvera_silu_p_kernel(
         lb_table = keep.tile([P, R + SPARE], F32, name="lb_table")
         word_table = keep.tile([P, T], I32, name="word_table")
         scale_table = keep.tile([P, T], U8, name="scale_table")
-        piece = H // W1_PIECES
-        w1_raw = [keep.tile([P, PACK, piece], F32, name=f"w1_raw{i}") for i in range(W1_PIECES)]
+        w1_raw = keep.tile([P, PACK, H], F32, name="w1_raw", tag="w1_then_ld")
         w2_raw = keep.tile([P, PACK, N], F32, name="w2_raw")
         w3_raw = keep.tile([P, PACK, N], F32, name="w3_raw")
 
@@ -55,68 +56,105 @@ def tile_picked_yvera_silu_p_kernel(
         warm_out = keep.tile([P, 1], F32, name="warm_out")
         nc.gpsimd.memset(warm_in[:], 0.0)
         nc.scalar.activation(warm_out[:], warm_in[:], SILU)
+        identity = keep.tile([P, P], F32, name="identity")
+        make_identity(nc, identity[:])
 
         for table in ld_tables + [lb_table]:
             nc.vector.memset(table[:, R:], 0.0)
         nc.vector.memset(scale_table[:].bitcast(I32), 0)
 
         ld_rows = ld.rearrange("(p t) r -> p t r", t=PACK)
-        w1_rows = w1.rearrange("(p j) c -> p j c", j=PACK)
+        scale_rows = x_scales[0].rearrange("(q r) c -> r q c", r=4)
         nc.sync.dma_start(ad_list[:], ad)
         for t in range(PACK):
             nc.sync.dma_start(ld_tables[t][:, :R], ld_rows[:, t, :])
+        nc.sync.dma_start(w1_raw[:], w1.rearrange("(p j) c -> p j c", j=PACK))
         nc.sync.dma_start(lb_table[:, :R], lb)
         nc.sync.dma_start(token_list[:], offs)
-        for q in range(4):
-            nc.sync.dma_start(
-                scale_table[32 * q : 32 * q + 4, :].bitcast(I32),
-                x_scales[0, 4 * q : 4 * q + 4, :].bitcast(I32),
-            )
+        for r in range(4):
+            nc.sync.dma_start(scale_table[r:P:32, :].bitcast(I32), scale_rows[r].bitcast(I32))
         nc.sync.dma_start(word_table[:], x_words[0].rearrange("p c t -> p (c t)").bitcast(I32))
-        for i in range(W1_PIECES):
-            nc.sync.dma_start(w1_raw[i][:], w1_rows[:, :, i * piece : (i + 1) * piece])
         nc.sync.dma_start(w3_raw[:], w3.rearrange("(p j) c -> p j c", j=PACK))
         nc.sync.dma_start(w2_raw[:], w2.rearrange("(p j) c -> p j c", j=PACK))
 
-        ld_picked = keep.tile([P, PACK, HALF], F32, name="ld_picked")
+        ld_picked = keep.tile([P, PACK, EARLY], F32, name="ld_picked")
         for t in range(PACK):
             nc.vector.tensor_copy(
-                ld_picked[:, t, :], ld_tables[t][:].indirect(entries(ad_list, HALF, HALF))
+                ld_picked[:, t, :], ld_tables[t][:].indirect(entries(ad_list, FUSED, EARLY))
             )
-        lb_picked = [keep.tile([P, HALF], F32, name="lb_picked0")]
-        nc.vector.tensor_copy(lb_picked[0][:], lb_table[:].indirect(entries(ad_list, 0, HALF)))
-        ld_woven = keep.tile([P, HALF, PACK], F32, name="ld_woven")
+        lb_picked = keep.tile([P, S], F32, name="lb_picked")
+        for first in range(0, S, HALF):
+            nc.vector.tensor_copy(
+                lb_picked[:, first : first + HALF],
+                lb_table[:].indirect(entries(ad_list, first, HALF)),
+            )
+
+        x_bytes = []
+        for half in range(S // HALF):
+            scale_bytes = keep.tile([P, HALF], U8, name=f"x_bytes{half}", align_bytes=64)
+            nc.vector.tensor_copy(
+                scale_bytes[:], scale_table[:].indirect(entries(token_list, half * HALF, HALF))
+            )
+            x_bytes.append(scale_bytes)
+
+        w1_bf = keep.tile([P, PACK * H], BF16, name="w1_bf", align_bytes=64)
+        nc.scalar.copy(
+            w1_bf[:].rearrange("p (t m j) -> p m t j", t=PACK, j=PACK),
+            w1_raw[:].rearrange("p j (m t) -> p m t j", t=PACK),
+        )
+        w1_codes = keep.tile([P, H], U32, name="w1_codes", align_bytes=64)
+        w1_scales = keep.tile([P, H], U8, name="w1_scales", align_bytes=64)
+        nc.vector.quantize_mx(w1_codes[:].bitcast(FP8X4), w1_scales[:], w1_bf[:])
+
+        ld_woven = keep.tile([P, EARLY, PACK], F32, name="ld_woven", tag="w1_then_ld")
         nc.scalar.copy(
             ld_woven[:].rearrange("p (c i) t -> p c t i", i=RUN),
             ld_picked[:].rearrange("p t (c i) -> p c t i", i=RUN),
         )
 
-        x_codes = []
-        x_bytes = []
+        lb_turned = keep.tile([P, S // CHUNK, N], F32, name="lb_turned")
+        per_bank = HALF // CHUNK
         for half in range(S // HALF):
-            picked = entries(token_list, half * HALF, HALF)
+            bank = psum.tile([P, per_bank, N], F32, name="lb_bank", tag="total", bufs=2)
+            for c in range(per_bank):
+                first = half * HALF + c * CHUNK
+                nc.tensor.transpose(bank[:, c, :], lb_picked[:, first : first + CHUNK], identity[:])
+            nc.scalar.copy(lb_turned[:, half * per_bank : (half + 1) * per_bank, :], bank[:])
+
+        x_codes = []
+        for half in range(S // HALF):
             codes = keep.tile([P, HALF], U32, name=f"x_codes{half}", align_bytes=64)
-            scale_bytes = keep.tile([P, HALF], U8, name=f"x_bytes{half}", align_bytes=64)
-            nc.vector.tensor_copy(codes[:], word_table[:].bitcast(U32).indirect(picked))
-            nc.vector.tensor_copy(scale_bytes[:], scale_table[:].indirect(picked))
-            x_codes.append(codes)
-            x_bytes.append(scale_bytes)
-
-        w1_bf = keep.tile([P, PACK * H], BF16, name="w1_bf", tag="w1_then_lb", align_bytes=64)
-        w1_dealt = w1_bf[:].rearrange("p (t m j) -> p m t j", t=PACK, j=PACK)
-        for i in range(W1_PIECES):
-            nc.scalar.copy(
-                w1_dealt[:, i * piece // PACK : (i + 1) * piece // PACK],
-                w1_raw[i][:].rearrange("p j (m t) -> p m t j", t=PACK),
+            nc.vector.tensor_copy(
+                codes[:],
+                word_table[:].bitcast(U32).indirect(entries(token_list, half * HALF, HALF)),
             )
-        w1_codes = keep.tile([P, H], U32, name="w1_codes", align_bytes=64)
-        w1_scales = keep.tile([P, H], U8, name="w1_scales", align_bytes=64)
-        nc.vector.quantize_mx(w1_codes[:].bitcast(FP8X4), w1_scales[:], w1_bf[:])
+            x_codes.append(codes)
 
-        lb_picked.append(
-            keep.tile([P, HALF], F32, name="lb_picked1", tag="w1_then_lb", align_bytes=64)
-        )
-        nc.vector.tensor_copy(lb_picked[1][:], lb_table[:].indirect(entries(ad_list, HALF, HALF)))
+        def picked_x(first, width):
+            half, col = divmod(first, HALF)
+            return x_codes[half][:, col : col + width].bitcast(FP8X4), x_bytes[half][:, col : col + width]
+
+        def first_product(target, t, first, width):
+            codes, scale_bytes = picked_x(first, width)
+            nc.tensor.matmul_mx(
+                target,
+                lhsT=w1_codes[:, t * P : (t + 1) * P].bitcast(FP8X4),
+                lhsT_scale=w1_scales[:, t * P : (t + 1) * P],
+                rhs=codes,
+                rhs_scale=scale_bytes,
+                start=True,
+                stop=True,
+            )
+
+        groups = FUSED_GROUPS + EARLY_GROUPS
+        starts = [sum(groups[:g]) for g in range(len(groups))]
+
+        y_sb = keep.tile([P, PACK, FUSED], F32, name="y_sb", tag="y_then_h", align_bytes=64)
+        for t in range(PACK):
+            y = psum.tile([P, FUSED], F32, name="y_wide", tag="y", bufs=4)
+            for first, width in zip(starts, FUSED_GROUPS):
+                first_product(y[:, first : first + width], t, first, width)
+            nc.scalar.copy(y_sb[:, t, :], y[:])
 
         w32_bf = keep.tile([P, 2, N, PACK], BF16, name="w32_bf", align_bytes=64)
         for slot, raw in enumerate((w3_raw, w2_raw)):
@@ -130,108 +168,101 @@ def tile_picked_yvera_silu_p_kernel(
             w32_codes[:].bitcast(FP8X4), w32_scales[:], w32_bf[:].rearrange("p w c j -> p (w c j)")
         )
 
-        def first_product(target, t, half, cols):
-            nc.tensor.matmul_mx(
-                target,
-                lhsT=w1_codes[:, t * P : (t + 1) * P].bitcast(FP8X4),
-                lhsT_scale=w1_scales[:, t * P : (t + 1) * P],
-                rhs=x_codes[half][:, cols].bitcast(FP8X4),
-                rhs_scale=x_bytes[half][:, cols],
-                start=True,
-                stop=True,
-            )
-
-        y_sb = keep.tile([P, PACK, HALF], F32, name="y_sb", tag="y_then_h", align_bytes=64)
-        for t in range(PACK):
-            y = psum.tile([P, HALF], F32, name="y_wide", tag="y", bufs=4)
-            first_product(y[:], t, 0, slice(0, HALF))
-            nc.scalar.copy(y_sb[:, t, :], y[:])
-
-        frozen = []
-        for half in range(S // HALF):
-            ee = psum.tile([P, HALF], F32, name=f"ee{half}")
-            nc.tensor.matmul_mx(
-                ee[:],
-                lhsT=w32_codes[:, :N].bitcast(FP8X4),
-                lhsT_scale=w32_scales[:, :N],
-                rhs=x_codes[half][:].bitcast(FP8X4),
-                rhs_scale=x_bytes[half][:],
-                start=True,
-                stop=True,
-            )
-            frozen.append(ee)
-
-        h_first = keep.tile([P, HALF, PACK], BF16, name="h_first", align_bytes=64)
-        for first in range(0, HALF, FUSED_GROUP):
-            cols = slice(first, first + FUSED_GROUP)
-            h_planes = keep.tile([P, PACK, FUSED_GROUP], F32, name=f"h_planes{first}")
+        h_fused = keep.tile([P, FUSED, PACK], BF16, name="h_fused", align_bytes=64)
+        for first, width in zip(starts, FUSED_GROUPS):
+            cols = slice(first, first + width)
+            h_planes = keep.tile([P, PACK, width], F32, name=f"h_planes{first}")
             for t in range(PACK):
                 nc.vector.tensor_tensor(
                     h_planes[:, t, :],
-                    ld_tables[t][:].indirect(entries(ad_list, first, FUSED_GROUP)),
+                    ld_tables[t][:].indirect(entries(ad_list, first, width)),
                     y_sb[:, t, cols],
                     MULT,
                 )
             nc.scalar.copy(
-                h_first[:, cols, :].rearrange("p (c i) t -> p c t i", i=RUN),
+                h_fused[:, cols, :].rearrange("p (c i) t -> p c t i", i=RUN),
                 h_planes[:].rearrange("p t (c i) -> p c t i", i=RUN),
             )
 
-        h_second = keep.tile([P, HALF, PACK], BF16, name="h_second", tag="y_then_h", align_bytes=64)
+        ee_turned = keep.tile([P, S // CHUNK, N], F32, name="ee_turned")
+        for half in range(S // HALF):
+            bank = psum.tile([P, per_bank, N], F32, name="ee_bank", tag="rr", bufs=2)
+            for c in range(per_bank):
+                codes, scale_bytes = picked_x(half * HALF + c * CHUNK, CHUNK)
+                nc.tensor.matmul_mx(
+                    bank[:, c, :],
+                    lhsT=codes,
+                    lhsT_scale=scale_bytes,
+                    rhs=w32_codes[:, :N].bitcast(FP8X4),
+                    rhs_scale=w32_scales[:, :N],
+                    start=True,
+                    stop=True,
+                )
+            nc.scalar.copy(ee_turned[:, half * per_bank : (half + 1) * per_bank, :], bank[:])
+
+        h_early = keep.tile([P, EARLY, PACK], BF16, name="h_early", tag="y_then_h", align_bytes=64)
 
         def hidden(first):
-            cols = slice(first, first + CHUNK)
+            cols = slice(first - FUSED, first - FUSED + CHUNK)
             y = psum.tile([P, PACK, CHUNK], F32, name="y_chunk", tag="y", bufs=4)
             for t in range(PACK):
-                first_product(y[:, t, :], t, 1, cols)
+                first_product(y[:, t, :], t, first, CHUNK)
             nc.vector.tensor_tensor(
-                h_second[:, cols, :], y[:].rearrange("p t n -> p n t"), ld_woven[:, cols, :], MULT
+                h_early[:, cols, :], y[:].rearrange("p t n -> p n t"), ld_woven[:, cols, :], MULT
             )
 
         def second(first, width):
-            half, col = divmod(first, HALF)
-            h_bf = (h_first, h_second)[half][:, col : col + width, :]
+            if first < FUSED:
+                h_bf = h_fused[:, first : first + width, :]
+            else:
+                h_bf = h_early[:, first - FUSED : first - FUSED + width, :]
             h_codes = keep.tile([P, width], U32, name=f"h_codes{first}", align_bytes=64)
             h_scales = keep.tile([P, width], U8, name=f"h_scales{first}", align_bytes=64)
             nc.vector.quantize_mx(
                 h_codes[:].bitcast(FP8X4), h_scales[:], h_bf.rearrange("p n t -> p (n t)")
             )
-            rr = psum.tile([P, width], F32, name="rr", tag="rr", bufs=2)
-            nc.tensor.matmul_mx(
-                rr[:],
-                lhsT=w32_codes[:, N:].bitcast(FP8X4),
-                lhsT_scale=w32_scales[:, N:],
-                rhs=h_codes[:].bitcast(FP8X4),
-                rhs_scale=h_scales[:],
-                start=True,
-                stop=True,
-            )
+            rr = psum.tile([P, width // CHUNK, N], F32, name="rr", tag="rr", bufs=2)
+            for c in range(width // CHUNK):
+                nc.tensor.matmul_mx(
+                    rr[:, c, :],
+                    lhsT=h_codes[:, c * CHUNK : (c + 1) * CHUNK].bitcast(FP8X4),
+                    lhsT_scale=h_scales[:, c * CHUNK : (c + 1) * CHUNK],
+                    rhs=w32_codes[:, N:].bitcast(FP8X4),
+                    rhs_scale=w32_scales[:, N:],
+                    start=True,
+                    stop=True,
+                )
             return rr
 
         def scaled(first, width, rr):
-            half, col = divmod(first, HALF)
-            term = keep.tile([P, width], F32, name=f"term{first}")
-            nc.vector.tensor_tensor(term[:], rr[:], lb_picked[half][:, col : col + width], MULT)
+            term = keep.tile([P, width // CHUNK, N], F32, name=f"term{first}")
+            chunks = slice(first // CHUNK, (first + width) // CHUNK)
+            nc.vector.tensor_tensor(term[:], rr[:], lb_turned[:, chunks, :], MULT)
             return term
 
         def finish(first, width, term):
-            half, col = divmod(first, HALF)
-            total = keep.tile([P, width], F32, name=f"total{first}")
-            nc.vector.tensor_tensor(total[:], frozen[half][:, col : col + width], term[:], ADD)
+            total = psum.tile([P, width], F32, name="total", tag="total", bufs=2)
+            for c in range(width // CHUNK):
+                target = total[:, c * CHUNK : (c + 1) * CHUNK]
+                for turn, addend in enumerate((ee_turned[:, first // CHUNK + c, :], term[:, c, :])):
+                    nc.tensor.matmul(
+                        target, lhsT=addend, rhs=identity[:], is_transpose=True, start=turn == 0, stop=turn == 1
+                    )
             result = keep.tile([P, width], F32, name=f"result{first}")
             nc.scalar.activation(result[:], total[:], SILU)
             nc.sync.dma_start(out[:, first : first + width], result[:])
 
-        starts = [sum(GROUPS[:g]) for g in range(len(GROUPS))]
-        chunks = list(range(0, HALF, CHUNK))
+        chunks = list(range(FUSED, S, CHUNK))
+        made = FUSED
         rr_tiles = {}
         terms = {}
-        for step in range(len(GROUPS) + 2):
-            if step < len(chunks):
-                hidden(chunks[step])
+        for step in range(len(groups) + 2):
+            while made < S and (made < FUSED + CHUNK * (step + 1) or made < sum(groups[: step + 1]) + CHUNK):
+                hidden(made)
+                made = made + CHUNK
             if 0 <= step - 2:
-                finish(starts[step - 2], GROUPS[step - 2], terms[step - 2])
-            if 0 <= step - 1 < len(GROUPS):
-                terms[step - 1] = scaled(starts[step - 1], GROUPS[step - 1], rr_tiles[step - 1])
-            if step < len(GROUPS):
-                rr_tiles[step] = second(starts[step], GROUPS[step])
+                finish(starts[step - 2], groups[step - 2], terms[step - 2])
+            if 0 <= step - 1 < len(groups):
+                terms[step - 1] = scaled(starts[step - 1], groups[step - 1], rr_tiles[step - 1])
+            if step < len(groups):
+                rr_tiles[step] = second(starts[step], groups[step])

@@ -23,11 +23,12 @@ LIST = 16
 HALF = 512
 CHUNK = 128
 RUN = 4
-FUSED_GROUPS = (256, 128)
-EARLY_GROUPS = (256, 256, 128)
+FUSED_GROUPS = (256, 256)
+EARLY_GROUPS = (256, 128, 128)
 FUSED = sum(FUSED_GROUPS)
 EARLY = sum(EARLY_GROUPS)
-SPARE = EARLY - R + 32
+SPARE = max(EARLY, FUSED, R) - R + 32
+LB_WINDOW = 1376
 
 
 def tile_picked_yvera_silu_p_kernel(
@@ -42,60 +43,56 @@ def tile_picked_yvera_silu_p_kernel(
         ad_list = lists.tile([P, S // LIST], U16, name="ad_list")
         token_list = lists.tile([P, S // LIST], U16, name="token_list")
         ld_tables = [keep.tile([P, R + SPARE], F32, name=f"ld_table{t}") for t in range(PACK)]
-        lb_table = keep.tile([P, R + SPARE], F32, name="lb_table")
+        lb_table = keep.tile([P, LB_WINDOW], F32, name="lb_table")
         word_table = keep.tile([P, T], I32, name="word_table")
-        scale_table = keep.tile([P, T], U8, name="scale_table")
+        scale_table = keep.tile([P, T], U8, name="scale_table", tag="scales_then_w")
         w1_raw = keep.tile([P, PACK, H], F32, name="w1_raw", tag="w1_then_ld")
-        w2_raw = keep.tile([P, PACK, N], F32, name="w2_raw")
-        w3_raw = keep.tile([P, PACK, N], F32, name="w3_raw")
 
         def entries(index_list, first, count):
             return index_list[:, first // LIST : (first + count) // LIST]
 
+        nc.gpsimd.memset(scale_table[:].bitcast(I32), 0)
         warm_in = keep.tile([P, 1], F32, name="warm_in")
         warm_out = keep.tile([P, 1], F32, name="warm_out")
-        nc.gpsimd.memset(warm_in[:], 0.0)
+        nc.vector.memset(warm_in[:], 0.0)
         nc.scalar.activation(warm_out[:], warm_in[:], SILU)
         identity = keep.tile([P, P], F32, name="identity")
         make_identity(nc, identity[:])
 
-        for table in ld_tables + [lb_table]:
+        nc.vector.memset(lb_table[:, R:], 0.0)
+        for table in ld_tables:
             nc.vector.memset(table[:, R:], 0.0)
-        nc.vector.memset(scale_table[:].bitcast(I32), 0)
 
         ld_rows = ld.rearrange("(p t) r -> p t r", t=PACK)
-        scale_rows = x_scales[0].rearrange("(q r) c -> r q c", r=4)
+        nc.sync.dma_start(ld_tables[0][:, :R], ld_rows[:, 0, :])
         nc.sync.dma_start(ad_list[:], ad)
-        for t in range(PACK):
+        nc.sync.dma_start(token_list[:], offs)
+        nc.sync.dma_start(scale_table[0:P:8, :].bitcast(I32), x_scales[0].bitcast(I32))
+        for t in range(1, PACK):
             nc.sync.dma_start(ld_tables[t][:, :R], ld_rows[:, t, :])
         nc.sync.dma_start(w1_raw[:], w1.rearrange("(p j) c -> p j c", j=PACK))
         nc.sync.dma_start(lb_table[:, :R], lb)
-        nc.sync.dma_start(token_list[:], offs)
-        for r in range(4):
-            nc.sync.dma_start(scale_table[r:P:32, :].bitcast(I32), scale_rows[r].bitcast(I32))
         nc.sync.dma_start(word_table[:], x_words[0].rearrange("p c t -> p (c t)").bitcast(I32))
-        nc.sync.dma_start(w3_raw[:], w3.rearrange("(p j) c -> p j c", j=PACK))
-        nc.sync.dma_start(w2_raw[:], w2.rearrange("(p j) c -> p j c", j=PACK))
 
-        ld_picked = keep.tile([P, PACK, EARLY], F32, name="ld_picked")
+        spread_bytes = keep.tile([P, S], U8, name="spread_bytes")
+        nc.vector.tensor_copy(spread_bytes[:], scale_table[:].indirect(token_list[:]))
+        x_bytes = keep.tile([P, S], U8, name="x_bytes", align_bytes=64)
+        nc.vector.memset(x_bytes[:].bitcast(I32), 0)
+        for r in range(4):
+            nc.sync.dma_start(
+                x_bytes[r:P:32, :].bitcast(I32), spread_bytes[8 * r : P : 32, :].bitcast(I32)
+            )
+        w32_raw = keep.tile([P, 2, PACK, N], F32, name="w32_raw", tag="scales_then_w")
+        for slot, weight in enumerate((w3, w2)):
+            nc.sync.dma_start(w32_raw[:, slot], weight.rearrange("(p j) c -> p j c", j=PACK))
+
+        ld_picked = keep.tile([P, PACK, EARLY], F32, name="ld_picked", tag="ld_then_lb")
         for t in range(PACK):
             nc.vector.tensor_copy(
                 ld_picked[:, t, :], ld_tables[t][:].indirect(entries(ad_list, FUSED, EARLY))
             )
         lb_picked = keep.tile([P, S], F32, name="lb_picked")
-        for first in range(0, S, HALF):
-            nc.vector.tensor_copy(
-                lb_picked[:, first : first + HALF],
-                lb_table[:].indirect(entries(ad_list, first, HALF)),
-            )
-
-        x_bytes = []
-        for half in range(S // HALF):
-            scale_bytes = keep.tile([P, HALF], U8, name=f"x_bytes{half}", align_bytes=64)
-            nc.vector.tensor_copy(
-                scale_bytes[:], scale_table[:].indirect(entries(token_list, half * HALF, HALF))
-            )
-            x_bytes.append(scale_bytes)
+        nc.vector.tensor_copy(lb_picked[:], lb_table[:].indirect(ad_list[:]))
 
         w1_bf = keep.tile([P, PACK * H], BF16, name="w1_bf", align_bytes=64)
         nc.scalar.copy(
@@ -112,7 +109,7 @@ def tile_picked_yvera_silu_p_kernel(
             ld_picked[:].rearrange("p t (c i) -> p c t i", i=RUN),
         )
 
-        lb_turned = keep.tile([P, S // CHUNK, N], F32, name="lb_turned")
+        lb_turned = keep.tile([P, S // CHUNK, N], F32, name="lb_turned", tag="ld_then_lb")
         per_bank = HALF // CHUNK
         for half in range(S // HALF):
             bank = psum.tile([P, per_bank, N], F32, name="lb_bank", tag="total", bufs=2)
@@ -132,7 +129,7 @@ def tile_picked_yvera_silu_p_kernel(
 
         def picked_x(first, width):
             half, col = divmod(first, HALF)
-            return x_codes[half][:, col : col + width].bitcast(FP8X4), x_bytes[half][:, col : col + width]
+            return x_codes[half][:, col : col + width].bitcast(FP8X4), x_bytes[:, first : first + width]
 
         def first_product(target, t, first, width):
             codes, scale_bytes = picked_x(first, width)
@@ -150,28 +147,32 @@ def tile_picked_yvera_silu_p_kernel(
         starts = [sum(groups[:g]) for g in range(len(groups))]
 
         y_sb = keep.tile([P, PACK, FUSED], F32, name="y_sb", tag="y_then_h", align_bytes=64)
-        for t in range(PACK):
-            y = psum.tile([P, FUSED], F32, name="y_wide", tag="y", bufs=4)
-            for first, width in zip(starts, FUSED_GROUPS):
-                first_product(y[:, first : first + width], t, first, width)
-            nc.scalar.copy(y_sb[:, t, :], y[:])
+        for first, width in zip(starts, FUSED_GROUPS):
+            for t in range(PACK):
+                y = psum.tile([P, width], F32, name="y_plane", tag="y", bufs=4)
+                first_product(y[:], t, first, width)
+                nc.scalar.copy(y_sb[:, t, first : first + width], y[:])
 
-        w32_bf = keep.tile([P, 2, N, PACK], BF16, name="w32_bf", align_bytes=64)
-        for slot, raw in enumerate((w3_raw, w2_raw)):
+        h_stage = keep.tile([P, PACK * FUSED], F32, name="h_stage", align_bytes=64)
+        w32_flat = h_stage[:, PACK * FUSED - PACK * N :].bitcast(BF16)
+        w32_bf = w32_flat.rearrange("p (w c j) -> p w c j", w=2, j=PACK)
+        for slot in range(2):
             nc.scalar.copy(
                 w32_bf[:, slot].rearrange("p (c i) j -> p c j i", i=RUN),
-                raw[:].rearrange("p j (c i) -> p c j i", i=RUN),
+                w32_raw[:, slot].rearrange("p j (c i) -> p c j i", i=RUN),
             )
         w32_codes = keep.tile([P, 2 * N], U32, name="w32_codes", align_bytes=64)
         w32_scales = keep.tile([P, 2 * N], U8, name="w32_scales", align_bytes=64)
         nc.vector.quantize_mx(
-            w32_codes[:].bitcast(FP8X4), w32_scales[:], w32_bf[:].rearrange("p w c j -> p (w c j)")
+            w32_codes[:].bitcast(FP8X4), w32_scales[:], w32_flat
         )
 
         h_fused = keep.tile([P, FUSED, PACK], BF16, name="h_fused", align_bytes=64)
         for first, width in zip(starts, FUSED_GROUPS):
             cols = slice(first, first + width)
-            h_planes = keep.tile([P, PACK, width], F32, name=f"h_planes{first}")
+            h_planes = h_stage[:, PACK * first : PACK * (first + width)].rearrange(
+                "p (t n) -> p t n", t=PACK
+            )
             for t in range(PACK):
                 nc.vector.tensor_tensor(
                     h_planes[:, t, :],
@@ -181,7 +182,7 @@ def tile_picked_yvera_silu_p_kernel(
                 )
             nc.scalar.copy(
                 h_fused[:, cols, :].rearrange("p (c i) t -> p c t i", i=RUN),
-                h_planes[:].rearrange("p t (c i) -> p c t i", i=RUN),
+                h_planes.rearrange("p t (c i) -> p c t i", i=RUN),
             )
 
         ee_turned = keep.tile([P, S // CHUNK, N], F32, name="ee_turned")
@@ -250,9 +251,9 @@ def tile_picked_yvera_silu_p_kernel(
                     )
             result = keep.tile([P, width], F32, name=f"result{first}")
             nc.scalar.activation(result[:], total[:], SILU)
-            nc.sync.dma_start(out[:, first : first + width], result[:])
+            queue = nc.scalar if first + width == S else nc.sync
+            queue.dma_start(out[:, first : first + width], result[:])
 
-        chunks = list(range(FUSED, S, CHUNK))
         made = FUSED
         rr_tiles = {}
         terms = {}

@@ -14,7 +14,6 @@ U16 = mybir.dt.uint16
 U8 = mybir.dt.uint8
 FP8X4 = mybir.dt.float8_e4m3fn_x4
 MULT = mybir.AluOpType.mult
-ADD = mybir.AluOpType.add
 SILU = mybir.ActivationFunctionType.Silu
 
 P = 128
@@ -23,12 +22,8 @@ LIST = 16
 HALF = 512
 CHUNK = 128
 RUN = 4
-FUSED_GROUPS = (256, 256)
-EARLY_GROUPS = (256, 128, 128)
-FUSED = sum(FUSED_GROUPS)
-EARLY = sum(EARLY_GROUPS)
-SPARE = max(EARLY, FUSED, R) - R + 32
-LB_WINDOW = 1376
+GROUPS = (256, 256, 256, 128, 128)
+SPARE = 32
 
 
 def tile_picked_yvera_silu_p_kernel(
@@ -38,20 +33,27 @@ def tile_picked_yvera_silu_p_kernel(
     with ExitStack() as ctx:
         lists = ctx.enter_context(tc.tile_pool(name="lists", bufs=1))
         keep = ctx.enter_context(tc.tile_pool(name="keep", bufs=1))
+        turns = ctx.enter_context(tc.tile_pool(name="turns", bufs=1))
         psum = ctx.enter_context(tc.psum_pool(name="psum", bufs=1))
 
         ad_list = lists.tile([P, S // LIST], U16, name="ad_list")
         token_list = lists.tile([P, S // LIST], U16, name="token_list")
-        ld_tables = [keep.tile([P, R + SPARE], F32, name=f"ld_table{t}") for t in range(PACK)]
-        lb_table = keep.tile([P, LB_WINDOW], F32, name="lb_table")
+        ld_early = turns.tile([P, R + SPARE], F32, name="ld_early", offset=T)
+        ld_tables = {t: turns.tile([P, R], F32, name=f"ld_table{t}", offset=4 * R * (t - 1)) for t in range(1, PACK)}
+        lb_table = keep.tile([P, R + SPARE], F32, name="lb_table")
         word_table = keep.tile([P, T], I32, name="word_table")
-        scale_table = keep.tile([P, T], U8, name="scale_table", tag="scales_then_w")
-        w1_raw = keep.tile([P, PACK, H], F32, name="w1_raw", tag="w1_then_ld")
+        scale_table = turns.tile([P, T], U8, name="scale_table", offset=0)
+        w1_raw = turns.tile([P, PACK, H], F32, name="w1_raw", offset=2 * T)
+        x_bytes = keep.tile([P, S], U8, name="x_bytes", align_bytes=64)
 
         def entries(index_list, first, count):
             return index_list[:, first // LIST : (first + count) // LIST]
 
-        nc.gpsimd.memset(scale_table[:].bitcast(I32), 0)
+        nc.gpsimd.memset(scale_table[:].bitcast(I32)[:, :640], 0)
+        nc.vector.memset(scale_table[:].bitcast(I32)[:, 640:], 0)
+        nc.gpsimd.memset(lb_table[:, R:], 0.0)
+        nc.gpsimd.memset(ld_early[:, R:], 0.0)
+        nc.gpsimd.memset(x_bytes[:].bitcast(I32), 0)
         warm_in = keep.tile([P, 1], F32, name="warm_in")
         warm_out = keep.tile([P, 1], F32, name="warm_out")
         nc.vector.memset(warm_in[:], 0.0)
@@ -59,57 +61,53 @@ def tile_picked_yvera_silu_p_kernel(
         identity = keep.tile([P, P], F32, name="identity")
         make_identity(nc, identity[:])
 
-        nc.vector.memset(lb_table[:, R:], 0.0)
-        for table in ld_tables:
-            nc.vector.memset(table[:, R:], 0.0)
-
-        ld_rows = ld.rearrange("(p t) r -> p t r", t=PACK)
-        nc.sync.dma_start(ld_tables[0][:, :R], ld_rows[:, 0, :])
+        nc.sync.dma_start(lb_table[:, :R], lb)
         nc.sync.dma_start(ad_list[:], ad)
         nc.sync.dma_start(token_list[:], offs)
         nc.sync.dma_start(scale_table[0:P:8, :].bitcast(I32), x_scales[0].bitcast(I32))
-        for t in range(1, PACK):
-            nc.sync.dma_start(ld_tables[t][:, :R], ld_rows[:, t, :])
+        ld_rows = ld.rearrange("(p t) r -> p t r", t=PACK)
+        nc.sync.dma_start(ld_early[:, :R], ld_rows[:, 0, :])
         nc.sync.dma_start(w1_raw[:], w1.rearrange("(p j) c -> p j c", j=PACK))
-        nc.sync.dma_start(lb_table[:, :R], lb)
         nc.sync.dma_start(word_table[:], x_words[0].rearrange("p c t -> p (c t)").bitcast(I32))
 
+        lb_picked = keep.tile([P, S], F32, name="lb_picked")
+
+        def pick_lb(first):
+            nc.vector.tensor_copy(
+                lb_picked[:, first : first + HALF], lb_table[:].indirect(entries(ad_list, first, HALF))
+            )
+
+        pick_lb(0)
         spread_bytes = keep.tile([P, S], U8, name="spread_bytes")
         nc.vector.tensor_copy(spread_bytes[:], scale_table[:].indirect(token_list[:]))
-        x_bytes = keep.tile([P, S], U8, name="x_bytes", align_bytes=64)
-        nc.vector.memset(x_bytes[:].bitcast(I32), 0)
         for r in range(4):
             nc.sync.dma_start(
                 x_bytes[r:P:32, :].bitcast(I32), spread_bytes[8 * r : P : 32, :].bitcast(I32)
             )
-        w32_raw = keep.tile([P, 2, PACK, N], F32, name="w32_raw", tag="scales_then_w")
-        for slot, weight in enumerate((w3, w2)):
-            nc.sync.dma_start(w32_raw[:, slot], weight.rearrange("(p j) c -> p j c", j=PACK))
+        pick_lb(HALF)
 
-        ld_picked = keep.tile([P, PACK, EARLY], F32, name="ld_picked", tag="ld_then_lb")
-        for t in range(PACK):
+        ld_picked = keep.tile([P, S], F32, name="ld_picked")
+        for first in range(0, S, HALF):
             nc.vector.tensor_copy(
-                ld_picked[:, t, :], ld_tables[t][:].indirect(entries(ad_list, FUSED, EARLY))
+                ld_picked[:, first : first + HALF], ld_early[:].indirect(entries(ad_list, first, HALF))
             )
-        lb_picked = keep.tile([P, S], F32, name="lb_picked")
-        nc.vector.tensor_copy(lb_picked[:], lb_table[:].indirect(ad_list[:]))
+
+        for t in range(1, PACK):
+            nc.sync.dma_start(ld_tables[t][:], ld_rows[:, t, :])
 
         w1_bf = keep.tile([P, PACK * H], BF16, name="w1_bf", align_bytes=64)
         nc.scalar.copy(
-            w1_bf[:].rearrange("p (t m j) -> p m t j", t=PACK, j=PACK),
-            w1_raw[:].rearrange("p j (m t) -> p m t j", t=PACK),
+            w1_bf[:].rearrange("p (t m j) -> p m j t", t=PACK, j=PACK),
+            w1_raw[:].rearrange("p j (m t) -> p m j t", t=PACK),
         )
+        w32_raw = turns.tile([P, 2, PACK, N], F32, name="w32_raw", offset=2 * T)
+        for slot, weight in enumerate((w3, w2)):
+            nc.sync.dma_start(w32_raw[:, slot], weight.rearrange("(p j) c -> p j c", j=PACK))
         w1_codes = keep.tile([P, H], U32, name="w1_codes", align_bytes=64)
         w1_scales = keep.tile([P, H], U8, name="w1_scales", align_bytes=64)
         nc.vector.quantize_mx(w1_codes[:].bitcast(FP8X4), w1_scales[:], w1_bf[:])
 
-        ld_woven = keep.tile([P, EARLY, PACK], F32, name="ld_woven", tag="w1_then_ld")
-        nc.scalar.copy(
-            ld_woven[:].rearrange("p (c i) t -> p c t i", i=RUN),
-            ld_picked[:].rearrange("p t (c i) -> p c t i", i=RUN),
-        )
-
-        lb_turned = keep.tile([P, S // CHUNK, N], F32, name="lb_turned", tag="ld_then_lb")
+        lb_turned = keep.tile([P, S // CHUNK, N], F32, name="lb_turned")
         per_bank = HALF // CHUNK
         for half in range(S // HALF):
             bank = psum.tile([P, per_bank, N], F32, name="lb_bank", tag="total", bufs=2)
@@ -131,6 +129,8 @@ def tile_picked_yvera_silu_p_kernel(
             half, col = divmod(first, HALF)
             return x_codes[half][:, col : col + width].bitcast(FP8X4), x_bytes[:, first : first + width]
 
+        starts = [sum(GROUPS[:g]) for g in range(len(GROUPS))]
+
         def first_product(target, t, first, width):
             codes, scale_bytes = picked_x(first, width)
             nc.tensor.matmul_mx(
@@ -143,51 +143,65 @@ def tile_picked_yvera_silu_p_kernel(
                 stop=True,
             )
 
-        groups = FUSED_GROUPS + EARLY_GROUPS
-        starts = [sum(groups[:g]) for g in range(len(groups))]
+        h_rows = keep.tile([P, PACK + 2, HALF], F32, name="h_rows")
+        places = ((2, 0), (2, 256), (1, 0), (1, 256), (0, 0))
 
-        y_sb = keep.tile([P, PACK, FUSED], F32, name="y_sb", tag="y_then_h", align_bytes=64)
-        for first, width in zip(starts, FUSED_GROUPS):
-            for t in range(PACK):
-                y = psum.tile([P, width], F32, name="y_plane", tag="y", bufs=4)
-                first_product(y[:], t, first, width)
-                nc.scalar.copy(y_sb[:, t, first : first + width], y[:])
+        def early_plane(half):
+            y = psum.tile([P, HALF], F32, name="y_early", tag="y", bufs=4)
+            first_product(y[:], 0, half * HALF, HALF)
+            runs = ((0, HALF, 2),) if half == 0 else ((0, 384, 1), (384, CHUNK, 0))
+            for col, width, row in runs:
+                first = half * HALF + col
+                nc.vector.tensor_tensor(
+                    h_rows[:, row, :width], y[:, col : col + width], ld_picked[:, first : first + width], MULT
+                )
 
-        h_stage = keep.tile([P, PACK * FUSED], F32, name="h_stage", align_bytes=64)
-        w32_flat = h_stage[:, PACK * FUSED - PACK * N :].bitcast(BF16)
-        w32_bf = w32_flat.rearrange("p (w c j) -> p w c j", w=2, j=PACK)
-        for slot in range(2):
-            nc.scalar.copy(
-                w32_bf[:, slot].rearrange("p (c i) j -> p c j i", i=RUN),
-                w32_raw[:, slot].rearrange("p j (c i) -> p c j i", i=RUN),
-            )
-        w32_codes = keep.tile([P, 2 * N], U32, name="w32_codes", align_bytes=64)
-        w32_scales = keep.tile([P, 2 * N], U8, name="w32_scales", align_bytes=64)
-        nc.vector.quantize_mx(
-            w32_codes[:].bitcast(FP8X4), w32_scales[:], w32_flat
-        )
+        def late_planes(g):
+            first, width = starts[g], GROUPS[g]
+            y_sb = keep.tile([P, (PACK - 1) * width], F32, name=f"y_sb{g}")
+            for t0, planes in ((1, 3),) if 3 * width <= HALF else ((1, 1), (2, 2)):
+                y = psum.tile([P, planes * width], F32, name="y", tag="y", bufs=4)
+                for t in range(planes):
+                    first_product(y[:, t * width : (t + 1) * width], t0 + t, first, width)
+                nc.scalar.copy(y_sb[:, (t0 - 1) * width : (t0 - 1 + planes) * width], y[:])
+            return y_sb
 
-        h_fused = keep.tile([P, FUSED, PACK], BF16, name="h_fused", align_bytes=64)
-        for first, width in zip(starts, FUSED_GROUPS):
-            cols = slice(first, first + width)
-            h_planes = h_stage[:, PACK * first : PACK * (first + width)].rearrange(
-                "p (t n) -> p t n", t=PACK
-            )
-            for t in range(PACK):
+        def hidden(g, y_sb):
+            first, width = starts[g], GROUPS[g]
+            row, col = places[g]
+            h_planes = h_rows[:, row : row + PACK, col : col + width]
+            for t in range(1, PACK):
                 nc.vector.tensor_tensor(
                     h_planes[:, t, :],
                     ld_tables[t][:].indirect(entries(ad_list, first, width)),
-                    y_sb[:, t, cols],
+                    y_sb[:, (t - 1) * width : t * width],
                     MULT,
                 )
+            h_bf = keep.tile([P, width * PACK], BF16, name=f"h_bf{g}", align_bytes=64)
             nc.scalar.copy(
-                h_fused[:, cols, :].rearrange("p (c i) t -> p c t i", i=RUN),
+                h_bf[:].rearrange("p (c i t) -> p c t i", i=RUN, t=PACK),
                 h_planes.rearrange("p t (c i) -> p c t i", i=RUN),
             )
+            return h_bf
+
+        def other_weights():
+            w32_bf = keep.tile([P, 2, N, PACK], BF16, name="w32_bf", align_bytes=64)
+            for slot in range(2):
+                nc.scalar.copy(
+                    w32_bf[:, slot].rearrange("p (c i) j -> p c j i", i=RUN),
+                    w32_raw[:, slot].rearrange("p j (c i) -> p c j i", i=RUN),
+                )
+            codes = keep.tile([P, 2 * N], U32, name="w32_codes", align_bytes=64)
+            scales = keep.tile([P, 2 * N], U8, name="w32_scales", align_bytes=64)
+            nc.vector.quantize_mx(
+                codes[:].bitcast(FP8X4), scales[:], w32_bf[:].rearrange("p w c j -> p (w c j)")
+            )
+            return codes, scales
 
         ee_turned = keep.tile([P, S // CHUNK, N], F32, name="ee_turned")
-        for half in range(S // HALF):
-            bank = psum.tile([P, per_bank, N], F32, name="ee_bank", tag="rr", bufs=2)
+
+        def frozen(half, w32_codes, w32_scales):
+            bank = psum.tile([P, per_bank, N], F32, name="ee_bank", tag="y", bufs=4)
             for c in range(per_bank):
                 codes, scale_bytes = picked_x(half * HALF + c * CHUNK, CHUNK)
                 nc.tensor.matmul_mx(
@@ -201,26 +215,12 @@ def tile_picked_yvera_silu_p_kernel(
                 )
             nc.scalar.copy(ee_turned[:, half * per_bank : (half + 1) * per_bank, :], bank[:])
 
-        h_early = keep.tile([P, EARLY, PACK], BF16, name="h_early", tag="y_then_h", align_bytes=64)
-
-        def hidden(first):
-            cols = slice(first - FUSED, first - FUSED + CHUNK)
-            y = psum.tile([P, PACK, CHUNK], F32, name="y_chunk", tag="y", bufs=4)
-            for t in range(PACK):
-                first_product(y[:, t, :], t, first, CHUNK)
-            nc.vector.tensor_tensor(
-                h_early[:, cols, :], y[:].rearrange("p t n -> p n t"), ld_woven[:, cols, :], MULT
-            )
-
-        def second(first, width):
-            if first < FUSED:
-                h_bf = h_fused[:, first : first + width, :]
-            else:
-                h_bf = h_early[:, first - FUSED : first - FUSED + width, :]
-            h_codes = keep.tile([P, width], U32, name=f"h_codes{first}", align_bytes=64)
-            h_scales = keep.tile([P, width], U8, name=f"h_scales{first}", align_bytes=64)
+        def second(g, h_bf, w32_codes, w32_scales):
+            width = GROUPS[g]
+            h_codes = keep.tile([P, width], U32, name=f"h_codes{g}", align_bytes=64)
+            h_scales = keep.tile([P, width], U8, name=f"h_scales{g}", align_bytes=64)
             nc.vector.quantize_mx(
-                h_codes[:].bitcast(FP8X4), h_scales[:], h_bf.rearrange("p n t -> p (n t)")
+                h_codes[:].bitcast(FP8X4), h_scales[:], h_bf[:]
             )
             rr = psum.tile([P, width // CHUNK, N], F32, name="rr", tag="rr", bufs=2)
             for c in range(width // CHUNK):
@@ -235,13 +235,11 @@ def tile_picked_yvera_silu_p_kernel(
                 )
             return rr
 
-        def scaled(first, width, rr):
-            term = keep.tile([P, width // CHUNK, N], F32, name=f"term{first}")
+        def scaled_sum(g, rr):
+            first, width = starts[g], GROUPS[g]
+            term = keep.tile([P, width // CHUNK, N], F32, name=f"term{g}")
             chunks = slice(first // CHUNK, (first + width) // CHUNK)
             nc.vector.tensor_tensor(term[:], rr[:], lb_turned[:, chunks, :], MULT)
-            return term
-
-        def finish(first, width, term):
             total = psum.tile([P, width], F32, name="total", tag="total", bufs=2)
             for c in range(width // CHUNK):
                 target = total[:, c * CHUNK : (c + 1) * CHUNK]
@@ -249,21 +247,39 @@ def tile_picked_yvera_silu_p_kernel(
                     nc.tensor.matmul(
                         target, lhsT=addend, rhs=identity[:], is_transpose=True, start=turn == 0, stop=turn == 1
                     )
-            result = keep.tile([P, width], F32, name=f"result{first}")
+            return total
+
+        def finish(g, total):
+            first, width = starts[g], GROUPS[g]
+            result = keep.tile([P, width], F32, name=f"result{g}")
             nc.scalar.activation(result[:], total[:], SILU)
             queue = nc.scalar if first + width == S else nc.sync
             queue.dma_start(out[:, first : first + width], result[:])
 
-        made = FUSED
-        rr_tiles = {}
-        terms = {}
-        for step in range(len(groups) + 2):
-            while made < S and (made < FUSED + CHUNK * (step + 1) or made < sum(groups[: step + 1]) + CHUNK):
-                hidden(made)
-                made = made + CHUNK
-            if 0 <= step - 2:
-                finish(starts[step - 2], groups[step - 2], terms[step - 2])
-            if 0 <= step - 1 < len(groups):
-                terms[step - 1] = scaled(starts[step - 1], groups[step - 1], rr_tiles[step - 1])
-            if step < len(groups):
-                rr_tiles[step] = second(starts[step], groups[step])
+        count = len(GROUPS)
+        y0 = late_planes(0)
+        early_plane(0)
+        y1 = late_planes(1)
+        early_plane(1)
+        y2 = late_planes(2)
+        w32_codes, w32_scales = other_weights()
+        h0 = hidden(0, y0)
+        y3 = late_planes(3)
+        y4 = late_planes(4)
+        h1 = hidden(1, y1)
+        rr0 = second(0, h0, w32_codes, w32_scales)
+        frozen(0, w32_codes, w32_scales)
+        frozen(1, w32_codes, w32_scales)
+        h2 = hidden(2, y2)
+        finish(0, scaled_sum(0, rr0))
+        rr1 = second(1, h1, w32_codes, w32_scales)
+        h3 = hidden(3, y3)
+        finish(1, scaled_sum(1, rr1))
+        rr2 = second(2, h2, w32_codes, w32_scales)
+        h4 = hidden(4, y4)
+        total2 = scaled_sum(2, rr2)
+        rr3 = second(3, h3, w32_codes, w32_scales)
+        rr4 = second(4, h4, w32_codes, w32_scales)
+        finish(2, total2)
+        finish(3, scaled_sum(3, rr3))
+        finish(4, scaled_sum(4, rr4))

@@ -17,13 +17,16 @@ MULT = mybir.AluOpType.mult
 SILU = mybir.ActivationFunctionType.Silu
 
 P = 128
+KIB = 1024
 PACK = 4
 LIST = 16
-HALF = 512
+BANK = 512
 CHUNK = 128
 RUN = 4
 GROUPS = (256, 256, 256, 128, 128)
-SPARE = 32
+WIDE = max(GROUPS)
+WINDOW = R + 32
+CLEARED_BY_GPSIMD = 640
 
 
 def tile_picked_yvera_silu_p_kernel(
@@ -38,22 +41,24 @@ def tile_picked_yvera_silu_p_kernel(
 
         ad_list = lists.tile([P, S // LIST], U16, name="ad_list")
         token_list = lists.tile([P, S // LIST], U16, name="token_list")
-        ld_early = turns.tile([P, R + SPARE], F32, name="ld_early", offset=T)
-        ld_tables = {t: turns.tile([P, R], F32, name=f"ld_table{t}", offset=4 * R * (t - 1)) for t in range(1, PACK)}
-        lb_table = keep.tile([P, R + SPARE], F32, name="lb_table")
+        ld_first = turns.tile([P, WINDOW], F32, name="ld_first", offset=8 * KIB)
+        ld_tables = {
+            t: turns.tile([P, R], F32, name=f"ld_table{t}", offset=(2 + 2 * t) * KIB) for t in range(1, PACK)
+        }
+        lb_table = keep.tile([P, WINDOW], F32, name="lb_table")
         word_table = keep.tile([P, T], I32, name="word_table")
-        scale_table = turns.tile([P, T], U8, name="scale_table", offset=0)
-        w1_raw = turns.tile([P, PACK, H], F32, name="w1_raw", offset=2 * T)
+        scale_table = turns.tile([P, T], U8, name="scale_table", offset=4 * KIB - 32)
+        w1_raw = turns.tile([P, PACK, H], F32, name="w1_raw", offset=12 * KIB)
         x_bytes = keep.tile([P, S], U8, name="x_bytes", align_bytes=64)
 
         def entries(index_list, first, count):
             return index_list[:, first // LIST : (first + count) // LIST]
 
-        nc.gpsimd.memset(scale_table[:].bitcast(I32)[:, :640], 0)
-        nc.vector.memset(scale_table[:].bitcast(I32)[:, 640:], 0)
-        nc.gpsimd.memset(lb_table[:, R:], 0.0)
-        nc.gpsimd.memset(ld_early[:, R:], 0.0)
-        nc.gpsimd.memset(x_bytes[:].bitcast(I32), 0)
+        nc.gpsimd.memset(scale_table[:].bitcast(I32)[:, :CLEARED_BY_GPSIMD], 0)
+        nc.vector.memset(scale_table[:].bitcast(I32)[:, CLEARED_BY_GPSIMD:], 0)
+        nc.vector.memset(lb_table[:, R:], 0.0)
+        nc.vector.memset(ld_first[:, R:], 0.0)
+        nc.vector.memset(x_bytes[:].bitcast(I32), 0)
         warm_in = keep.tile([P, 1], F32, name="warm_in")
         warm_out = keep.tile([P, 1], F32, name="warm_out")
         nc.vector.memset(warm_in[:], 0.0)
@@ -64,112 +69,112 @@ def tile_picked_yvera_silu_p_kernel(
         nc.sync.dma_start(lb_table[:, :R], lb)
         nc.sync.dma_start(ad_list[:], ad)
         nc.sync.dma_start(token_list[:], offs)
-        nc.sync.dma_start(scale_table[0:P:8, :].bitcast(I32), x_scales[0].bitcast(I32))
         ld_rows = ld.rearrange("(p t) r -> p t r", t=PACK)
-        nc.sync.dma_start(ld_early[:, :R], ld_rows[:, 0, :])
+        nc.sync.dma_start(ld_first[:, :R], ld_rows[:, 0, :])
+        nc.sync.dma_start(scale_table[0:P:8, :].bitcast(I32), x_scales[0].bitcast(I32))
         nc.sync.dma_start(w1_raw[:], w1.rearrange("(p j) c -> p j c", j=PACK))
         nc.sync.dma_start(word_table[:], x_words[0].rearrange("p c t -> p (c t)").bitcast(I32))
 
+        def picked_columns(target, table, first):
+            nc.vector.tensor_copy(target[:, first : first + BANK], table[:].indirect(entries(ad_list, first, BANK)))
+
         lb_picked = keep.tile([P, S], F32, name="lb_picked")
-
-        def pick_lb(first):
-            nc.vector.tensor_copy(
-                lb_picked[:, first : first + HALF], lb_table[:].indirect(entries(ad_list, first, HALF))
-            )
-
-        pick_lb(0)
+        picked_columns(lb_picked, lb_table, 0)
         spread_bytes = keep.tile([P, S], U8, name="spread_bytes")
         nc.vector.tensor_copy(spread_bytes[:], scale_table[:].indirect(token_list[:]))
         for r in range(4):
             nc.sync.dma_start(
                 x_bytes[r:P:32, :].bitcast(I32), spread_bytes[8 * r : P : 32, :].bitcast(I32)
             )
-        pick_lb(HALF)
+        picked_columns(lb_picked, lb_table, BANK)
 
-        ld_picked = keep.tile([P, S], F32, name="ld_picked")
-        for first in range(0, S, HALF):
-            nc.vector.tensor_copy(
-                ld_picked[:, first : first + HALF], ld_early[:].indirect(entries(ad_list, first, HALF))
-            )
-
+        ld_picked = turns.tile([P, S], F32, name="ld_picked", offset=0)
+        for first in range(0, S, BANK):
+            picked_columns(ld_picked, ld_first, first)
         for t in range(1, PACK):
             nc.sync.dma_start(ld_tables[t][:], ld_rows[:, t, :])
 
         w1_bf = keep.tile([P, PACK * H], BF16, name="w1_bf", align_bytes=64)
         nc.scalar.copy(
-            w1_bf[:].rearrange("p (t m j) -> p m j t", t=PACK, j=PACK),
-            w1_raw[:].rearrange("p j (m t) -> p m j t", t=PACK),
+            w1_bf[:].rearrange("p (t m j) -> p m t j", t=PACK, j=PACK),
+            w1_raw[:].rearrange("p j (m t) -> p m t j", t=PACK),
         )
-        w32_raw = turns.tile([P, 2, PACK, N], F32, name="w32_raw", offset=2 * T)
+        w32_raw = turns.tile([P, 2, PACK, N], F32, name="w32_raw", offset=12 * KIB)
         for slot, weight in enumerate((w3, w2)):
             nc.sync.dma_start(w32_raw[:, slot], weight.rearrange("(p j) c -> p j c", j=PACK))
         w1_codes = keep.tile([P, H], U32, name="w1_codes", align_bytes=64)
         w1_scales = keep.tile([P, H], U8, name="w1_scales", align_bytes=64)
         nc.vector.quantize_mx(w1_codes[:].bitcast(FP8X4), w1_scales[:], w1_bf[:])
 
-        lb_turned = keep.tile([P, S // CHUNK, N], F32, name="lb_turned")
-        per_bank = HALF // CHUNK
-        for half in range(S // HALF):
+        per_bank = BANK // CHUNK
+        lb_turned = turns.tile([P, S // CHUNK, N], F32, name="lb_turned", offset=16 * KIB)
+        for c0 in range(0, S // CHUNK, per_bank):
             bank = psum.tile([P, per_bank, N], F32, name="lb_bank", tag="total", bufs=2)
             for c in range(per_bank):
-                first = half * HALF + c * CHUNK
+                first = (c0 + c) * CHUNK
                 nc.tensor.transpose(bank[:, c, :], lb_picked[:, first : first + CHUNK], identity[:])
-            nc.scalar.copy(lb_turned[:, half * per_bank : (half + 1) * per_bank, :], bank[:])
+            nc.scalar.copy(lb_turned[:, c0 : c0 + per_bank, :], bank[:])
 
         x_codes = []
-        for half in range(S // HALF):
-            codes = keep.tile([P, HALF], U32, name=f"x_codes{half}", align_bytes=64)
+        for first in range(0, S, BANK):
+            codes = keep.tile([P, BANK], U32, name=f"x_codes{first}", align_bytes=64)
             nc.vector.tensor_copy(
-                codes[:],
-                word_table[:].bitcast(U32).indirect(entries(token_list, half * HALF, HALF)),
+                codes[:], word_table[:].bitcast(U32).indirect(entries(token_list, first, BANK))
             )
             x_codes.append(codes)
 
         def picked_x(first, width):
-            half, col = divmod(first, HALF)
-            return x_codes[half][:, col : col + width].bitcast(FP8X4), x_bytes[:, first : first + width]
+            tile, col = divmod(first, BANK)
+            return x_codes[tile][:, col : col + width], x_bytes[:, first : first + width]
 
-        starts = [sum(GROUPS[:g]) for g in range(len(GROUPS))]
-
-        def first_product(target, t, first, width):
-            codes, scale_bytes = picked_x(first, width)
+        def product(target, stationary, moving):
             nc.tensor.matmul_mx(
                 target,
-                lhsT=w1_codes[:, t * P : (t + 1) * P].bitcast(FP8X4),
-                lhsT_scale=w1_scales[:, t * P : (t + 1) * P],
-                rhs=codes,
-                rhs_scale=scale_bytes,
+                lhsT=stationary[0].bitcast(FP8X4),
+                lhsT_scale=stationary[1],
+                rhs=moving[0].bitcast(FP8X4),
+                rhs_scale=moving[1],
                 start=True,
                 stop=True,
             )
 
-        h_rows = keep.tile([P, PACK + 2, HALF], F32, name="h_rows")
-        places = ((2, 0), (2, 256), (1, 0), (1, 256), (0, 0))
+        def w1_plane(t):
+            return w1_codes[:, t * P : (t + 1) * P], w1_scales[:, t * P : (t + 1) * P]
 
-        def early_plane(half):
-            y = psum.tile([P, HALF], F32, name="y_early", tag="y", bufs=4)
-            first_product(y[:], 0, half * HALF, HALF)
-            runs = ((0, HALF, 2),) if half == 0 else ((0, 384, 1), (384, CHUNK, 0))
-            for col, width, row in runs:
-                first = half * HALF + col
+        starts = [sum(GROUPS[:g]) for g in range(len(GROUPS))]
+        last = len(GROUPS) - 1
+
+        h_rows = keep.tile([P, PACK + (last + 1) // 2, 2 * WIDE], F32, name="h_rows")
+
+        def planes_of(g):
+            row, col = (last - g + 1) // 2, WIDE * (g % 2)
+            return h_rows[:, row : row + PACK, col : col + GROUPS[g]]
+
+        def first_plane(first, runs):
+            y = psum.tile([P, BANK], F32, name="y_first", tag="y", bufs=4)
+            product(y[:], w1_plane(0), picked_x(first, BANK))
+            for run in runs:
+                begin, width = starts[run[0]], sum(GROUPS[g] for g in run)
                 nc.vector.tensor_tensor(
-                    h_rows[:, row, :width], y[:, col : col + width], ld_picked[:, first : first + width], MULT
+                    h_rows[:, (last - run[0] + 1) // 2, :width],
+                    y[:, begin - first : begin - first + width],
+                    ld_picked[:, begin : begin + width],
+                    MULT,
                 )
 
-        def late_planes(g):
+        def copied_planes(g):
             first, width = starts[g], GROUPS[g]
             y_sb = keep.tile([P, (PACK - 1) * width], F32, name=f"y_sb{g}")
-            for t0, planes in ((1, 3),) if 3 * width <= HALF else ((1, 1), (2, 2)):
-                y = psum.tile([P, planes * width], F32, name="y", tag="y", bufs=4)
-                for t in range(planes):
-                    first_product(y[:, t * width : (t + 1) * width], t0 + t, first, width)
-                nc.scalar.copy(y_sb[:, (t0 - 1) * width : (t0 - 1 + planes) * width], y[:])
+            for planes in ((1, 2, 3),) if (PACK - 1) * width <= BANK else ((1,), (2, 3)):
+                y = psum.tile([P, len(planes) * width], F32, name="y", tag="y", bufs=4)
+                for place, t in enumerate(planes):
+                    product(y[:, place * width : (place + 1) * width], w1_plane(t), picked_x(first, width))
+                nc.scalar.copy(y_sb[:, (planes[0] - 1) * width : planes[-1] * width], y[:])
             return y_sb
 
         def hidden(g, y_sb):
             first, width = starts[g], GROUPS[g]
-            row, col = places[g]
-            h_planes = h_rows[:, row : row + PACK, col : col + width]
+            h_planes = planes_of(g)
             for t in range(1, PACK):
                 nc.vector.tensor_tensor(
                     h_planes[:, t, :],
@@ -184,7 +189,7 @@ def tile_picked_yvera_silu_p_kernel(
             )
             return h_bf
 
-        def other_weights():
+        def quantised_w3_w2():
             w32_bf = keep.tile([P, 2, N, PACK], BF16, name="w32_bf", align_bytes=64)
             for slot in range(2):
                 nc.scalar.copy(
@@ -196,56 +201,43 @@ def tile_picked_yvera_silu_p_kernel(
             nc.vector.quantize_mx(
                 codes[:].bitcast(FP8X4), scales[:], w32_bf[:].rearrange("p w c j -> p (w c j)")
             )
-            return codes, scales
+            return (codes[:, :N], scales[:, :N]), (codes[:, N:], scales[:, N:])
 
         ee_turned = keep.tile([P, S // CHUNK, N], F32, name="ee_turned")
 
-        def frozen(half, w32_codes, w32_scales):
-            bank = psum.tile([P, per_bank, N], F32, name="ee_bank", tag="y", bufs=4)
-            for c in range(per_bank):
-                codes, scale_bytes = picked_x(half * HALF + c * CHUNK, CHUNK)
-                nc.tensor.matmul_mx(
-                    bank[:, c, :],
-                    lhsT=codes,
-                    lhsT_scale=scale_bytes,
-                    rhs=w32_codes[:, :N].bitcast(FP8X4),
-                    rhs_scale=w32_scales[:, :N],
-                    start=True,
-                    stop=True,
-                )
-            nc.scalar.copy(ee_turned[:, half * per_bank : (half + 1) * per_bank, :], bank[:])
+        def frozen_layer(w3_quantised):
+            for c0 in range(0, S // CHUNK, per_bank):
+                bank = psum.tile([P, per_bank, N], F32, name="ee_bank", tag="y", bufs=4)
+                for c in range(per_bank):
+                    product(bank[:, c, :], picked_x((c0 + c) * CHUNK, CHUNK), w3_quantised)
+                nc.scalar.copy(ee_turned[:, c0 : c0 + per_bank, :], bank[:])
 
-        def second(g, h_bf, w32_codes, w32_scales):
+        def second_product(g, h_bf, w2_quantised):
             width = GROUPS[g]
             h_codes = keep.tile([P, width], U32, name=f"h_codes{g}", align_bytes=64)
             h_scales = keep.tile([P, width], U8, name=f"h_scales{g}", align_bytes=64)
-            nc.vector.quantize_mx(
-                h_codes[:].bitcast(FP8X4), h_scales[:], h_bf[:]
-            )
+            nc.vector.quantize_mx(h_codes[:].bitcast(FP8X4), h_scales[:], h_bf[:])
             rr = psum.tile([P, width // CHUNK, N], F32, name="rr", tag="rr", bufs=2)
             for c in range(width // CHUNK):
-                nc.tensor.matmul_mx(
-                    rr[:, c, :],
-                    lhsT=h_codes[:, c * CHUNK : (c + 1) * CHUNK].bitcast(FP8X4),
-                    lhsT_scale=h_scales[:, c * CHUNK : (c + 1) * CHUNK],
-                    rhs=w32_codes[:, N:].bitcast(FP8X4),
-                    rhs_scale=w32_scales[:, N:],
-                    start=True,
-                    stop=True,
-                )
+                cols = slice(c * CHUNK, (c + 1) * CHUNK)
+                product(rr[:, c, :], (h_codes[:, cols], h_scales[:, cols]), w2_quantised)
             return rr
 
-        def scaled_sum(g, rr):
+        def summed(g, rr):
             first, width = starts[g], GROUPS[g]
             term = keep.tile([P, width // CHUNK, N], F32, name=f"term{g}")
             chunks = slice(first // CHUNK, (first + width) // CHUNK)
             nc.vector.tensor_tensor(term[:], rr[:], lb_turned[:, chunks, :], MULT)
             total = psum.tile([P, width], F32, name="total", tag="total", bufs=2)
             for c in range(width // CHUNK):
-                target = total[:, c * CHUNK : (c + 1) * CHUNK]
                 for turn, addend in enumerate((ee_turned[:, first // CHUNK + c, :], term[:, c, :])):
                     nc.tensor.matmul(
-                        target, lhsT=addend, rhs=identity[:], is_transpose=True, start=turn == 0, stop=turn == 1
+                        total[:, c * CHUNK : (c + 1) * CHUNK],
+                        lhsT=addend,
+                        rhs=identity[:],
+                        is_transpose=True,
+                        start=turn == 0,
+                        stop=turn == 1,
                     )
             return total
 
@@ -253,33 +245,31 @@ def tile_picked_yvera_silu_p_kernel(
             first, width = starts[g], GROUPS[g]
             result = keep.tile([P, width], F32, name=f"result{g}")
             nc.scalar.activation(result[:], total[:], SILU)
-            queue = nc.scalar if first + width == S else nc.sync
+            queue = nc.scalar if g == last else nc.sync
             queue.dma_start(out[:, first : first + width], result[:])
 
-        count = len(GROUPS)
-        y0 = late_planes(0)
-        early_plane(0)
-        y1 = late_planes(1)
-        early_plane(1)
-        y2 = late_planes(2)
-        w32_codes, w32_scales = other_weights()
+        y0 = copied_planes(0)
+        first_plane(0, ((0, 1),))
+        y1 = copied_planes(1)
+        y2 = copied_planes(2)
+        first_plane(BANK, ((2, 3), (4,)))
+        w3_quantised, w2_quantised = quantised_w3_w2()
         h0 = hidden(0, y0)
-        y3 = late_planes(3)
-        y4 = late_planes(4)
+        y3 = copied_planes(3)
+        y4 = copied_planes(4)
         h1 = hidden(1, y1)
-        rr0 = second(0, h0, w32_codes, w32_scales)
-        frozen(0, w32_codes, w32_scales)
-        frozen(1, w32_codes, w32_scales)
+        rr0 = second_product(0, h0, w2_quantised)
+        frozen_layer(w3_quantised)
         h2 = hidden(2, y2)
-        finish(0, scaled_sum(0, rr0))
-        rr1 = second(1, h1, w32_codes, w32_scales)
+        finish(0, summed(0, rr0))
+        rr1 = second_product(1, h1, w2_quantised)
         h3 = hidden(3, y3)
-        finish(1, scaled_sum(1, rr1))
-        rr2 = second(2, h2, w32_codes, w32_scales)
+        finish(1, summed(1, rr1))
+        rr2 = second_product(2, h2, w2_quantised)
         h4 = hidden(4, y4)
-        total2 = scaled_sum(2, rr2)
-        rr3 = second(3, h3, w32_codes, w32_scales)
-        rr4 = second(4, h4, w32_codes, w32_scales)
+        total2 = summed(2, rr2)
+        rr3 = second_product(3, h3, w2_quantised)
+        rr4 = second_product(4, h4, w2_quantised)
         finish(2, total2)
-        finish(3, scaled_sum(3, rr3))
-        finish(4, scaled_sum(4, rr4))
+        finish(3, summed(3, rr3))
+        finish(4, summed(4, rr4))

@@ -24,7 +24,6 @@ BANK = 512
 CHUNK = 128
 RUN = 4
 GROUPS = (256, 256, 256, 128, 128)
-WIDE = max(GROUPS)
 WINDOW = R + 32
 CLEARED_BY_GPSIMD = 640
 
@@ -41,9 +40,9 @@ def tile_picked_yvera_silu_p_kernel(
 
         ad_list = lists.tile([P, S // LIST], U16, name="ad_list")
         token_list = lists.tile([P, S // LIST], U16, name="token_list")
-        ld_first = turns.tile([P, WINDOW], F32, name="ld_first", offset=8 * KIB)
+        ld_first = keep.tile([P, WINDOW], F32, name="ld_first")
         ld_tables = {
-            t: turns.tile([P, R], F32, name=f"ld_table{t}", offset=(2 + 2 * t) * KIB) for t in range(1, PACK)
+            t: turns.tile([P, R], F32, name=f"ld_table{t}", offset=(10 + 2 * t) * KIB) for t in range(1, PACK)
         }
         lb_table = keep.tile([P, WINDOW], F32, name="lb_table")
         word_table = keep.tile([P, T], I32, name="word_table")
@@ -91,23 +90,25 @@ def tile_picked_yvera_silu_p_kernel(
         ld_picked = turns.tile([P, S], F32, name="ld_picked", offset=0)
         for first in range(0, S, BANK):
             picked_columns(ld_picked, ld_first, first)
-        for t in range(1, PACK):
-            nc.sync.dma_start(ld_tables[t][:], ld_rows[:, t, :])
+        w32_raw = []
+        for slot, weight in enumerate((w3, w2)):
+            raw = turns.tile([P, PACK, N], F32, name=f"w32_raw{slot}", offset=(4 + 2 * slot) * KIB)
+            nc.sync.dma_start(raw[:], weight.rearrange("(p j) c -> p j c", j=PACK))
+            w32_raw.append(raw)
 
         w1_bf = keep.tile([P, PACK * H], BF16, name="w1_bf", align_bytes=64)
         nc.scalar.copy(
             w1_bf[:].rearrange("p (t m j) -> p m t j", t=PACK, j=PACK),
             w1_raw[:].rearrange("p j (m t) -> p m t j", t=PACK),
         )
-        w32_raw = turns.tile([P, 2, PACK, N], F32, name="w32_raw", offset=12 * KIB)
-        for slot, weight in enumerate((w3, w2)):
-            nc.sync.dma_start(w32_raw[:, slot], weight.rearrange("(p j) c -> p j c", j=PACK))
+        for t in range(1, PACK):
+            nc.sync.dma_start(ld_tables[t][:], ld_rows[:, t, :])
         w1_codes = keep.tile([P, H], U32, name="w1_codes", align_bytes=64)
         w1_scales = keep.tile([P, H], U8, name="w1_scales", align_bytes=64)
         nc.vector.quantize_mx(w1_codes[:].bitcast(FP8X4), w1_scales[:], w1_bf[:])
 
         per_bank = BANK // CHUNK
-        lb_turned = turns.tile([P, S // CHUNK, N], F32, name="lb_turned", offset=16 * KIB)
+        lb_turned = turns.tile([P, S // CHUNK, N], F32, name="lb_turned", offset=18 * KIB)
         for c0 in range(0, S // CHUNK, per_bank):
             bank = psum.tile([P, per_bank, N], F32, name="lb_bank", tag="total", bufs=2)
             for c in range(per_bank):
@@ -144,27 +145,23 @@ def tile_picked_yvera_silu_p_kernel(
         starts = [sum(GROUPS[:g]) for g in range(len(GROUPS))]
         last = len(GROUPS) - 1
 
-        h_rows = keep.tile([P, PACK + (last + 1) // 2, 2 * WIDE], F32, name="h_rows")
+        h_rows = keep.tile([P, PACK + 1, BANK], F32, name="h_rows")
 
         def planes_of(g):
-            row, col = (last - g + 1) // 2, WIDE * (g % 2)
-            return h_rows[:, row : row + PACK, col : col + GROUPS[g]]
+            half, col = divmod(starts[g], BANK)
+            return h_rows[:, 1 - half : 1 - half + PACK, col : col + GROUPS[g]]
 
-        def first_plane(first, runs):
+        def first_plane(first):
             y = psum.tile([P, BANK], F32, name="y_first", tag="y", bufs=4)
             product(y[:], w1_plane(0), picked_x(first, BANK))
-            for run in runs:
-                begin, width = starts[run[0]], sum(GROUPS[g] for g in run)
-                nc.vector.tensor_tensor(
-                    h_rows[:, (last - run[0] + 1) // 2, :width],
-                    y[:, begin - first : begin - first + width],
-                    ld_picked[:, begin : begin + width],
-                    MULT,
-                )
+            nc.vector.tensor_tensor(h_rows[:, 1 - first // BANK, :], y[:], ld_picked[:, first : first + BANK], MULT)
 
         def copied_planes(g):
             first, width = starts[g], GROUPS[g]
-            y_sb = keep.tile([P, (PACK - 1) * width], F32, name=f"y_sb{g}")
+            if g < 2:
+                y_sb = turns.tile([P, (PACK - 1) * width], F32, name=f"y_sb{g}", offset=(4 + 3 * g) * KIB)
+            else:
+                y_sb = keep.tile([P, (PACK - 1) * width], F32, name=f"y_sb{g}")
             for planes in ((1, 2, 3),) if (PACK - 1) * width <= BANK else ((1,), (2, 3)):
                 y = psum.tile([P, len(planes) * width], F32, name="y", tag="y", bufs=4)
                 for place, t in enumerate(planes):
@@ -182,7 +179,10 @@ def tile_picked_yvera_silu_p_kernel(
                     y_sb[:, (t - 1) * width : t * width],
                     MULT,
                 )
-            h_bf = keep.tile([P, width * PACK], BF16, name=f"h_bf{g}", align_bytes=64)
+            if g == 2:
+                h_bf = turns.tile([P, width * PACK], BF16, name="h_bf2", offset=22 * KIB, align_bytes=64)
+            else:
+                h_bf = keep.tile([P, width * PACK], BF16, name=f"h_bf{g}", align_bytes=64)
             nc.scalar.copy(
                 h_bf[:].rearrange("p (c i t) -> p c t i", i=RUN, t=PACK),
                 h_planes.rearrange("p t (c i) -> p c t i", i=RUN),
@@ -194,7 +194,7 @@ def tile_picked_yvera_silu_p_kernel(
             for slot in range(2):
                 nc.scalar.copy(
                     w32_bf[:, slot].rearrange("p (c i) j -> p c j i", i=RUN),
-                    w32_raw[:, slot].rearrange("p j (c i) -> p c j i", i=RUN),
+                    w32_raw[slot][:].rearrange("p j (c i) -> p c j i", i=RUN),
                 )
             codes = keep.tile([P, 2 * N], U32, name="w32_codes", align_bytes=64)
             scales = keep.tile([P, 2 * N], U8, name="w32_scales", align_bytes=64)
@@ -212,34 +212,45 @@ def tile_picked_yvera_silu_p_kernel(
                     product(bank[:, c, :], picked_x((c0 + c) * CHUNK, CHUNK), w3_quantised)
                 nc.scalar.copy(ee_turned[:, c0 : c0 + per_bank, :], bank[:])
 
-        def second_product(g, h_bf, w2_quantised):
+        def second_product(g, h_bf, w2_quantised, tag, bufs):
             width = GROUPS[g]
             h_codes = keep.tile([P, width], U32, name=f"h_codes{g}", align_bytes=64)
             h_scales = keep.tile([P, width], U8, name=f"h_scales{g}", align_bytes=64)
             nc.vector.quantize_mx(h_codes[:].bitcast(FP8X4), h_scales[:], h_bf[:])
-            rr = psum.tile([P, width // CHUNK, N], F32, name="rr", tag="rr", bufs=2)
+            rr = psum.tile([P, width // CHUNK, N], F32, name="rr", tag=tag, bufs=bufs)
             for c in range(width // CHUNK):
                 cols = slice(c * CHUNK, (c + 1) * CHUNK)
                 product(rr[:, c, :], (h_codes[:, cols], h_scales[:, cols]), w2_quantised)
             return rr
 
-        def summed(g, rr):
-            first, width = starts[g], GROUPS[g]
-            term = keep.tile([P, width // CHUNK, N], F32, name=f"term{g}")
-            chunks = slice(first // CHUNK, (first + width) // CHUNK)
-            nc.vector.tensor_tensor(term[:], rr[:], lb_turned[:, chunks, :], MULT)
-            total = psum.tile([P, width], F32, name="total", tag="total", bufs=2)
-            for c in range(width // CHUNK):
-                for turn, addend in enumerate((ee_turned[:, first // CHUNK + c, :], term[:, c, :])):
-                    nc.tensor.matmul(
-                        total[:, c * CHUNK : (c + 1) * CHUNK],
-                        lhsT=addend,
-                        rhs=identity[:],
-                        is_transpose=True,
-                        start=turn == 0,
-                        stop=turn == 1,
-                    )
+        def turned_back(total, addend, opens):
+            count = addend.shape[1]
+            for c in range(count):
+                nc.tensor.matmul(
+                    total[:, c * CHUNK : (c + 1) * CHUNK],
+                    lhsT=addend[:, c, :],
+                    rhs=identity[:],
+                    is_transpose=True,
+                    start=opens and c == 0,
+                    stop=not opens and c == count - 1,
+                )
+
+        def chunks_of(g):
+            return slice(starts[g] // CHUNK, (starts[g] + GROUPS[g]) // CHUNK)
+
+        def opened(g, tag, bufs):
+            total = psum.tile([P, GROUPS[g]], F32, name="total", tag=tag, bufs=bufs)
+            turned_back(total, ee_turned[:, chunks_of(g), :], True)
             return total
+
+        def summed(g, rr, total):
+            shape = [P, GROUPS[g] // CHUNK, N]
+            if g == 1:
+                term = turns.tile(shape, F32, name="term1", offset=22 * KIB, align_bytes=64)
+            else:
+                term = keep.tile(shape, F32, name=f"term{g}")
+            nc.vector.tensor_tensor(term[:], rr[:], lb_turned[:, chunks_of(g), :], MULT)
+            turned_back(total, term[:], False)
 
         def finish(g, total):
             first, width = starts[g], GROUPS[g]
@@ -248,28 +259,33 @@ def tile_picked_yvera_silu_p_kernel(
             queue = nc.scalar if g == last else nc.sync
             queue.dma_start(out[:, first : first + width], result[:])
 
+        first_plane(0)
+        w3_quantised, w2_quantised = quantised_w3_w2()
         y0 = copied_planes(0)
-        first_plane(0, ((0, 1),))
         y1 = copied_planes(1)
         y2 = copied_planes(2)
-        first_plane(BANK, ((2, 3), (4,)))
-        w3_quantised, w2_quantised = quantised_w3_w2()
+        first_plane(BANK)
         h0 = hidden(0, y0)
         y3 = copied_planes(3)
         y4 = copied_planes(4)
         h1 = hidden(1, y1)
-        rr0 = second_product(0, h0, w2_quantised)
+        rr0 = second_product(0, h0, w2_quantised, "rr", 2)
         frozen_layer(w3_quantised)
+        totals = [opened(g, "total", 2) if g < 2 else opened(g, "y", 4) for g in range(len(GROUPS))]
         h2 = hidden(2, y2)
-        finish(0, summed(0, rr0))
-        rr1 = second_product(1, h1, w2_quantised)
+        summed(0, rr0, totals[0])
+        rr1 = second_product(1, h1, w2_quantised, "rr", 2)
         h3 = hidden(3, y3)
-        finish(1, summed(1, rr1))
-        rr2 = second_product(2, h2, w2_quantised)
         h4 = hidden(4, y4)
-        total2 = summed(2, rr2)
-        rr3 = second_product(3, h3, w2_quantised)
-        rr4 = second_product(4, h4, w2_quantised)
-        finish(2, total2)
-        finish(3, summed(3, rr3))
-        finish(4, summed(4, rr4))
+        finish(0, totals[0])
+        rr2 = second_product(2, h2, w2_quantised, "rr", 2)
+        summed(1, rr1, totals[1])
+        rr3 = second_product(3, h3, w2_quantised, "y", 4)
+        finish(1, totals[1])
+        summed(2, rr2, totals[2])
+        rr4 = second_product(4, h4, w2_quantised, "rr", 2)
+        finish(2, totals[2])
+        summed(3, rr3, totals[3])
+        finish(3, totals[3])
+        summed(4, rr4, totals[4])
+        finish(4, totals[4])

@@ -25,7 +25,6 @@ CHUNK = 128
 RUN = 4
 GROUPS = (256, 256, 256, 128, 128)
 WINDOW = R + 32
-CLEARED_BY_GPSIMD = 640
 
 
 def tile_picked_yvera_silu_p_kernel(
@@ -53,8 +52,7 @@ def tile_picked_yvera_silu_p_kernel(
         def entries(index_list, first, count):
             return index_list[:, first // LIST : (first + count) // LIST]
 
-        nc.gpsimd.memset(scale_table[:].bitcast(I32)[:, :CLEARED_BY_GPSIMD], 0)
-        nc.vector.memset(scale_table[:].bitcast(I32)[:, CLEARED_BY_GPSIMD:], 0)
+        nc.vector.memset(scale_table[:].bitcast(I32), 0)
         nc.vector.memset(lb_table[:, R:], 0.0)
         nc.vector.memset(ld_first[:, R:], 0.0)
         nc.vector.memset(x_bytes[:].bitcast(I32), 0)
@@ -67,29 +65,30 @@ def tile_picked_yvera_silu_p_kernel(
 
         nc.sync.dma_start(lb_table[:, :R], lb)
         nc.sync.dma_start(ad_list[:], ad)
-        nc.sync.dma_start(token_list[:], offs)
         ld_rows = ld.rearrange("(p t) r -> p t r", t=PACK)
         nc.sync.dma_start(ld_first[:, :R], ld_rows[:, 0, :])
-        nc.sync.dma_start(scale_table[0:P:8, :].bitcast(I32), x_scales[0].bitcast(I32))
+        nc.sync.dma_start(token_list[:], offs)
         nc.sync.dma_start(w1_raw[:], w1.rearrange("(p j) c -> p j c", j=PACK))
+        nc.sync.dma_start(scale_table[0:P:8, :].bitcast(I32), x_scales[0].bitcast(I32))
         nc.sync.dma_start(word_table[:], x_words[0].rearrange("p c t -> p (c t)").bitcast(I32))
 
         def picked_columns(target, table, first):
-            nc.vector.tensor_copy(target[:, first : first + BANK], table[:].indirect(entries(ad_list, first, BANK)))
+            nc.vector.tensor_copy(target, table[:].indirect(entries(ad_list, first, BANK)))
 
         lb_picked = keep.tile([P, S], F32, name="lb_picked")
-        picked_columns(lb_picked, lb_table, 0)
+        for first in range(0, S, BANK):
+            picked_columns(lb_picked[:, first : first + BANK], lb_table, first)
+        ld_picked = [
+            turns.tile([P, BANK], F32, name=f"ld_picked{half}", offset=2 * half * KIB) for half in range(S // BANK)
+        ]
+        picked_columns(ld_picked[0][:], ld_first, 0)
         spread_bytes = keep.tile([P, S], U8, name="spread_bytes")
         nc.vector.tensor_copy(spread_bytes[:], scale_table[:].indirect(token_list[:]))
         for r in range(4):
             nc.sync.dma_start(
                 x_bytes[r:P:32, :].bitcast(I32), spread_bytes[8 * r : P : 32, :].bitcast(I32)
             )
-        picked_columns(lb_picked, lb_table, BANK)
-
-        ld_picked = turns.tile([P, S], F32, name="ld_picked", offset=0)
-        for first in range(0, S, BANK):
-            picked_columns(ld_picked, ld_first, first)
+        picked_columns(ld_picked[1][:], ld_first, BANK)
         w32_raw = []
         for slot, weight in enumerate((w3, w2)):
             raw = turns.tile([P, PACK, N], F32, name=f"w32_raw{slot}", offset=(4 + 2 * slot) * KIB)
@@ -154,7 +153,7 @@ def tile_picked_yvera_silu_p_kernel(
         def first_plane(first):
             y = psum.tile([P, BANK], F32, name="y_first", tag="y", bufs=4)
             product(y[:], w1_plane(0), picked_x(first, BANK))
-            nc.vector.tensor_tensor(h_rows[:, 1 - first // BANK, :], y[:], ld_picked[:, first : first + BANK], MULT)
+            nc.vector.tensor_tensor(h_rows[:, 1 - first // BANK, :], y[:], ld_picked[first // BANK][:], MULT)
 
         def copied_planes(g):
             first, width = starts[g], GROUPS[g]

@@ -25,6 +25,7 @@ CHUNK = 128
 RUN = 4
 GROUPS = (256, 256, 256, 128, 128)
 WINDOW = R + 32
+BANKS = {"y": 4, "rr": 2, "total": 2}
 
 
 def tile_picked_yvera_silu_p_kernel(
@@ -85,9 +86,7 @@ def tile_picked_yvera_silu_p_kernel(
         spread_bytes = keep.tile([P, S], U8, name="spread_bytes")
         nc.vector.tensor_copy(spread_bytes[:], scale_table[:].indirect(token_list[:]))
         for r in range(4):
-            nc.sync.dma_start(
-                x_bytes[r:P:32, :].bitcast(I32), spread_bytes[8 * r : P : 32, :].bitcast(I32)
-            )
+            nc.sync.dma_start(x_bytes[r:P:32, :].bitcast(I32), spread_bytes[8 * r : P : 32, :].bitcast(I32))
         picked_columns(ld_picked[1][:], ld_first, BANK)
         w32_raw = []
         for slot, weight in enumerate((w3, w2)):
@@ -109,7 +108,7 @@ def tile_picked_yvera_silu_p_kernel(
         per_bank = BANK // CHUNK
         lb_turned = turns.tile([P, S // CHUNK, N], F32, name="lb_turned", offset=18 * KIB)
         for c0 in range(0, S // CHUNK, per_bank):
-            bank = psum.tile([P, per_bank, N], F32, name="lb_bank", tag="total", bufs=2)
+            bank = psum.tile([P, per_bank, N], F32, name="lb_bank", tag="total", bufs=BANKS["total"])
             for c in range(per_bank):
                 first = (c0 + c) * CHUNK
                 nc.tensor.transpose(bank[:, c, :], lb_picked[:, first : first + CHUNK], identity[:])
@@ -151,18 +150,24 @@ def tile_picked_yvera_silu_p_kernel(
             return h_rows[:, 1 - half : 1 - half + PACK, col : col + GROUPS[g]]
 
         def first_plane(first):
-            y = psum.tile([P, BANK], F32, name="y_first", tag="y", bufs=4)
+            y = psum.tile([P, BANK], F32, name="y_first", tag="y", bufs=BANKS["y"])
             product(y[:], w1_plane(0), picked_x(first, BANK))
             nc.vector.tensor_tensor(h_rows[:, 1 - first // BANK, :], y[:], ld_picked[first // BANK][:], MULT)
 
         def copied_planes(g):
             first, width = starts[g], GROUPS[g]
-            if g < 2:
+            if starts[g] < BANK:
                 y_sb = turns.tile([P, (PACK - 1) * width], F32, name=f"y_sb{g}", offset=(4 + 3 * g) * KIB)
             else:
                 y_sb = keep.tile([P, (PACK - 1) * width], F32, name=f"y_sb{g}")
-            for planes in ((1, 2, 3),) if (PACK - 1) * width <= BANK else ((1,), (2, 3)):
-                y = psum.tile([P, len(planes) * width], F32, name="y", tag="y", bufs=4)
+            if g == 0:
+                batches = ((1,), (2,), (3,))
+            elif (PACK - 1) * width <= BANK:
+                batches = ((1, 2, 3),)
+            else:
+                batches = ((1,), (2, 3))
+            for planes in batches:
+                y = psum.tile([P, len(planes) * width], F32, name="y", tag="y", bufs=BANKS["y"])
                 for place, t in enumerate(planes):
                     product(y[:, place * width : (place + 1) * width], w1_plane(t), picked_x(first, width))
                 nc.scalar.copy(y_sb[:, (planes[0] - 1) * width : planes[-1] * width], y[:])
@@ -178,10 +183,7 @@ def tile_picked_yvera_silu_p_kernel(
                     y_sb[:, (t - 1) * width : t * width],
                     MULT,
                 )
-            if g == 2:
-                h_bf = turns.tile([P, width * PACK], BF16, name="h_bf2", offset=22 * KIB, align_bytes=64)
-            else:
-                h_bf = keep.tile([P, width * PACK], BF16, name=f"h_bf{g}", align_bytes=64)
+            h_bf = keep.tile([P, width * PACK], BF16, name=f"h_bf{g}", align_bytes=64)
             nc.scalar.copy(
                 h_bf[:].rearrange("p (c i t) -> p c t i", i=RUN, t=PACK),
                 h_planes.rearrange("p t (c i) -> p c t i", i=RUN),
@@ -206,17 +208,17 @@ def tile_picked_yvera_silu_p_kernel(
 
         def frozen_layer(w3_quantised):
             for c0 in range(0, S // CHUNK, per_bank):
-                bank = psum.tile([P, per_bank, N], F32, name="ee_bank", tag="y", bufs=4)
+                bank = psum.tile([P, per_bank, N], F32, name="ee_bank", tag="y", bufs=BANKS["y"])
                 for c in range(per_bank):
                     product(bank[:, c, :], picked_x((c0 + c) * CHUNK, CHUNK), w3_quantised)
                 nc.scalar.copy(ee_turned[:, c0 : c0 + per_bank, :], bank[:])
 
-        def second_product(g, h_bf, w2_quantised, tag, bufs):
+        def second_product(g, h_bf, w2_quantised, tag):
             width = GROUPS[g]
             h_codes = keep.tile([P, width], U32, name=f"h_codes{g}", align_bytes=64)
             h_scales = keep.tile([P, width], U8, name=f"h_scales{g}", align_bytes=64)
             nc.vector.quantize_mx(h_codes[:].bitcast(FP8X4), h_scales[:], h_bf[:])
-            rr = psum.tile([P, width // CHUNK, N], F32, name="rr", tag=tag, bufs=bufs)
+            rr = psum.tile([P, width // CHUNK, N], F32, name="rr", tag=tag, bufs=BANKS[tag])
             for c in range(width // CHUNK):
                 cols = slice(c * CHUNK, (c + 1) * CHUNK)
                 product(rr[:, c, :], (h_codes[:, cols], h_scales[:, cols]), w2_quantised)
@@ -237,19 +239,19 @@ def tile_picked_yvera_silu_p_kernel(
         def chunks_of(g):
             return slice(starts[g] // CHUNK, (starts[g] + GROUPS[g]) // CHUNK)
 
-        def opened(g, tag, bufs):
-            total = psum.tile([P, GROUPS[g]], F32, name="total", tag=tag, bufs=bufs)
+        def opened(g, tag):
+            total = psum.tile([P, GROUPS[g]], F32, name="total", tag=tag, bufs=BANKS[tag])
             turned_back(total, ee_turned[:, chunks_of(g), :], True)
             return total
 
         def summed(g, rr, total):
-            shape = [P, GROUPS[g] // CHUNK, N]
             if g == 1:
-                term = turns.tile(shape, F32, name="term1", offset=22 * KIB, align_bytes=64)
+                term = planes_of(2)[:, PACK - 1, :].rearrange("p (c n) -> p c n", n=N)
             else:
-                term = keep.tile(shape, F32, name=f"term{g}")
-            nc.vector.tensor_tensor(term[:], rr[:], lb_turned[:, chunks_of(g), :], MULT)
-            turned_back(total, term[:], False)
+                own = keep.tile([P, GROUPS[g] // CHUNK, N], F32, name=f"term{g}")
+                term = own[:]
+            nc.vector.tensor_tensor(term, rr[:], lb_turned[:, chunks_of(g), :], MULT)
+            turned_back(total, term, False)
 
         def finish(g, total):
             first, width = starts[g], GROUPS[g]
@@ -268,21 +270,21 @@ def tile_picked_yvera_silu_p_kernel(
         y3 = copied_planes(3)
         y4 = copied_planes(4)
         h1 = hidden(1, y1)
-        rr0 = second_product(0, h0, w2_quantised, "rr", 2)
+        rr0 = second_product(0, h0, w2_quantised, "rr")
         frozen_layer(w3_quantised)
-        totals = [opened(g, "total", 2) if g < 2 else opened(g, "y", 4) for g in range(len(GROUPS))]
+        totals = [opened(g, "total" if g < BANKS["total"] else "y") for g in range(len(GROUPS))]
         h2 = hidden(2, y2)
         summed(0, rr0, totals[0])
-        rr1 = second_product(1, h1, w2_quantised, "rr", 2)
+        rr1 = second_product(1, h1, w2_quantised, "rr")
         h3 = hidden(3, y3)
         h4 = hidden(4, y4)
         finish(0, totals[0])
-        rr2 = second_product(2, h2, w2_quantised, "rr", 2)
+        rr2 = second_product(2, h2, w2_quantised, "rr")
         summed(1, rr1, totals[1])
-        rr3 = second_product(3, h3, w2_quantised, "y", 4)
+        rr3 = second_product(3, h3, w2_quantised, "y")
         finish(1, totals[1])
         summed(2, rr2, totals[2])
-        rr4 = second_product(4, h4, w2_quantised, "rr", 2)
+        rr4 = second_product(4, h4, w2_quantised, "rr")
         finish(2, totals[2])
         summed(3, rr3, totals[3])
         finish(3, totals[3])

@@ -15,6 +15,7 @@ U8 = mybir.dt.uint8
 FP8X4 = mybir.dt.float8_e4m3fn_x4
 MULT = mybir.AluOpType.mult
 SILU = mybir.ActivationFunctionType.Silu
+COPY = mybir.ActivationFunctionType.Copy
 
 P = 128
 KIB = 1024
@@ -22,10 +23,11 @@ PACK = 4
 LIST = 16
 BANK = 512
 CHUNK = 128
+PIECE = 256
 RUN = 4
+PAIR = 2
 GROUPS = (256, 256, 256, 128, 128)
-WINDOW = R + 32
-BANKS = {"y": 4, "rr": 2, "total": 2}
+BANKS = {"y": 3, "rr": 2, "total": 3}
 
 
 def tile_picked_yvera_silu_p_kernel(
@@ -40,22 +42,18 @@ def tile_picked_yvera_silu_p_kernel(
 
         ad_list = lists.tile([P, S // LIST], U16, name="ad_list")
         token_list = lists.tile([P, S // LIST], U16, name="token_list")
-        ld_first = keep.tile([P, WINDOW], F32, name="ld_first")
-        ld_tables = {
-            t: turns.tile([P, R], F32, name=f"ld_table{t}", offset=(10 + 2 * t) * KIB) for t in range(1, PACK)
-        }
-        lb_table = keep.tile([P, WINDOW], F32, name="lb_table")
+        ld_tables = [keep.tile([P, R], F32, name=f"ld_table{t}") for t in range(2)]
+        ld_tables.extend(turns.tile([P, R], F32, name=f"ld_table{t}", offset=2 * (t - 2) * KIB) for t in range(2, PACK))
+        lb_table = keep.tile([P, R], F32, name="lb_table")
         word_table = keep.tile([P, T], I32, name="word_table")
-        scale_table = turns.tile([P, T], U8, name="scale_table", offset=4 * KIB - 32)
-        w1_raw = turns.tile([P, PACK, H], F32, name="w1_raw", offset=12 * KIB)
+        scale_table = turns.tile([P, T], U8, name="scale_table", offset=2 * KIB - 32)
+        w1_raw = turns.tile([P, PACK, H], F32, name="w1_raw", offset=6 * KIB)
         x_bytes = keep.tile([P, S], U8, name="x_bytes", align_bytes=64)
 
         def entries(index_list, first, count):
             return index_list[:, first // LIST : (first + count) // LIST]
 
         nc.vector.memset(scale_table[:].bitcast(I32), 0)
-        nc.vector.memset(lb_table[:, R:], 0.0)
-        nc.vector.memset(ld_first[:, R:], 0.0)
         nc.vector.memset(x_bytes[:].bitcast(I32), 0)
         warm_in = keep.tile([P, 1], F32, name="warm_in")
         warm_out = keep.tile([P, 1], F32, name="warm_out")
@@ -64,49 +62,63 @@ def tile_picked_yvera_silu_p_kernel(
         identity = keep.tile([P, P], F32, name="identity")
         make_identity(nc, identity[:])
 
-        nc.sync.dma_start(lb_table[:, :R], lb)
-        nc.sync.dma_start(ad_list[:], ad)
         ld_rows = ld.rearrange("(p t) r -> p t r", t=PACK)
-        nc.sync.dma_start(ld_first[:, :R], ld_rows[:, 0, :])
+        nc.sync.dma_start(ad_list[:], ad)
+        nc.sync.dma_start(ld_tables[0][:], ld_rows[:, 0, :])
+        nc.sync.dma_start(lb_table[:], lb)
         nc.sync.dma_start(token_list[:], offs)
-        nc.sync.dma_start(w1_raw[:], w1.rearrange("(p j) c -> p j c", j=PACK))
         nc.sync.dma_start(scale_table[0:P:8, :].bitcast(I32), x_scales[0].bitcast(I32))
+        nc.sync.dma_start(ld_tables[1][:], ld_rows[:, 1, :])
+        nc.sync.dma_start(w1_raw[:], w1.rearrange("(p j) c -> p j c", j=PACK))
         nc.sync.dma_start(word_table[:], x_words[0].rearrange("p c t -> p (c t)").bitcast(I32))
 
-        def picked_columns(target, table, first):
-            nc.vector.tensor_copy(target, table[:].indirect(entries(ad_list, first, BANK)))
+        def on_vector(target, table, first):
+            nc.vector.tensor_copy(target, table[:].indirect(entries(ad_list, first, PIECE)))
 
+        def on_scalar(target, table, first):
+            nc.scalar.activation(target, table[:].indirect(entries(ad_list, first, PIECE)), COPY)
+
+        ld_picked = keep.tile([P, PACK + 2, BANK], F32, name="ld_picked")
+
+        def picked_planes(first, width):
+            half, col = divmod(first, BANK)
+            row = 2 - 2 * half
+            return ld_picked[:, row : row + PACK, col : col + width]
+
+        def look_up(engine, t, first):
+            engine(picked_planes(first, PIECE)[:, t, :], ld_tables[t], first)
+
+        pieces = range(0, S, PIECE)
         lb_picked = keep.tile([P, S], F32, name="lb_picked")
-        for first in range(0, S, BANK):
-            picked_columns(lb_picked[:, first : first + BANK], lb_table, first)
-        ld_picked = [
-            turns.tile([P, BANK], F32, name=f"ld_picked{half}", offset=2 * half * KIB) for half in range(S // BANK)
-        ]
-        picked_columns(ld_picked[0][:], ld_first, 0)
+        for first in pieces:
+            look_up(on_scalar, 0, first)
+        for first in pieces:
+            engine = on_vector if first < BANK else on_scalar
+            engine(lb_picked[:, first : first + PIECE], lb_table, first)
         spread_bytes = keep.tile([P, S], U8, name="spread_bytes")
         nc.vector.tensor_copy(spread_bytes[:], scale_table[:].indirect(token_list[:]))
         for r in range(4):
             nc.sync.dma_start(x_bytes[r:P:32, :].bitcast(I32), spread_bytes[8 * r : P : 32, :].bitcast(I32))
-        picked_columns(ld_picked[1][:], ld_first, BANK)
-        w32_raw = []
-        for slot, weight in enumerate((w3, w2)):
-            raw = turns.tile([P, PACK, N], F32, name=f"w32_raw{slot}", offset=(4 + 2 * slot) * KIB)
-            nc.sync.dma_start(raw[:], weight.rearrange("(p j) c -> p j c", j=PACK))
-            w32_raw.append(raw)
+        for first in pieces:
+            look_up(on_vector, 1, first)
+        for t in range(2, PACK):
+            nc.sync.dma_start(ld_tables[t][:], ld_rows[:, t, :])
+        w3_raw = turns.tile([P, PACK, N], F32, name="w3_raw", offset=4 * KIB)
+        nc.sync.dma_start(w3_raw[:], w3.rearrange("(p j) c -> p j c", j=PACK))
 
         w1_bf = keep.tile([P, PACK * H], BF16, name="w1_bf", align_bytes=64)
         nc.scalar.copy(
             w1_bf[:].rearrange("p (t m j) -> p m t j", t=PACK, j=PACK),
             w1_raw[:].rearrange("p j (m t) -> p m t j", t=PACK),
         )
-        for t in range(1, PACK):
-            nc.sync.dma_start(ld_tables[t][:], ld_rows[:, t, :])
+        w2_raw = turns.tile([P, PACK, N], F32, name="w2_raw", offset=6 * KIB)
+        nc.sync.dma_start(w2_raw[:], w2.rearrange("(p j) c -> p j c", j=PACK))
         w1_codes = keep.tile([P, H], U32, name="w1_codes", align_bytes=64)
         w1_scales = keep.tile([P, H], U8, name="w1_scales", align_bytes=64)
         nc.vector.quantize_mx(w1_codes[:].bitcast(FP8X4), w1_scales[:], w1_bf[:])
 
         per_bank = BANK // CHUNK
-        lb_turned = turns.tile([P, S // CHUNK, N], F32, name="lb_turned", offset=18 * KIB)
+        lb_turned = turns.tile([P, S // CHUNK, N], F32, name="lb_turned", offset=8 * KIB)
         for c0 in range(0, S // CHUNK, per_bank):
             bank = psum.tile([P, per_bank, N], F32, name="lb_bank", tag="total", bufs=BANKS["total"])
             for c in range(per_bank):
@@ -143,83 +155,56 @@ def tile_picked_yvera_silu_p_kernel(
         starts = [sum(GROUPS[:g]) for g in range(len(GROUPS))]
         last = len(GROUPS) - 1
 
-        h_rows = keep.tile([P, PACK + 1, BANK], F32, name="h_rows")
+        def late_planes(first):
+            for t in range(2, PACK):
+                look_up(on_scalar, t, first)
 
-        def planes_of(g):
-            half, col = divmod(starts[g], BANK)
-            return h_rows[:, 1 - half : 1 - half + PACK, col : col + GROUPS[g]]
-
-        def first_plane(first):
-            y = psum.tile([P, BANK], F32, name="y_first", tag="y", bufs=BANKS["y"])
-            product(y[:], w1_plane(0), picked_x(first, BANK))
-            nc.vector.tensor_tensor(h_rows[:, 1 - first // BANK, :], y[:], ld_picked[first // BANK][:], MULT)
-
-        def copied_planes(g):
+        def hidden(g):
             first, width = starts[g], GROUPS[g]
-            if starts[g] < BANK:
-                y_sb = turns.tile([P, (PACK - 1) * width], F32, name=f"y_sb{g}", offset=(4 + 3 * g) * KIB)
-            else:
-                y_sb = keep.tile([P, (PACK - 1) * width], F32, name=f"y_sb{g}")
-            if g == 0:
-                batches = ((1,), (2,), (3,))
-            elif (PACK - 1) * width <= BANK:
-                batches = ((1, 2, 3),)
-            else:
-                batches = ((1,), (2, 3))
-            for planes in batches:
-                y = psum.tile([P, len(planes) * width], F32, name="y", tag="y", bufs=BANKS["y"])
-                for place, t in enumerate(planes):
-                    product(y[:, place * width : (place + 1) * width], w1_plane(t), picked_x(first, width))
-                nc.scalar.copy(y_sb[:, (planes[0] - 1) * width : planes[-1] * width], y[:])
-            return y_sb
-
-        def hidden(g, y_sb):
-            first, width = starts[g], GROUPS[g]
-            h_planes = planes_of(g)
-            for t in range(1, PACK):
+            h_bf = keep.tile([P, width * PACK], BF16, name=f"h_bf{g}", align_bytes=64)
+            for col in range(0, width, CHUNK):
+                y = psum.tile([P, PACK, CHUNK], F32, name="y", tag="y", bufs=BANKS["y"])
+                for t in range(PACK):
+                    product(y[:, t, :], w1_plane(t), picked_x(first + col, CHUNK))
                 nc.vector.tensor_tensor(
-                    h_planes[:, t, :],
-                    ld_tables[t][:].indirect(entries(ad_list, first, width)),
-                    y_sb[:, (t - 1) * width : t * width],
+                    h_bf[:, col * PACK : (col + CHUNK) * PACK].rearrange("p (c i t) -> p c t i", i=PAIR, t=PACK),
+                    y[:].rearrange("p t (c i) -> p c t i", i=PAIR),
+                    picked_planes(first + col, CHUNK).rearrange("p t (c i) -> p c t i", i=PAIR),
                     MULT,
                 )
-            h_bf = keep.tile([P, width * PACK], BF16, name=f"h_bf{g}", align_bytes=64)
-            nc.scalar.copy(
-                h_bf[:].rearrange("p (c i t) -> p c t i", i=RUN, t=PACK),
-                h_planes.rearrange("p t (c i) -> p c t i", i=RUN),
-            )
             return h_bf
 
-        def quantised_w3_w2():
-            w32_bf = keep.tile([P, 2, N, PACK], BF16, name="w32_bf", align_bytes=64)
-            for slot in range(2):
-                nc.scalar.copy(
-                    w32_bf[:, slot].rearrange("p (c i) j -> p c j i", i=RUN),
-                    w32_raw[slot][:].rearrange("p j (c i) -> p c j i", i=RUN),
-                )
-            codes = keep.tile([P, 2 * N], U32, name="w32_codes", align_bytes=64)
-            scales = keep.tile([P, 2 * N], U8, name="w32_scales", align_bytes=64)
-            nc.vector.quantize_mx(
-                codes[:].bitcast(FP8X4), scales[:], w32_bf[:].rearrange("p w c j -> p (w c j)")
+        def quantised(name, raw):
+            rounded = keep.tile([P, N, PACK], BF16, name=f"{name}_bf", align_bytes=64)
+            nc.scalar.copy(
+                rounded[:].rearrange("p (c i) j -> p c j i", i=RUN),
+                raw[:].rearrange("p j (c i) -> p c j i", i=RUN),
             )
-            return (codes[:, :N], scales[:, :N]), (codes[:, N:], scales[:, N:])
+            codes = keep.tile([P, N], U32, name=f"{name}_codes", align_bytes=64)
+            scales = keep.tile([P, N], U8, name=f"{name}_scales", align_bytes=64)
+            nc.vector.quantize_mx(codes[:].bitcast(FP8X4), scales[:], rounded[:].rearrange("p c j -> p (c j)"))
+            return codes[:], scales[:]
 
         ee_turned = keep.tile([P, S // CHUNK, N], F32, name="ee_turned")
 
         def frozen_layer(w3_quantised):
             for c0 in range(0, S // CHUNK, per_bank):
-                bank = psum.tile([P, per_bank, N], F32, name="ee_bank", tag="y", bufs=BANKS["y"])
+                bank = psum.tile([P, per_bank, N], F32, name="ee_bank", tag="total", bufs=BANKS["total"])
                 for c in range(per_bank):
                     product(bank[:, c, :], picked_x((c0 + c) * CHUNK, CHUNK), w3_quantised)
                 nc.scalar.copy(ee_turned[:, c0 : c0 + per_bank, :], bank[:])
 
-        def second_product(g, h_bf, w2_quantised, tag):
+        def quantised_hidden(g, h_bf):
             width = GROUPS[g]
             h_codes = keep.tile([P, width], U32, name=f"h_codes{g}", align_bytes=64)
             h_scales = keep.tile([P, width], U8, name=f"h_scales{g}", align_bytes=64)
             nc.vector.quantize_mx(h_codes[:].bitcast(FP8X4), h_scales[:], h_bf[:])
-            rr = psum.tile([P, width // CHUNK, N], F32, name="rr", tag=tag, bufs=BANKS[tag])
-            for c in range(width // CHUNK):
+            return h_codes, h_scales
+
+        def second_product(g, h_quantised, w2_quantised, tag):
+            h_codes, h_scales = h_quantised
+            rr = psum.tile([P, GROUPS[g] // CHUNK, N], F32, name="rr", tag=tag, bufs=BANKS[tag])
+            for c in range(GROUPS[g] // CHUNK):
                 cols = slice(c * CHUNK, (c + 1) * CHUNK)
                 product(rr[:, c, :], (h_codes[:, cols], h_scales[:, cols]), w2_quantised)
             return rr
@@ -245,13 +230,9 @@ def tile_picked_yvera_silu_p_kernel(
             return total
 
         def summed(g, rr, total):
-            if g == 1:
-                term = planes_of(2)[:, PACK - 1, :].rearrange("p (c n) -> p c n", n=N)
-            else:
-                own = keep.tile([P, GROUPS[g] // CHUNK, N], F32, name=f"term{g}")
-                term = own[:]
-            nc.vector.tensor_tensor(term, rr[:], lb_turned[:, chunks_of(g), :], MULT)
-            turned_back(total, term, False)
+            term = keep.tile([P, GROUPS[g] // CHUNK, N], F32, name=f"term{g}")
+            nc.vector.tensor_tensor(term[:], rr[:], lb_turned[:, chunks_of(g), :], MULT)
+            turned_back(total, term[:], False)
 
         def finish(g, total):
             first, width = starts[g], GROUPS[g]
@@ -260,33 +241,37 @@ def tile_picked_yvera_silu_p_kernel(
             queue = nc.scalar if g == last else nc.sync
             queue.dma_start(out[:, first : first + width], result[:])
 
-        first_plane(0)
-        w3_quantised, w2_quantised = quantised_w3_w2()
-        y0 = copied_planes(0)
-        y1 = copied_planes(1)
-        y2 = copied_planes(2)
-        first_plane(BANK)
-        h0 = hidden(0, y0)
-        y3 = copied_planes(3)
-        y4 = copied_planes(4)
-        h1 = hidden(1, y1)
-        rr0 = second_product(0, h0, w2_quantised, "rr")
+        late_planes(0)
+        late_planes(PIECE)
+        h0 = hidden(0)
+        w3_quantised = quantised("w3", w3_raw)
+        late_planes(2 * PIECE)
+        h1 = hidden(1)
+        q0 = quantised_hidden(0, h0)
+        w2_quantised = quantised("w2", w2_raw)
+        late_planes(3 * PIECE)
+        h2 = hidden(2)
+        q1 = quantised_hidden(1, h1)
         frozen_layer(w3_quantised)
-        totals = [opened(g, "total" if g < BANKS["total"] else "y") for g in range(len(GROUPS))]
-        h2 = hidden(2, y2)
+        h3 = hidden(3)
+        q2 = quantised_hidden(2, h2)
+        h4 = hidden(4)
+        rr0 = second_product(0, q0, w2_quantised, "rr")
+        rr1 = second_product(1, q1, w2_quantised, "rr")
+        q3 = quantised_hidden(3, h3)
+        totals = [opened(g, "total") for g in range(3)]
         summed(0, rr0, totals[0])
-        rr1 = second_product(1, h1, w2_quantised, "rr")
-        h3 = hidden(3, y3)
-        h4 = hidden(4, y4)
-        finish(0, totals[0])
-        rr2 = second_product(2, h2, w2_quantised, "rr")
+        q4 = quantised_hidden(4, h4)
+        rr2 = second_product(2, q2, w2_quantised, "y")
+        rr3 = second_product(3, q3, w2_quantised, "rr")
+        totals.extend(opened(g, "y") for g in range(3, 5))
         summed(1, rr1, totals[1])
-        rr3 = second_product(3, h3, w2_quantised, "y")
-        finish(1, totals[1])
+        rr4 = second_product(4, q4, w2_quantised, "rr")
+        finish(0, totals[0])
         summed(2, rr2, totals[2])
-        rr4 = second_product(4, h4, w2_quantised, "rr")
-        finish(2, totals[2])
+        finish(1, totals[1])
         summed(3, rr3, totals[3])
-        finish(3, totals[3])
+        finish(2, totals[2])
         summed(4, rr4, totals[4])
+        finish(3, totals[3])
         finish(4, totals[4])

@@ -78,12 +78,12 @@ def tile_picked_yvera_silu_p_kernel(
         def on_scalar(target, table, first):
             nc.scalar.activation(target, table[:].indirect(entries(ad_list, first, PIECE)), COPY)
 
-        ld_picked = keep.tile([P, PACK + 2, BANK], F32, name="ld_picked")
+        ld_picked = [keep.tile([P, PACK + 2, PIECE], F32, name=f"ld_picked{u}") for u in range(2)]
 
         def picked_planes(first, width):
-            half, col = divmod(first, BANK)
-            row = 2 - 2 * half
-            return ld_picked[:, row : row + PACK, col : col + width]
+            piece, col = divmod(first, PIECE)
+            row = 2 - 2 * (piece // 2)
+            return ld_picked[piece % 2][:, row : row + PACK, col : col + width]
 
         def look_up(engine, t, first):
             engine(picked_planes(first, PIECE)[:, t, :], ld_tables[t], first)
@@ -185,7 +185,7 @@ def tile_picked_yvera_silu_p_kernel(
             nc.vector.quantize_mx(codes[:].bitcast(FP8X4), scales[:], rounded[:].rearrange("p c j -> p (c j)"))
             return codes[:], scales[:]
 
-        ee_turned = keep.tile([P, S // CHUNK, N], F32, name="ee_turned")
+        ee_turned = turns.tile([P, S // CHUNK, N], F32, name="ee_turned", offset=0)
 
         def frozen_layer(w3_quantised):
             for c0 in range(0, S // CHUNK, per_bank):

@@ -78,12 +78,11 @@ def tile_picked_yvera_silu_p_kernel(
         def on_scalar(target, table, first):
             nc.scalar.activation(target, table[:].indirect(entries(ad_list, first, PIECE)), COPY)
 
-        ld_picked = [keep.tile([P, PACK + 2, PIECE], F32, name=f"ld_picked{u}") for u in range(2)]
+        ld_picked = [keep.tile([P, PACK, PIECE], F32, name=f"ld_picked{u}") for u in range(S // PIECE)]
 
         def picked_planes(first, width):
             piece, col = divmod(first, PIECE)
-            row = 2 - 2 * (piece // 2)
-            return ld_picked[piece % 2][:, row : row + PACK, col : col + width]
+            return ld_picked[piece][:, :, col : col + width]
 
         def look_up(engine, t, first):
             engine(picked_planes(first, PIECE)[:, t, :], ld_tables[t], first)
@@ -241,21 +240,19 @@ def tile_picked_yvera_silu_p_kernel(
             queue = nc.scalar if g == last else nc.sync
             queue.dma_start(out[:, first : first + width], result[:])
 
-        late_planes(0)
-        late_planes(PIECE)
+        for first in pieces:
+            late_planes(first)
         h0 = hidden(0)
-        w3_quantised = quantised("w3", w3_raw)
-        late_planes(2 * PIECE)
         h1 = hidden(1)
         q0 = quantised_hidden(0, h0)
-        w2_quantised = quantised("w2", w2_raw)
-        late_planes(3 * PIECE)
         h2 = hidden(2)
         q1 = quantised_hidden(1, h1)
-        frozen_layer(w3_quantised)
+        w3_quantised = quantised("w3", w3_raw)
+        w2_quantised = quantised("w2", w2_raw)
         h3 = hidden(3)
         q2 = quantised_hidden(2, h2)
         h4 = hidden(4)
+        frozen_layer(w3_quantised)
         rr0 = second_product(0, q0, w2_quantised, "rr")
         rr1 = second_product(1, q1, w2_quantised, "rr")
         q3 = quantised_hidden(3, h3)

@@ -42,8 +42,8 @@ def tile_picked_yvera_silu_p_kernel(
 
         ad_list = lists.tile([P, S // LIST], U16, name="ad_list")
         token_list = lists.tile([P, S // LIST], U16, name="token_list")
-        ld_tables = [keep.tile([P, R], F32, name=f"ld_table{t}") for t in range(2)]
-        ld_tables.extend(turns.tile([P, R], F32, name=f"ld_table{t}", offset=2 * (t - 2) * KIB) for t in range(2, PACK))
+        ld_tables = [keep.tile([P, R], F32, name=f"ld_table{t}") for t in range(3)]
+        ld_tables.extend(turns.tile([P, R], F32, name=f"ld_table{t}", offset=2 * KIB) for t in range(3, PACK))
         lb_table = keep.tile([P, R], F32, name="lb_table")
         word_table = keep.tile([P, T], I32, name="word_table")
         scale_table = turns.tile([P, T], U8, name="scale_table", offset=2 * KIB - 32)
@@ -68,6 +68,7 @@ def tile_picked_yvera_silu_p_kernel(
         nc.sync.dma_start(lb_table[:], lb)
         nc.sync.dma_start(token_list[:], offs)
         nc.sync.dma_start(scale_table[0:P:8, :].bitcast(I32), x_scales[0].bitcast(I32))
+        nc.sync.dma_start(ld_tables[2][:], ld_rows[:, 2, :])
         nc.sync.dma_start(ld_tables[1][:], ld_rows[:, 1, :])
         nc.sync.dma_start(w1_raw[:], w1.rearrange("(p j) c -> p j c", j=PACK))
         nc.sync.dma_start(word_table[:], x_words[0].rearrange("p c t -> p (c t)").bitcast(I32))
@@ -92,26 +93,26 @@ def tile_picked_yvera_silu_p_kernel(
         for first in pieces:
             look_up(on_scalar, 0, first)
         for first in pieces:
-            engine = on_vector if first < BANK else on_scalar
-            engine(lb_picked[:, first : first + PIECE], lb_table, first)
+            on_vector(lb_picked[:, first : first + PIECE], lb_table, first)
+        for first in pieces:
+            look_up(on_scalar, 2, first)
         spread_bytes = keep.tile([P, S], U8, name="spread_bytes")
         nc.vector.tensor_copy(spread_bytes[:], scale_table[:].indirect(token_list[:]))
         for r in range(4):
             nc.sync.dma_start(x_bytes[r:P:32, :].bitcast(I32), spread_bytes[8 * r : P : 32, :].bitcast(I32))
         for first in pieces:
             look_up(on_vector, 1, first)
-        for t in range(2, PACK):
-            nc.sync.dma_start(ld_tables[t][:], ld_rows[:, t, :])
+        nc.sync.dma_start(ld_tables[3][:], ld_rows[:, 3, :])
         w3_raw = turns.tile([P, PACK, N], F32, name="w3_raw", offset=4 * KIB)
         nc.sync.dma_start(w3_raw[:], w3.rearrange("(p j) c -> p j c", j=PACK))
+        w2_raw = turns.tile([P, PACK, N], F32, name="w2_raw", offset=0)
+        nc.sync.dma_start(w2_raw[:], w2.rearrange("(p j) c -> p j c", j=PACK))
 
         w1_bf = keep.tile([P, PACK * H], BF16, name="w1_bf", align_bytes=64)
         nc.scalar.copy(
             w1_bf[:].rearrange("p (t m j) -> p m t j", t=PACK, j=PACK),
             w1_raw[:].rearrange("p j (m t) -> p m t j", t=PACK),
         )
-        w2_raw = turns.tile([P, PACK, N], F32, name="w2_raw", offset=6 * KIB)
-        nc.sync.dma_start(w2_raw[:], w2.rearrange("(p j) c -> p j c", j=PACK))
         w1_codes = keep.tile([P, H], U32, name="w1_codes", align_bytes=64)
         w1_scales = keep.tile([P, H], U8, name="w1_scales", align_bytes=64)
         nc.vector.quantize_mx(w1_codes[:].bitcast(FP8X4), w1_scales[:], w1_bf[:])
@@ -155,8 +156,7 @@ def tile_picked_yvera_silu_p_kernel(
         last = len(GROUPS) - 1
 
         def late_planes(first):
-            for t in range(2, PACK):
-                look_up(on_scalar, t, first)
+            look_up(on_scalar, PACK - 1, first)
 
         def hidden(g):
             first, width = starts[g], GROUPS[g]
@@ -184,7 +184,7 @@ def tile_picked_yvera_silu_p_kernel(
             nc.vector.quantize_mx(codes[:].bitcast(FP8X4), scales[:], rounded[:].rearrange("p c j -> p (c j)"))
             return codes[:], scales[:]
 
-        ee_turned = turns.tile([P, S // CHUNK, N], F32, name="ee_turned", offset=0)
+        ee_turned = keep.tile([P, S // CHUNK, N], F32, name="ee_turned")
 
         def frozen_layer(w3_quantised):
             for c0 in range(0, S // CHUNK, per_bank):
@@ -228,10 +228,13 @@ def tile_picked_yvera_silu_p_kernel(
             turned_back(total, ee_turned[:, chunks_of(g), :], True)
             return total
 
-        def summed(g, rr, total):
+        def term_of(g, rr):
             term = keep.tile([P, GROUPS[g] // CHUNK, N], F32, name=f"term{g}")
             nc.vector.tensor_tensor(term[:], rr[:], lb_turned[:, chunks_of(g), :], MULT)
-            turned_back(total, term[:], False)
+            return term[:]
+
+        def summed(g, rr, total):
+            turned_back(total, term_of(g, rr), False)
 
         def finish(g, total):
             first, width = starts[g], GROUPS[g]
@@ -240,35 +243,38 @@ def tile_picked_yvera_silu_p_kernel(
             queue = nc.scalar if g == last else nc.sync
             queue.dma_start(out[:, first : first + width], result[:])
 
-        for first in pieces:
-            late_planes(first)
+        late_planes(0)
+        late_planes(PIECE)
         h0 = hidden(0)
-        h1 = hidden(1)
-        q0 = quantised_hidden(0, h0)
-        h2 = hidden(2)
-        q1 = quantised_hidden(1, h1)
         w3_quantised = quantised("w3", w3_raw)
         w2_quantised = quantised("w2", w2_raw)
-        h3 = hidden(3)
-        q2 = quantised_hidden(2, h2)
-        h4 = hidden(4)
+        late_planes(2 * PIECE)
+        late_planes(3 * PIECE)
+        h1 = hidden(1)
         frozen_layer(w3_quantised)
+        q0 = quantised_hidden(0, h0)
+        h2 = hidden(2)
         rr0 = second_product(0, q0, w2_quantised, "rr")
-        rr1 = second_product(1, q1, w2_quantised, "rr")
-        q3 = quantised_hidden(3, h3)
+        q1 = quantised_hidden(1, h1)
         totals = [opened(g, "total") for g in range(3)]
         summed(0, rr0, totals[0])
-        q4 = quantised_hidden(4, h4)
-        rr2 = second_product(2, q2, w2_quantised, "y")
-        rr3 = second_product(3, q3, w2_quantised, "rr")
-        totals.extend(opened(g, "y") for g in range(3, 5))
-        summed(1, rr1, totals[1])
-        rr4 = second_product(4, q4, w2_quantised, "rr")
+        rr1 = second_product(1, q1, w2_quantised, "rr")
+        h3 = hidden(3)
         finish(0, totals[0])
-        summed(2, rr2, totals[2])
+        q2 = quantised_hidden(2, h2)
+        summed(1, rr1, totals[1])
+        rr2 = second_product(2, q2, w2_quantised, "rr")
+        h4 = hidden(4)
         finish(1, totals[1])
-        summed(3, rr3, totals[3])
+        totals.append(opened(3, "total"))
+        q3 = quantised_hidden(3, h3)
+        rr3 = second_product(3, q3, w2_quantised, "rr")
+        totals.append(opened(4, "total"))
+        q4 = quantised_hidden(4, h4)
+        rr4 = second_product(4, q4, w2_quantised, "y")
+        summed(2, rr2, totals[2])
         finish(2, totals[2])
-        summed(4, rr4, totals[4])
+        summed(3, rr3, totals[3])
         finish(3, totals[3])
+        summed(4, rr4, totals[4])
         finish(4, totals[4])

@@ -42,8 +42,9 @@ def tile_picked_yvera_silu_p_kernel(
 
         ad_list = lists.tile([P, S // LIST], U16, name="ad_list")
         token_list = lists.tile([P, S // LIST], U16, name="token_list")
-        ld_tables = [keep.tile([P, R], F32, name=f"ld_table{t}") for t in range(3)]
-        ld_tables.extend(turns.tile([P, R], F32, name=f"ld_table{t}", offset=2 * KIB) for t in range(3, PACK))
+        late = PACK - 1
+        ld_tables = [keep.tile([P, R], F32, name=f"ld_table{t}") for t in range(late)]
+        ld_tables.append(turns.tile([P, R], F32, name=f"ld_table{late}", offset=2 * KIB))
         lb_table = keep.tile([P, R], F32, name="lb_table")
         word_table = keep.tile([P, T], I32, name="word_table")
         scale_table = turns.tile([P, T], U8, name="scale_table", offset=2 * KIB - 32)
@@ -63,14 +64,14 @@ def tile_picked_yvera_silu_p_kernel(
         make_identity(nc, identity[:])
 
         ld_rows = ld.rearrange("(p t) r -> p t r", t=PACK)
-        nc.sync.dma_start(ad_list[:], ad)
         nc.sync.dma_start(ld_tables[0][:], ld_rows[:, 0, :])
+        nc.sync.dma_start(ad_list[:], ad)
         nc.sync.dma_start(lb_table[:], lb)
         nc.sync.dma_start(token_list[:], offs)
         nc.sync.dma_start(scale_table[0:P:8, :].bitcast(I32), x_scales[0].bitcast(I32))
         nc.sync.dma_start(ld_tables[2][:], ld_rows[:, 2, :])
-        nc.sync.dma_start(ld_tables[1][:], ld_rows[:, 1, :])
         nc.sync.dma_start(w1_raw[:], w1.rearrange("(p j) c -> p j c", j=PACK))
+        nc.sync.dma_start(ld_tables[1][:], ld_rows[:, 1, :])
         nc.sync.dma_start(word_table[:], x_words[0].rearrange("p c t -> p (c t)").bitcast(I32))
 
         def on_vector(target, table, first):
@@ -100,9 +101,9 @@ def tile_picked_yvera_silu_p_kernel(
         nc.vector.tensor_copy(spread_bytes[:], scale_table[:].indirect(token_list[:]))
         for r in range(4):
             nc.sync.dma_start(x_bytes[r:P:32, :].bitcast(I32), spread_bytes[8 * r : P : 32, :].bitcast(I32))
-        for first in pieces:
+        for first in pieces[:-1]:
             look_up(on_vector, 1, first)
-        nc.sync.dma_start(ld_tables[3][:], ld_rows[:, 3, :])
+        nc.sync.dma_start(ld_tables[late][:], ld_rows[:, late, :])
         w3_raw = turns.tile([P, PACK, N], F32, name="w3_raw", offset=4 * KIB)
         nc.sync.dma_start(w3_raw[:], w3.rearrange("(p j) c -> p j c", j=PACK))
         w2_raw = turns.tile([P, PACK, N], F32, name="w2_raw", offset=0)
@@ -113,6 +114,7 @@ def tile_picked_yvera_silu_p_kernel(
             w1_bf[:].rearrange("p (t m j) -> p m t j", t=PACK, j=PACK),
             w1_raw[:].rearrange("p j (m t) -> p m t j", t=PACK),
         )
+        look_up(on_scalar, 1, pieces[-1])
         w1_codes = keep.tile([P, H], U32, name="w1_codes", align_bytes=64)
         w1_scales = keep.tile([P, H], U8, name="w1_scales", align_bytes=64)
         nc.vector.quantize_mx(w1_codes[:].bitcast(FP8X4), w1_scales[:], w1_bf[:])
@@ -155,9 +157,6 @@ def tile_picked_yvera_silu_p_kernel(
         starts = [sum(GROUPS[:g]) for g in range(len(GROUPS))]
         last = len(GROUPS) - 1
 
-        def late_planes(first):
-            look_up(on_scalar, PACK - 1, first)
-
         def hidden(g):
             first, width = starts[g], GROUPS[g]
             h_bf = keep.tile([P, width * PACK], BF16, name=f"h_bf{g}", align_bytes=64)
@@ -173,7 +172,7 @@ def tile_picked_yvera_silu_p_kernel(
                 )
             return h_bf
 
-        def quantised(name, raw):
+        def quantised_weight(name, raw):
             rounded = keep.tile([P, N, PACK], BF16, name=f"{name}_bf", align_bytes=64)
             nc.scalar.copy(
                 rounded[:].rearrange("p (c i) j -> p c j i", i=RUN),
@@ -200,13 +199,16 @@ def tile_picked_yvera_silu_p_kernel(
             nc.vector.quantize_mx(h_codes[:].bitcast(FP8X4), h_scales[:], h_bf[:])
             return h_codes, h_scales
 
-        def second_product(g, h_quantised, w2_quantised, tag):
+        def rr_slots(groups, tag):
+            counts = [GROUPS[g] // CHUNK for g in groups]
+            bank = psum.tile([P, sum(counts), N], F32, name="rr", tag=tag, bufs=BANKS[tag])
+            return [bank[:, sum(counts[:place]) : sum(counts[: place + 1]), :] for place in range(len(counts))]
+
+        def second_product(rr, h_quantised, w2_quantised):
             h_codes, h_scales = h_quantised
-            rr = psum.tile([P, GROUPS[g] // CHUNK, N], F32, name="rr", tag=tag, bufs=BANKS[tag])
-            for c in range(GROUPS[g] // CHUNK):
+            for c in range(rr.shape[1]):
                 cols = slice(c * CHUNK, (c + 1) * CHUNK)
                 product(rr[:, c, :], (h_codes[:, cols], h_scales[:, cols]), w2_quantised)
-            return rr
 
         def turned_back(total, addend, opens):
             count = addend.shape[1]
@@ -228,53 +230,42 @@ def tile_picked_yvera_silu_p_kernel(
             turned_back(total, ee_turned[:, chunks_of(g), :], True)
             return total
 
-        def term_of(g, rr):
-            term = keep.tile([P, GROUPS[g] // CHUNK, N], F32, name=f"term{g}")
-            nc.vector.tensor_tensor(term[:], rr[:], lb_turned[:, chunks_of(g), :], MULT)
-            return term[:]
-
-        def summed(g, rr, total):
-            turned_back(total, term_of(g, rr), False)
-
-        def finish(g, total):
+        def finish(g, rr, total):
             first, width = starts[g], GROUPS[g]
+            term = keep.tile([P, width // CHUNK, N], F32, name=f"term{g}")
+            nc.vector.tensor_tensor(term[:], rr, lb_turned[:, chunks_of(g), :], MULT)
+            turned_back(total, term[:], False)
             result = keep.tile([P, width], F32, name=f"result{g}")
             nc.scalar.activation(result[:], total[:], SILU)
             queue = nc.scalar if g == last else nc.sync
             queue.dma_start(out[:, first : first + width], result[:])
 
-        late_planes(0)
-        late_planes(PIECE)
+        for first in pieces[:2]:
+            look_up(on_scalar, late, first)
         h0 = hidden(0)
-        w3_quantised = quantised("w3", w3_raw)
-        w2_quantised = quantised("w2", w2_raw)
-        late_planes(2 * PIECE)
-        late_planes(3 * PIECE)
+        w3_quantised = quantised_weight("w3", w3_raw)
+        w2_quantised = quantised_weight("w2", w2_raw)
+        for first in pieces[2:]:
+            look_up(on_scalar, late, first)
         h1 = hidden(1)
         frozen_layer(w3_quantised)
-        q0 = quantised_hidden(0, h0)
+        h0_quantised = quantised_hidden(0, h0)
         h2 = hidden(2)
-        rr0 = second_product(0, q0, w2_quantised, "rr")
-        q1 = quantised_hidden(1, h1)
-        totals = [opened(g, "total") for g in range(3)]
-        summed(0, rr0, totals[0])
-        rr1 = second_product(1, q1, w2_quantised, "rr")
+        h1_quantised = quantised_hidden(1, h1)
         h3 = hidden(3)
-        finish(0, totals[0])
-        q2 = quantised_hidden(2, h2)
-        summed(1, rr1, totals[1])
-        rr2 = second_product(2, q2, w2_quantised, "rr")
+        totals = [opened(g, "total") for g in range(BANKS["total"])]
+        rr0, rr1 = rr_slots((0, 1), "rr")
+        second_product(rr0, h0_quantised, w2_quantised)
+        second_product(rr1, h1_quantised, w2_quantised)
+        h2_quantised = quantised_hidden(2, h2)
         h4 = hidden(4)
-        finish(1, totals[1])
-        totals.append(opened(3, "total"))
-        q3 = quantised_hidden(3, h3)
-        rr3 = second_product(3, q3, w2_quantised, "rr")
-        totals.append(opened(4, "total"))
-        q4 = quantised_hidden(4, h4)
-        rr4 = second_product(4, q4, w2_quantised, "y")
-        summed(2, rr2, totals[2])
-        finish(2, totals[2])
-        summed(3, rr3, totals[3])
-        finish(3, totals[3])
-        summed(4, rr4, totals[4])
-        finish(4, totals[4])
+        totals.extend([opened(3, "y"), opened(4, "rr")])
+        rr2, rr3 = rr_slots((2, 3), "y")
+        second_product(rr2, h2_quantised, w2_quantised)
+        h3_quantised = quantised_hidden(3, h3)
+        h4_quantised = quantised_hidden(4, h4)
+        second_product(rr3, h3_quantised, w2_quantised)
+        (rr4,) = rr_slots((4,), "y")
+        second_product(rr4, h4_quantised, w2_quantised)
+        for g, rr in enumerate((rr0, rr1, rr2, rr3, rr4)):
+            finish(g, rr, totals[g])

@@ -26,8 +26,8 @@ CHUNK = 128
 PIECE = 256
 RUN = 4
 PAIR = 2
-GROUPS = (256, 256, 256, 128, 128)
-BANKS = {"y": 3, "rr": 2, "total": 3}
+ASIDE = (2, 3)
+WORDS = (256, 256, 512)
 
 
 def tile_picked_yvera_silu_p_kernel(
@@ -42,12 +42,13 @@ def tile_picked_yvera_silu_p_kernel(
 
         ad_list = lists.tile([P, S // LIST], U16, name="ad_list")
         token_list = lists.tile([P, S // LIST], U16, name="token_list")
-        late = PACK - 1
-        ld_tables = [keep.tile([P, R], F32, name=f"ld_table{t}") for t in range(late)]
-        ld_tables.append(turns.tile([P, R], F32, name=f"ld_table{late}", offset=2 * KIB))
-        lb_table = keep.tile([P, R], F32, name="lb_table")
+        ld_tables = [keep.tile([P, R], F32, name=f"ld_table{t}") for t in range(PACK - 1)]
+        ld_tables.append(turns.tile([P, R], F32, name="ld_table3", offset=2 * KIB))
         word_table = keep.tile([P, T], I32, name="word_table")
         scale_table = turns.tile([P, T], U8, name="scale_table", offset=2 * KIB - 32)
+        lb_table = keep.tile([P, R], F32, name="lb_table")
+        w3_raw = turns.tile([P, PACK, N], F32, name="w3_raw", offset=4 * KIB)
+        w2_raw = turns.tile([P, PACK, N], F32, name="w2_raw", offset=0)
         w1_raw = turns.tile([P, PACK, H], F32, name="w1_raw", offset=6 * KIB)
         x_bytes = keep.tile([P, S], U8, name="x_bytes", align_bytes=64)
 
@@ -80,7 +81,10 @@ def tile_picked_yvera_silu_p_kernel(
         def on_scalar(target, table, first):
             nc.scalar.activation(target, table[:].indirect(entries(ad_list, first, PIECE)), COPY)
 
-        ld_picked = [keep.tile([P, PACK, PIECE], F32, name=f"ld_picked{u}") for u in range(S // PIECE)]
+        ld_picked = [
+            turns.tile([P, PACK, PIECE], F32, name=f"ld_picked{u}", offset=offset * KIB)
+            for u, offset in enumerate((20, 24, 14, 28))
+        ]
 
         def picked_planes(first, width):
             piece, col = divmod(first, PIECE)
@@ -90,9 +94,9 @@ def tile_picked_yvera_silu_p_kernel(
             engine(picked_planes(first, PIECE)[:, t, :], ld_tables[t], first)
 
         pieces = range(0, S, PIECE)
-        lb_picked = keep.tile([P, S], F32, name="lb_picked")
         for first in pieces:
             look_up(on_scalar, 0, first)
+        lb_picked = keep.tile([P, S], F32, name="lb_picked")
         for first in pieces:
             on_vector(lb_picked[:, first : first + PIECE], lb_table, first)
         for first in pieces:
@@ -103,10 +107,8 @@ def tile_picked_yvera_silu_p_kernel(
             nc.sync.dma_start(x_bytes[r:P:32, :].bitcast(I32), spread_bytes[8 * r : P : 32, :].bitcast(I32))
         for first in pieces[:-1]:
             look_up(on_vector, 1, first)
-        nc.sync.dma_start(ld_tables[late][:], ld_rows[:, late, :])
-        w3_raw = turns.tile([P, PACK, N], F32, name="w3_raw", offset=4 * KIB)
+        nc.sync.dma_start(ld_tables[3][:], ld_rows[:, 3, :])
         nc.sync.dma_start(w3_raw[:], w3.rearrange("(p j) c -> p j c", j=PACK))
-        w2_raw = turns.tile([P, PACK, N], F32, name="w2_raw", offset=0)
         nc.sync.dma_start(w2_raw[:], w2.rearrange("(p j) c -> p j c", j=PACK))
 
         w1_bf = keep.tile([P, PACK * H], BF16, name="w1_bf", align_bytes=64)
@@ -121,24 +123,26 @@ def tile_picked_yvera_silu_p_kernel(
 
         per_bank = BANK // CHUNK
         lb_turned = turns.tile([P, S // CHUNK, N], F32, name="lb_turned", offset=8 * KIB)
-        for c0 in range(0, S // CHUNK, per_bank):
-            bank = psum.tile([P, per_bank, N], F32, name="lb_bank", tag="total", bufs=BANKS["total"])
+        for half, tag in enumerate("cd"):
+            bank = psum.tile([P, per_bank, N], F32, name="lb_bank", tag=tag, bufs=1)
             for c in range(per_bank):
-                first = (c0 + c) * CHUNK
+                first = (half * per_bank + c) * CHUNK
                 nc.tensor.transpose(bank[:, c, :], lb_picked[:, first : first + CHUNK], identity[:])
-            nc.scalar.copy(lb_turned[:, c0 : c0 + per_bank, :], bank[:])
+            nc.scalar.copy(lb_turned[:, half * per_bank : (half + 1) * per_bank, :], bank[:])
 
-        x_codes = []
-        for first in range(0, S, BANK):
-            codes = keep.tile([P, BANK], U32, name=f"x_codes{first}", align_bytes=64)
+        x_codes = {}
+        first = 0
+        for width in WORDS:
+            codes = keep.tile([P, width], U32, name=f"x_codes{first}", align_bytes=64)
             nc.vector.tensor_copy(
-                codes[:], word_table[:].bitcast(U32).indirect(entries(token_list, first, BANK))
+                codes[:], word_table[:].bitcast(U32).indirect(entries(token_list, first, width))
             )
-            x_codes.append(codes)
+            for col in range(0, width, CHUNK):
+                x_codes[first + col] = codes[:, col : col + CHUNK]
+            first = first + width
 
         def picked_x(first, width):
-            tile, col = divmod(first, BANK)
-            return x_codes[tile][:, col : col + width], x_bytes[:, first : first + width]
+            return x_codes[first], x_bytes[:, first : first + width]
 
         def product(target, stationary, moving):
             nc.tensor.matmul_mx(
@@ -154,55 +158,68 @@ def tile_picked_yvera_silu_p_kernel(
         def w1_plane(t):
             return w1_codes[:, t * P : (t + 1) * P], w1_scales[:, t * P : (t + 1) * P]
 
-        starts = [sum(GROUPS[:g]) for g in range(len(GROUPS))]
-        last = len(GROUPS) - 1
+        h_bf = [keep.tile([P, PIECE * PACK], BF16, name=f"h_bf{u}", align_bytes=64) for u in range(S // PIECE - 1)]
+        h_bf.append(turns.tile([P, PIECE * PACK], BF16, name="h_bf3", align_bytes=64, offset=18 * KIB))
 
-        def hidden(g):
-            first, width = starts[g], GROUPS[g]
-            h_bf = keep.tile([P, width * PACK], BF16, name=f"h_bf{g}", align_bytes=64)
-            for col in range(0, width, CHUNK):
-                y = psum.tile([P, PACK, CHUNK], F32, name="y", tag="y", bufs=BANKS["y"])
-                for t in range(PACK):
-                    product(y[:, t, :], w1_plane(t), picked_x(first + col, CHUNK))
-                nc.vector.tensor_tensor(
-                    h_bf[:, col * PACK : (col + CHUNK) * PACK].rearrange("p (c i t) -> p c t i", i=PAIR, t=PACK),
-                    y[:].rearrange("p t (c i) -> p c t i", i=PAIR),
-                    picked_planes(first + col, CHUNK).rearrange("p t (c i) -> p c t i", i=PAIR),
-                    MULT,
-                )
-            return h_bf
+        def h_of(c):
+            piece, col = divmod(c * CHUNK, PIECE)
+            return h_bf[piece][:, col * PACK : (col + CHUNK) * PACK]
 
-        def quantised_weight(name, raw):
-            rounded = keep.tile([P, N, PACK], BF16, name=f"{name}_bf", align_bytes=64)
+        def planes_of_y(c, tag, bufs):
+            y = psum.tile([P, PACK, CHUNK], F32, name="y", tag=tag, bufs=bufs)
+            for t in range(PACK):
+                product(y[:, t, :], w1_plane(t), picked_x(c * CHUNK, CHUNK))
+            return y
+
+        def hidden(c):
+            y = planes_of_y(c, "y", 3)
+            nc.vector.tensor_tensor(
+                h_of(c).rearrange("p (c i t) -> p c t i", i=PAIR, t=PACK),
+                y[:].rearrange("p t (c i) -> p c t i", i=PAIR),
+                picked_planes(c * CHUNK, CHUNK).rearrange("p t (c i) -> p c t i", i=PAIR),
+                MULT,
+            )
+
+        def hidden_aside(c, y, offset):
+            woven = turns.tile([P, CHUNK, PACK], F32, name=f"woven{c}", offset=offset * KIB)
+            nc.scalar.copy(woven[:], y[:].rearrange("p t n -> p n t"))
+            nc.gpsimd.tensor_tensor(
+                h_of(c).rearrange("p (n t) -> p n t", t=PACK),
+                woven[:],
+                picked_planes(c * CHUNK, CHUNK).rearrange("p t n -> p n t"),
+                MULT,
+            )
+
+        def rounded_weight(rounded, raw):
             nc.scalar.copy(
-                rounded[:].rearrange("p (c i) j -> p c j i", i=RUN),
+                rounded.rearrange("p (c i j) -> p c j i", i=RUN, j=PACK),
                 raw[:].rearrange("p j (c i) -> p c j i", i=RUN),
             )
-            codes = keep.tile([P, N], U32, name=f"{name}_codes", align_bytes=64)
-            scales = keep.tile([P, N], U8, name=f"{name}_scales", align_bytes=64)
-            nc.vector.quantize_mx(codes[:].bitcast(FP8X4), scales[:], rounded[:].rearrange("p c j -> p (c j)"))
+            return rounded
+
+        def quantised(name, rounded, offset=None):
+            width = rounded.shape[1] // PACK
+            codes = keep.tile([P, width], U32, name=f"{name}_codes", align_bytes=64)
+            if offset is None:
+                scales = keep.tile([P, width], U8, name=f"{name}_scales", align_bytes=64)
+            else:
+                scales = turns.tile([P, width], U8, name=f"{name}_scales", align_bytes=64, offset=offset)
+            nc.vector.quantize_mx(codes[:].bitcast(FP8X4), scales[:], rounded)
             return codes[:], scales[:]
 
-        ee_turned = keep.tile([P, S // CHUNK, N], F32, name="ee_turned")
+        ee_turned = [
+            turns.tile([P, per_bank, N], F32, name=f"ee_turned{half}", offset=offset * KIB)
+            for half, offset in enumerate((22, 32))
+        ]
 
-        def frozen_layer(w3_quantised):
-            for c0 in range(0, S // CHUNK, per_bank):
-                bank = psum.tile([P, per_bank, N], F32, name="ee_bank", tag="total", bufs=BANKS["total"])
-                for c in range(per_bank):
-                    product(bank[:, c, :], picked_x((c0 + c) * CHUNK, CHUNK), w3_quantised)
-                nc.scalar.copy(ee_turned[:, c0 : c0 + per_bank, :], bank[:])
+        def frozen_layer(half, tag, w3_quantised):
+            bank = psum.tile([P, per_bank, N], F32, name="ee_bank", tag=tag, bufs=1)
+            for c in range(per_bank):
+                product(bank[:, c, :], picked_x((half * per_bank + c) * CHUNK, CHUNK), w3_quantised)
+            return bank
 
-        def quantised_hidden(g, h_bf):
-            width = GROUPS[g]
-            h_codes = keep.tile([P, width], U32, name=f"h_codes{g}", align_bytes=64)
-            h_scales = keep.tile([P, width], U8, name=f"h_scales{g}", align_bytes=64)
-            nc.vector.quantize_mx(h_codes[:].bitcast(FP8X4), h_scales[:], h_bf[:])
-            return h_codes, h_scales
-
-        def rr_slots(groups, tag):
-            counts = [GROUPS[g] // CHUNK for g in groups]
-            bank = psum.tile([P, sum(counts), N], F32, name="rr", tag=tag, bufs=BANKS[tag])
-            return [bank[:, sum(counts[:place]) : sum(counts[: place + 1]), :] for place in range(len(counts))]
+        def copy_ee(half, bank):
+            nc.scalar.copy(ee_turned[half][:], bank[:])
 
         def second_product(rr, h_quantised, w2_quantised):
             h_codes, h_scales = h_quantised
@@ -222,50 +239,57 @@ def tile_picked_yvera_silu_p_kernel(
                     stop=not opens and c == count - 1,
                 )
 
-        def chunks_of(g):
-            return slice(starts[g] // CHUNK, (starts[g] + GROUPS[g]) // CHUNK)
-
-        def opened(g, tag):
-            total = psum.tile([P, GROUPS[g]], F32, name="total", tag=tag, bufs=BANKS[tag])
-            turned_back(total, ee_turned[:, chunks_of(g), :], True)
+        def opened(chunks, tag, bufs):
+            total = psum.tile([P, (chunks.stop - chunks.start) * CHUNK], F32, name="total", tag=tag, bufs=bufs)
+            half, c = divmod(chunks.start, per_bank)
+            turned_back(total, ee_turned[half][:, c : c + chunks.stop - chunks.start, :], True)
             return total
 
-        def finish(g, rr, total):
-            first, width = starts[g], GROUPS[g]
-            term = keep.tile([P, width // CHUNK, N], F32, name=f"term{g}")
-            nc.vector.tensor_tensor(term[:], rr, lb_turned[:, chunks_of(g), :], MULT)
+        def finish(chunks, rr, total, term, queue):
+            first, width = chunks.start * CHUNK, (chunks.stop - chunks.start) * CHUNK
+            nc.vector.tensor_tensor(term[:], rr, lb_turned[:, chunks, :], MULT)
             turned_back(total, term[:], False)
-            result = keep.tile([P, width], F32, name=f"result{g}")
+            result = keep.tile([P, width], F32, name=f"result{first}")
             nc.scalar.activation(result[:], total[:], SILU)
-            queue = nc.scalar if g == last else nc.sync
             queue.dma_start(out[:, first : first + width], result[:])
 
-        for first in pieces[:2]:
-            look_up(on_scalar, late, first)
-        h0 = hidden(0)
-        w3_quantised = quantised_weight("w3", w3_raw)
-        w2_quantised = quantised_weight("w2", w2_raw)
-        for first in pieces[2:]:
-            look_up(on_scalar, late, first)
-        h1 = hidden(1)
-        frozen_layer(w3_quantised)
-        h0_quantised = quantised_hidden(0, h0)
-        h2 = hidden(2)
-        h1_quantised = quantised_hidden(1, h1)
-        h3 = hidden(3)
-        totals = [opened(g, "total") for g in range(BANKS["total"])]
-        rr0, rr1 = rr_slots((0, 1), "rr")
-        second_product(rr0, h0_quantised, w2_quantised)
-        second_product(rr1, h1_quantised, w2_quantised)
-        h2_quantised = quantised_hidden(2, h2)
-        h4 = hidden(4)
-        totals.extend([opened(3, "y"), opened(4, "rr")])
-        rr2, rr3 = rr_slots((2, 3), "y")
-        second_product(rr2, h2_quantised, w2_quantised)
-        h3_quantised = quantised_hidden(3, h3)
-        h4_quantised = quantised_hidden(4, h4)
-        second_product(rr3, h3_quantised, w2_quantised)
-        (rr4,) = rr_slots((4,), "y")
-        second_product(rr4, h4_quantised, w2_quantised)
-        for g, rr in enumerate((rr0, rr1, rr2, rr3, rr4)):
-            finish(g, rr, totals[g])
+        look_up(on_scalar, 3, pieces[0])
+        look_up(on_scalar, 3, pieces[1])
+        w3_bf = rounded_weight(h_of(ASIDE[0]), w3_raw)
+        hidden(0)
+        w3_quantised = quantised("w3", w3_bf)
+        hidden(1)
+        look_up(on_scalar, 3, pieces[2])
+        y_aside = planes_of_y(ASIDE[0], "a", 1)
+        hidden_aside(ASIDE[0], y_aside, 32)
+        hidden(4)
+        y_aside = planes_of_y(ASIDE[1], "b", 1)
+        look_up(on_scalar, 3, pieces[3])
+        hidden_aside(ASIDE[1], y_aside, 34)
+        hidden(6)
+        hidden(5)
+        hidden(7)
+        w2_bf = turns.tile([P, N * PACK], BF16, name="w2_bf", align_bytes=64, offset=21 * KIB)
+        rounded_weight(w2_bf[:], w2_raw)
+        copy_ee(0, frozen_layer(0, "c", w3_quantised))
+        copy_ee(1, frozen_layer(1, "d", w3_quantised))
+        h0 = quantised("h0", h_bf[0][:], 17 * KIB)
+        w2_quantised = quantised("w2", w2_bf[:], 17 * KIB + 256)
+        h2 = quantised("h2", h_bf[2][:], 17 * KIB + 512)
+        h3 = quantised("h3", h_bf[3][:])
+        h1 = quantised("h1", h_bf[1][:], 17 * KIB + 768)
+        groups = [slice(0, 2), slice(4, 6), slice(6, 8), slice(2, 3), slice(3, 4)]
+        totals = {0: opened(groups[0], "b", 1), 3: opened(groups[3], "y", 3), 4: opened(groups[4], "c", 1)}
+        rr02 = psum.tile([P, per_bank, N], F32, name="rr02", tag="a", bufs=1)
+        second_product(rr02[:, 0:2, :], h0, w2_quantised)
+        totals[1] = opened(groups[1], "d", 1)
+        totals[2] = opened(groups[2], "e", 1)
+        second_product(rr02[:, 2:4, :], h2, w2_quantised)
+        rr3 = psum.tile([P, 2, N], F32, name="rr3", tag="y", bufs=3)
+        second_product(rr3[:], h3, w2_quantised)
+        rr1 = psum.tile([P, 2, N], F32, name="rr1", tag="y", bufs=3)
+        second_product(rr1[:], h1, w2_quantised)
+        terms = [turns.tile([P, 2, N], F32, name=f"term{g}", offset=(18 + g) * KIB) for g in range(2)]
+        terms.extend(keep.tile([P, count, N], F32, name=f"term{2 + g}") for g, count in enumerate((2, 1, 1)))
+        for g, rr in enumerate((rr02[:, 0:2, :], rr02[:, 2:4, :], rr3[:], rr1[:, 0:1, :], rr1[:, 1:2, :])):
+            finish(groups[g], rr, totals[g], terms[g], nc.scalar if g == 4 else nc.sync)

@@ -181,12 +181,12 @@ def tile_picked_yvera_silu_p_kernel(
             )
 
         def hidden_aside(c, y, offset):
-            woven = turns.tile([P, CHUNK, PACK], F32, name=f"woven{c}", offset=offset * KIB)
-            nc.scalar.copy(woven[:], y[:].rearrange("p t n -> p n t"))
+            woven = turns.tile([P, CHUNK // RUN, PACK, RUN], F32, name=f"woven{c}", offset=offset * KIB)
+            nc.scalar.copy(woven[:], y[:].rearrange("p t (c i) -> p c t i", i=RUN))
             nc.gpsimd.tensor_tensor(
-                h_of(c).rearrange("p (n t) -> p n t", t=PACK),
+                h_of(c).rearrange("p (c i t) -> p c t i", i=RUN, t=PACK),
                 woven[:],
-                picked_planes(c * CHUNK, CHUNK).rearrange("p t n -> p n t"),
+                picked_planes(c * CHUNK, CHUNK).rearrange("p t (c i) -> p c t i", i=RUN),
                 MULT,
             )
 

@@ -26,7 +26,7 @@ CHUNK = 128
 PIECE = 256
 RUN = 4
 PAIR = 2
-ASIDE = (2, 3)
+ASIDE = (2,)
 WORDS = (256, 256, 512)
 
 
@@ -83,7 +83,7 @@ def tile_picked_yvera_silu_p_kernel(
 
         ld_picked = [
             turns.tile([P, PACK, PIECE], F32, name=f"ld_picked{u}", offset=offset * KIB)
-            for u, offset in enumerate((20, 24, 14, 28))
+            for u, offset in enumerate((20, 24, 28, 14))
         ]
 
         def picked_planes(first, width):
@@ -260,15 +260,13 @@ def tile_picked_yvera_silu_p_kernel(
         w3_quantised = quantised("w3", w3_bf)
         hidden(1)
         look_up(on_scalar, 3, pieces[2])
-        y_aside = planes_of_y(ASIDE[0], "a", 1)
-        hidden_aside(ASIDE[0], y_aside, 32)
+        hidden_aside(ASIDE[0], planes_of_y(ASIDE[0], "a", 1), 32)
         hidden(4)
-        y_aside = planes_of_y(ASIDE[1], "b", 1)
         look_up(on_scalar, 3, pieces[3])
-        hidden_aside(ASIDE[1], y_aside, 34)
-        hidden(6)
         hidden(5)
+        hidden(6)
         hidden(7)
+        hidden(3)
         w2_bf = turns.tile([P, N * PACK], BF16, name="w2_bf", align_bytes=64, offset=21 * KIB)
         rounded_weight(w2_bf[:], w2_raw)
         copy_ee(0, frozen_layer(0, "c", w3_quantised))

@@ -70,8 +70,8 @@ def tile_picked_yvera_silu_p_kernel(
         nc.sync.dma_start(lb_table[:], lb)
         nc.sync.dma_start(token_list[:], offs)
         nc.sync.dma_start(scale_table[0:P:8, :].bitcast(I32), x_scales[0].bitcast(I32))
-        nc.sync.dma_start(ld_tables[2][:], ld_rows[:, 2, :])
         nc.sync.dma_start(w1_raw[:], w1.rearrange("(p j) c -> p j c", j=PACK))
+        nc.sync.dma_start(ld_tables[2][:], ld_rows[:, 2, :])
         nc.sync.dma_start(ld_tables[1][:], ld_rows[:, 1, :])
         nc.sync.dma_start(word_table[:], x_words[0].rearrange("p c t -> p (c t)").bitcast(I32))
 
@@ -99,13 +99,11 @@ def tile_picked_yvera_silu_p_kernel(
         lb_picked = keep.tile([P, S], F32, name="lb_picked")
         for first in pieces:
             on_vector(lb_picked[:, first : first + PIECE], lb_table, first)
-        for first in pieces:
-            look_up(on_scalar, 2, first)
         spread_bytes = keep.tile([P, S], U8, name="spread_bytes")
         nc.vector.tensor_copy(spread_bytes[:], scale_table[:].indirect(token_list[:]))
         for r in range(4):
             nc.sync.dma_start(x_bytes[r:P:32, :].bitcast(I32), spread_bytes[8 * r : P : 32, :].bitcast(I32))
-        for first in pieces[:-1]:
+        for first in pieces:
             look_up(on_vector, 1, first)
         nc.sync.dma_start(ld_tables[3][:], ld_rows[:, 3, :])
         nc.sync.dma_start(w3_raw[:], w3.rearrange("(p j) c -> p j c", j=PACK))
@@ -116,19 +114,25 @@ def tile_picked_yvera_silu_p_kernel(
             w1_bf[:].rearrange("p (t m j) -> p m t j", t=PACK, j=PACK),
             w1_raw[:].rearrange("p j (m t) -> p m t j", t=PACK),
         )
-        look_up(on_scalar, 1, pieces[-1])
+        for first in pieces:
+            look_up(on_scalar, 2, first)
         w1_codes = keep.tile([P, H], U32, name="w1_codes", align_bytes=64)
         w1_scales = keep.tile([P, H], U8, name="w1_scales", align_bytes=64)
         nc.vector.quantize_mx(w1_codes[:].bitcast(FP8X4), w1_scales[:], w1_bf[:])
 
         per_bank = BANK // CHUNK
-        lb_turned = turns.tile([P, S // CHUNK, N], F32, name="lb_turned", offset=8 * KIB)
+        lb_turned = [
+            turns.tile([P, per_bank, N], F32, name=f"lb_turned{half}", offset=offset * KIB)
+            for half, offset in enumerate((8, 28))
+        ]
+        lb_banks = []
         for half, tag in enumerate("cd"):
             bank = psum.tile([P, per_bank, N], F32, name="lb_bank", tag=tag, bufs=1)
             for c in range(per_bank):
                 first = (half * per_bank + c) * CHUNK
                 nc.tensor.transpose(bank[:, c, :], lb_picked[:, first : first + CHUNK], identity[:])
-            nc.scalar.copy(lb_turned[:, half * per_bank : (half + 1) * per_bank, :], bank[:])
+            lb_banks.append(bank)
+        nc.scalar.copy(lb_turned[0][:], lb_banks[0][:])
 
         x_codes = {}
         first = 0
@@ -247,7 +251,8 @@ def tile_picked_yvera_silu_p_kernel(
 
         def finish(chunks, rr, total, term, queue):
             first, width = chunks.start * CHUNK, (chunks.stop - chunks.start) * CHUNK
-            nc.vector.tensor_tensor(term[:], rr, lb_turned[:, chunks, :], MULT)
+            half, c = divmod(chunks.start, per_bank)
+            nc.vector.tensor_tensor(term[:], rr, lb_turned[half][:, c : c + width // CHUNK, :], MULT)
             turned_back(total, term[:], False)
             result = keep.tile([P, width], F32, name=f"result{first}")
             nc.scalar.activation(result[:], total[:], SILU)
@@ -270,7 +275,8 @@ def tile_picked_yvera_silu_p_kernel(
         w2_bf = turns.tile([P, N * PACK], BF16, name="w2_bf", align_bytes=64, offset=21 * KIB)
         rounded_weight(w2_bf[:], w2_raw)
         copy_ee(0, frozen_layer(0, "c", w3_quantised))
-        copy_ee(1, frozen_layer(1, "d", w3_quantised))
+        copy_ee(1, frozen_layer(1, "e", w3_quantised))
+        nc.scalar.copy(lb_turned[1][:], lb_banks[1][:])
         h0 = quantised("h0", h_bf[0][:], 17 * KIB)
         w2_quantised = quantised("w2", w2_bf[:], 17 * KIB + 256)
         h2 = quantised("h2", h_bf[2][:], 17 * KIB + 512)
@@ -280,9 +286,9 @@ def tile_picked_yvera_silu_p_kernel(
         totals = {0: opened(groups[0], "b", 1), 3: opened(groups[3], "y", 3), 4: opened(groups[4], "c", 1)}
         rr02 = psum.tile([P, per_bank, N], F32, name="rr02", tag="a", bufs=1)
         second_product(rr02[:, 0:2, :], h0, w2_quantised)
-        totals[1] = opened(groups[1], "d", 1)
-        totals[2] = opened(groups[2], "e", 1)
+        totals[1] = opened(groups[1], "e", 1)
         second_product(rr02[:, 2:4, :], h2, w2_quantised)
+        totals[2] = opened(groups[2], "d", 1)
         rr3 = psum.tile([P, 2, N], F32, name="rr3", tag="y", bufs=3)
         second_product(rr3[:], h3, w2_quantised)
         rr1 = psum.tile([P, 2, N], F32, name="rr1", tag="y", bufs=3)

@@ -25,8 +25,8 @@ BANK = 512
 CHUNK = 128
 PIECE = 256
 RUN = 4
+STRETCH = 2
 PAIR = 2
-ASIDE = (2,)
 WORDS = (256, 256, 512)
 
 
@@ -69,9 +69,9 @@ def tile_picked_yvera_silu_p_kernel(
         nc.sync.dma_start(ad_list[:], ad)
         nc.sync.dma_start(lb_table[:], lb)
         nc.sync.dma_start(token_list[:], offs)
+        nc.sync.dma_start(ld_tables[2][:], ld_rows[:, 2, :])
         nc.sync.dma_start(scale_table[0:P:8, :].bitcast(I32), x_scales[0].bitcast(I32))
         nc.sync.dma_start(w1_raw[:], w1.rearrange("(p j) c -> p j c", j=PACK))
-        nc.sync.dma_start(ld_tables[2][:], ld_rows[:, 2, :])
         nc.sync.dma_start(ld_tables[1][:], ld_rows[:, 1, :])
         nc.sync.dma_start(word_table[:], x_words[0].rearrange("p c t -> p (c t)").bitcast(I32))
 
@@ -83,7 +83,7 @@ def tile_picked_yvera_silu_p_kernel(
 
         ld_picked = [
             turns.tile([P, PACK, PIECE], F32, name=f"ld_picked{u}", offset=offset * KIB)
-            for u, offset in enumerate((20, 24, 28, 14))
+            for u, offset in enumerate((20, 24, 14, 28))
         ]
 
         def picked_planes(first, width):
@@ -123,7 +123,7 @@ def tile_picked_yvera_silu_p_kernel(
         per_bank = BANK // CHUNK
         lb_turned = [
             turns.tile([P, per_bank, N], F32, name=f"lb_turned{half}", offset=offset * KIB)
-            for half, offset in enumerate((8, 28))
+            for half, offset in enumerate((8, 10))
         ]
         lb_banks = []
         for half, tag in enumerate("cd"):
@@ -132,7 +132,8 @@ def tile_picked_yvera_silu_p_kernel(
                 first = (half * per_bank + c) * CHUNK
                 nc.tensor.transpose(bank[:, c, :], lb_picked[:, first : first + CHUNK], identity[:])
             lb_banks.append(bank)
-        nc.scalar.copy(lb_turned[0][:], lb_banks[0][:])
+        for half in range(2):
+            nc.scalar.copy(lb_turned[half][:], lb_banks[half][:])
 
         x_codes = {}
         first = 0
@@ -162,8 +163,8 @@ def tile_picked_yvera_silu_p_kernel(
         def w1_plane(t):
             return w1_codes[:, t * P : (t + 1) * P], w1_scales[:, t * P : (t + 1) * P]
 
-        h_bf = [keep.tile([P, PIECE * PACK], BF16, name=f"h_bf{u}", align_bytes=64) for u in range(S // PIECE - 1)]
-        h_bf.append(turns.tile([P, PIECE * PACK], BF16, name="h_bf3", align_bytes=64, offset=18 * KIB))
+        h_bf = {u: keep.tile([P, PIECE * PACK], BF16, name=f"h_bf{u}", align_bytes=64) for u in (0, 1, 2)}
+        h_bf[3] = turns.tile([P, PIECE * PACK], BF16, name="h_bf3", align_bytes=64, offset=18 * KIB)
 
         def h_of(c):
             piece, col = divmod(c * CHUNK, PIECE)
@@ -175,22 +176,24 @@ def tile_picked_yvera_silu_p_kernel(
                 product(y[:, t, :], w1_plane(t), picked_x(c * CHUNK, CHUNK))
             return y
 
-        def hidden(c):
-            y = planes_of_y(c, "y", 3)
+        def multiply(target, y, first, width):
             nc.vector.tensor_tensor(
-                h_of(c).rearrange("p (c i t) -> p c t i", i=PAIR, t=PACK),
-                y[:].rearrange("p t (c i) -> p c t i", i=PAIR),
-                picked_planes(c * CHUNK, CHUNK).rearrange("p t (c i) -> p c t i", i=PAIR),
+                target.rearrange("p (c i t) -> p c t i", i=PAIR, t=PACK),
+                y.rearrange("p t (c i) -> p c t i", i=PAIR),
+                picked_planes(first, width).rearrange("p t (c i) -> p c t i", i=PAIR),
                 MULT,
             )
 
-        def hidden_aside(c, y, offset):
-            woven = turns.tile([P, CHUNK // RUN, PACK, RUN], F32, name=f"woven{c}", offset=offset * KIB)
-            nc.scalar.copy(woven[:], y[:].rearrange("p t (c i) -> p c t i", i=RUN))
+        def hidden(c):
+            multiply(h_of(c), planes_of_y(c, "y", 3)[:], c * CHUNK, CHUNK)
+
+        def hidden_aside(target, y, first, width, offset):
+            woven = turns.tile([P, width // STRETCH, PACK, STRETCH], F32, name=f"woven{first}", offset=offset * KIB)
+            nc.scalar.copy(woven[:], y.rearrange("p t (c i) -> p c t i", i=STRETCH))
             nc.gpsimd.tensor_tensor(
-                h_of(c).rearrange("p (c i t) -> p c t i", i=RUN, t=PACK),
+                target.rearrange("p (c i t) -> p c t i", i=STRETCH, t=PACK),
                 woven[:],
-                picked_planes(c * CHUNK, CHUNK).rearrange("p t (c i) -> p c t i", i=RUN),
+                picked_planes(first, width).rearrange("p t (c i) -> p c t i", i=STRETCH),
                 MULT,
             )
 
@@ -260,40 +263,35 @@ def tile_picked_yvera_silu_p_kernel(
 
         look_up(on_scalar, 3, pieces[0])
         look_up(on_scalar, 3, pieces[1])
-        w3_bf = rounded_weight(h_of(ASIDE[0]), w3_raw)
+        w3_bf = rounded_weight(h_of(2), w3_raw)
         hidden(0)
         w3_quantised = quantised("w3", w3_bf)
         hidden(1)
         look_up(on_scalar, 3, pieces[2])
-        hidden_aside(ASIDE[0], planes_of_y(ASIDE[0], "a", 1), 32)
+        hidden_aside(h_of(2), planes_of_y(2, "a", 1)[:], 2 * CHUNK, CHUNK, 32)
         hidden(4)
         look_up(on_scalar, 3, pieces[3])
-        hidden(5)
+        hidden_aside(h_of(3), planes_of_y(3, "b", 1)[:], 3 * CHUNK, CHUNK, 34)
         hidden(6)
+        hidden(5)
         hidden(7)
-        hidden(3)
         w2_bf = turns.tile([P, N * PACK], BF16, name="w2_bf", align_bytes=64, offset=21 * KIB)
         rounded_weight(w2_bf[:], w2_raw)
         copy_ee(0, frozen_layer(0, "c", w3_quantised))
         copy_ee(1, frozen_layer(1, "e", w3_quantised))
-        nc.scalar.copy(lb_turned[1][:], lb_banks[1][:])
-        h0 = quantised("h0", h_bf[0][:], 17 * KIB)
         w2_quantised = quantised("w2", w2_bf[:], 17 * KIB + 256)
+        h0 = quantised("h0", h_bf[0][:], 17 * KIB)
         h2 = quantised("h2", h_bf[2][:], 17 * KIB + 512)
         h3 = quantised("h3", h_bf[3][:])
         h1 = quantised("h1", h_bf[1][:], 17 * KIB + 768)
-        groups = [slice(0, 2), slice(4, 6), slice(6, 8), slice(2, 3), slice(3, 4)]
-        totals = {0: opened(groups[0], "b", 1), 3: opened(groups[3], "y", 3), 4: opened(groups[4], "c", 1)}
-        rr02 = psum.tile([P, per_bank, N], F32, name="rr02", tag="a", bufs=1)
-        second_product(rr02[:, 0:2, :], h0, w2_quantised)
-        totals[1] = opened(groups[1], "e", 1)
-        second_product(rr02[:, 2:4, :], h2, w2_quantised)
-        totals[2] = opened(groups[2], "d", 1)
-        rr3 = psum.tile([P, 2, N], F32, name="rr3", tag="y", bufs=3)
-        second_product(rr3[:], h3, w2_quantised)
-        rr1 = psum.tile([P, 2, N], F32, name="rr1", tag="y", bufs=3)
-        second_product(rr1[:], h1, w2_quantised)
+        groups = [slice(0, 2), slice(4, 6), slice(6, 8), slice(2, 4)]
+        totals = [opened(chunks, tag, bufs) for chunks, tag, bufs in zip(groups, "cedy", (1, 1, 1, 3))]
+        rrs = []
+        for h, tag, bufs in zip((h0, h2, h3, h1), "ayyb", (1, 3, 3, 1)):
+            rr = psum.tile([P, 2, N], F32, name="rr", tag=tag, bufs=bufs)
+            second_product(rr[:], h, w2_quantised)
+            rrs.append(rr)
         terms = [turns.tile([P, 2, N], F32, name=f"term{g}", offset=(18 + g) * KIB) for g in range(2)]
-        terms.extend(keep.tile([P, count, N], F32, name=f"term{2 + g}") for g, count in enumerate((2, 1, 1)))
-        for g, rr in enumerate((rr02[:, 0:2, :], rr02[:, 2:4, :], rr3[:], rr1[:, 0:1, :], rr1[:, 1:2, :])):
-            finish(groups[g], rr, totals[g], terms[g], nc.scalar if g == 4 else nc.sync)
+        terms.extend(keep.tile([P, 2, N], F32, name=f"term{2 + g}") for g in range(2))
+        for g, rr in enumerate(rrs):
+            finish(groups[g], rr[:], totals[g], terms[g], nc.scalar if g == 3 else nc.sync)

@@ -26,6 +26,7 @@ CHUNK = 128
 PIECE = 256
 RUN = 4
 STRETCH = 2
+SHARE = 96
 PAIR = 2
 WORDS = (256, 256, 512)
 
@@ -163,10 +164,13 @@ def tile_picked_yvera_silu_p_kernel(
         def w1_plane(t):
             return w1_codes[:, t * P : (t + 1) * P], w1_scales[:, t * P : (t + 1) * P]
 
-        h_bf = {u: keep.tile([P, PIECE * PACK], BF16, name=f"h_bf{u}", align_bytes=64) for u in (0, 1, 2)}
+        h_bf = {u: keep.tile([P, PIECE * PACK], BF16, name=f"h_bf{u}", align_bytes=64) for u in (0, 2)}
+        h_single = {c: keep.tile([P, CHUNK * PACK], BF16, name=f"h_single{c}", align_bytes=64) for c in (2, 3)}
         h_bf[3] = turns.tile([P, PIECE * PACK], BF16, name="h_bf3", align_bytes=64, offset=18 * KIB)
 
         def h_of(c):
+            if c in h_single:
+                return h_single[c][:]
             piece, col = divmod(c * CHUNK, PIECE)
             return h_bf[piece][:, col * PACK : (col + CHUNK) * PACK]
 
@@ -187,9 +191,13 @@ def tile_picked_yvera_silu_p_kernel(
         def hidden(c):
             multiply(h_of(c), planes_of_y(c, "y", 3)[:], c * CHUNK, CHUNK)
 
-        def hidden_aside(target, y, first, width, offset):
-            woven = turns.tile([P, width // STRETCH, PACK, STRETCH], F32, name=f"woven{first}", offset=offset * KIB)
+        def copied_out(y, offset):
+            width = y.shape[2]
+            woven = turns.tile([P, width // STRETCH, PACK, STRETCH], F32, name=f"woven{offset}", offset=offset * KIB)
             nc.scalar.copy(woven[:], y.rearrange("p t (c i) -> p c t i", i=STRETCH))
+            return woven
+
+        def hidden_aside(target, woven, first, width):
             nc.gpsimd.tensor_tensor(
                 target.rearrange("p (c i t) -> p c t i", i=STRETCH, t=PACK),
                 woven[:],
@@ -268,11 +276,14 @@ def tile_picked_yvera_silu_p_kernel(
         w3_quantised = quantised("w3", w3_bf)
         hidden(1)
         look_up(on_scalar, 3, pieces[2])
-        hidden_aside(h_of(2), planes_of_y(2, "a", 1)[:], 2 * CHUNK, CHUNK, 32)
+        hidden_aside(h_of(2), copied_out(planes_of_y(2, "a", 1)[:], 32), 2 * CHUNK, CHUNK)
         hidden(4)
         look_up(on_scalar, 3, pieces[3])
-        hidden_aside(h_of(3), planes_of_y(3, "b", 1)[:], 3 * CHUNK, CHUNK, 34)
+        y_shared = planes_of_y(3, "b", 1)
+        woven_shared = copied_out(y_shared[:, :, 0:SHARE], 34)
         hidden(6)
+        multiply(h_of(3)[:, SHARE * PACK :], y_shared[:, :, SHARE:CHUNK], 3 * CHUNK + SHARE, CHUNK - SHARE)
+        hidden_aside(h_of(3)[:, 0 : SHARE * PACK], woven_shared, 3 * CHUNK, SHARE)
         hidden(5)
         hidden(7)
         w2_bf = turns.tile([P, N * PACK], BF16, name="w2_bf", align_bytes=64, offset=21 * KIB)
@@ -283,14 +294,19 @@ def tile_picked_yvera_silu_p_kernel(
         h0 = quantised("h0", h_bf[0][:], 17 * KIB)
         h2 = quantised("h2", h_bf[2][:], 17 * KIB + 512)
         h3 = quantised("h3", h_bf[3][:])
-        h1 = quantised("h1", h_bf[1][:], 17 * KIB + 768)
+        h10 = quantised("h10", h_of(2), 17 * KIB + 768)
+        h11 = quantised("h11", h_of(3), 17 * KIB + 896)
         groups = [slice(0, 2), slice(4, 6), slice(6, 8), slice(2, 4)]
         totals = [opened(chunks, tag, bufs) for chunks, tag, bufs in zip(groups, "cedy", (1, 1, 1, 3))]
         rrs = []
-        for h, tag, bufs in zip((h0, h2, h3, h1), "ayyb", (1, 3, 3, 1)):
+        for h, tag, bufs in zip((h0, h2, h3), "ayy", (1, 3, 3)):
             rr = psum.tile([P, 2, N], F32, name="rr", tag=tag, bufs=bufs)
             second_product(rr[:], h, w2_quantised)
             rrs.append(rr)
+        rr = psum.tile([P, 2, N], F32, name="rr", tag="b", bufs=1)
+        second_product(rr[:, 0:1, :], h10, w2_quantised)
+        second_product(rr[:, 1:2, :], h11, w2_quantised)
+        rrs.append(rr)
         terms = [turns.tile([P, 2, N], F32, name=f"term{g}", offset=(18 + g) * KIB) for g in range(2)]
         terms.extend(keep.tile([P, 2, N], F32, name=f"term{2 + g}") for g in range(2))
         for g, rr in enumerate(rrs):

@@ -14,6 +14,7 @@ U16 = mybir.dt.uint16
 U8 = mybir.dt.uint8
 FP8X4 = mybir.dt.float8_e4m3fn_x4
 MULT = mybir.AluOpType.mult
+ADD = mybir.AluOpType.add
 SILU = mybir.ActivationFunctionType.Silu
 COPY = mybir.ActivationFunctionType.Copy
 
@@ -21,14 +22,12 @@ P = 128
 KIB = 1024
 PACK = 4
 LIST = 16
-BANK = 512
 CHUNK = 128
 PIECE = 256
 RUN = 4
-STRETCH = 2
-SHARE = 96
 PAIR = 2
-WORDS = (256, 256, 512)
+HALF = H // 2
+SIDE = P // 2
 
 
 def tile_picked_yvera_silu_p_kernel(
@@ -43,18 +42,22 @@ def tile_picked_yvera_silu_p_kernel(
 
         ad_list = lists.tile([P, S // LIST], U16, name="ad_list")
         token_list = lists.tile([P, S // LIST], U16, name="token_list")
-        ld_tables = [keep.tile([P, R], F32, name=f"ld_table{t}") for t in range(PACK - 1)]
-        ld_tables.append(turns.tile([P, R], F32, name="ld_table3", offset=2 * KIB))
+        ld_first = keep.tile([P, R], F32, name="ld_first")
+        ld_middle = keep.tile([P, 2 * R], F32, name="ld_middle")
+        ld_last = keep.tile([P, R], F32, name="ld_last")
         word_table = keep.tile([P, T], I32, name="word_table")
-        scale_table = turns.tile([P, T], U8, name="scale_table", offset=2 * KIB - 32)
+        scale_table = keep.tile([P, T], U8, name="scale_table")
         lb_table = keep.tile([P, R], F32, name="lb_table")
-        w3_raw = turns.tile([P, PACK, N], F32, name="w3_raw", offset=4 * KIB)
-        w2_raw = turns.tile([P, PACK, N], F32, name="w2_raw", offset=0)
-        w1_raw = turns.tile([P, PACK, H], F32, name="w1_raw", offset=6 * KIB)
+        w1_raw = [keep.tile([P, PACK, HALF], F32, name=f"w1_raw{half}") for half in range(2)]
+        w3_raw = keep.tile([P, PACK, N], F32, name="w3_raw")
+        w2_raw = keep.tile([P, PACK, N], F32, name="w2_raw")
         x_bytes = keep.tile([P, S], U8, name="x_bytes", align_bytes=64)
 
         def entries(index_list, first, count):
             return index_list[:, first // LIST : (first + count) // LIST]
+
+        def bank(number, shape, name):
+            return psum.tile(shape, F32, name=name, tag=f"bank{number}", bufs=1)
 
         nc.vector.memset(scale_table[:].bitcast(I32), 0)
         nc.vector.memset(x_bytes[:].bitcast(I32), 0)
@@ -65,90 +68,90 @@ def tile_picked_yvera_silu_p_kernel(
         identity = keep.tile([P, P], F32, name="identity")
         make_identity(nc, identity[:])
 
-        ld_rows = ld.rearrange("(p t) r -> p t r", t=PACK)
-        nc.sync.dma_start(ld_tables[0][:], ld_rows[:, 0, :])
+        ld_rows = ld.rearrange("(p t) r -> p (t r)", t=PACK)
+        w1_rows = w1.rearrange("(p j) c -> p j c", j=PACK)
+        nc.sync.dma_start(ld_first[:], ld_rows[:, 0:R])
         nc.sync.dma_start(ad_list[:], ad)
-        nc.sync.dma_start(lb_table[:], lb)
+        nc.sync.dma_start(ld_middle[:], ld_rows[:, R : 3 * R])
         nc.sync.dma_start(token_list[:], offs)
-        nc.sync.dma_start(ld_tables[2][:], ld_rows[:, 2, :])
         nc.sync.dma_start(scale_table[0:P:8, :].bitcast(I32), x_scales[0].bitcast(I32))
-        nc.sync.dma_start(w1_raw[:], w1.rearrange("(p j) c -> p j c", j=PACK))
-        nc.sync.dma_start(ld_tables[1][:], ld_rows[:, 1, :])
+        nc.sync.dma_start(ld_last[:], ld_rows[:, 3 * R : 4 * R])
         nc.sync.dma_start(word_table[:], x_words[0].rearrange("p c t -> p (c t)").bitcast(I32))
-
-        def on_vector(target, table, first):
-            nc.vector.tensor_copy(target, table[:].indirect(entries(ad_list, first, PIECE)))
-
-        def on_scalar(target, table, first):
-            nc.scalar.activation(target, table[:].indirect(entries(ad_list, first, PIECE)), COPY)
+        for half in range(2):
+            nc.sync.dma_start(w1_raw[half][:], w1_rows[:, :, half * HALF : (half + 1) * HALF])
 
         ld_picked = [
-            turns.tile([P, PACK, PIECE], F32, name=f"ld_picked{u}", offset=offset * KIB)
-            for u, offset in enumerate((20, 24, 14, 28))
+            turns.tile([P, PACK, PIECE], F32, name=f"ld_picked{u}", offset=(4 + 4 * u) * KIB) for u in range(S // PIECE)
         ]
 
         def picked_planes(first, width):
             piece, col = divmod(first, PIECE)
             return ld_picked[piece][:, :, col : col + width]
 
-        def look_up(engine, t, first):
-            engine(picked_planes(first, PIECE)[:, t, :], ld_tables[t], first)
+        def on_scalar(target, window, first):
+            nc.scalar.activation(target, window.indirect(entries(ad_list, first, PIECE)), COPY)
 
         pieces = range(0, S, PIECE)
-        for first in pieces:
-            look_up(on_scalar, 0, first)
-        lb_picked = keep.tile([P, S], F32, name="lb_picked")
-        for first in pieces:
-            on_vector(lb_picked[:, first : first + PIECE], lb_table, first)
         spread_bytes = keep.tile([P, S], U8, name="spread_bytes")
         nc.vector.tensor_copy(spread_bytes[:], scale_table[:].indirect(token_list[:]))
+        for first in pieces:
+            nc.vector.tensor_copy(
+                picked_planes(first, PIECE)[:, 2, :], ld_middle[:, R : 2 * R].indirect(entries(ad_list, first, PIECE))
+            )
+        for t, table in ((0, ld_first), (1, ld_middle), (3, ld_last)):
+            for first in pieces:
+                on_scalar(picked_planes(first, PIECE)[:, t, :], table[:], first)
         for r in range(4):
             nc.sync.dma_start(x_bytes[r:P:32, :].bitcast(I32), spread_bytes[8 * r : P : 32, :].bitcast(I32))
-        for first in pieces:
-            look_up(on_vector, 1, first)
-        nc.sync.dma_start(ld_tables[3][:], ld_rows[:, 3, :])
         nc.sync.dma_start(w3_raw[:], w3.rearrange("(p j) c -> p j c", j=PACK))
         nc.sync.dma_start(w2_raw[:], w2.rearrange("(p j) c -> p j c", j=PACK))
-
-        w1_bf = keep.tile([P, PACK * H], BF16, name="w1_bf", align_bytes=64)
-        nc.scalar.copy(
-            w1_bf[:].rearrange("p (t m j) -> p m t j", t=PACK, j=PACK),
-            w1_raw[:].rearrange("p j (m t) -> p m t j", t=PACK),
-        )
-        for first in pieces:
-            look_up(on_scalar, 2, first)
-        w1_codes = keep.tile([P, H], U32, name="w1_codes", align_bytes=64)
-        w1_scales = keep.tile([P, H], U8, name="w1_scales", align_bytes=64)
-        nc.vector.quantize_mx(w1_codes[:].bitcast(FP8X4), w1_scales[:], w1_bf[:])
-
-        per_bank = BANK // CHUNK
-        lb_turned = [
-            turns.tile([P, per_bank, N], F32, name=f"lb_turned{half}", offset=offset * KIB)
-            for half, offset in enumerate((8, 10))
-        ]
-        lb_banks = []
-        for half, tag in enumerate("cd"):
-            bank = psum.tile([P, per_bank, N], F32, name="lb_bank", tag=tag, bufs=1)
-            for c in range(per_bank):
-                first = (half * per_bank + c) * CHUNK
-                nc.tensor.transpose(bank[:, c, :], lb_picked[:, first : first + CHUNK], identity[:])
-            lb_banks.append(bank)
-        for half in range(2):
-            nc.scalar.copy(lb_turned[half][:], lb_banks[half][:])
+        nc.sync.dma_start(lb_table[:], lb)
 
         x_codes = {}
-        first = 0
-        for width in WORDS:
-            codes = keep.tile([P, width], U32, name=f"x_codes{first}", align_bytes=64)
-            nc.vector.tensor_copy(
-                codes[:], word_table[:].bitcast(U32).indirect(entries(token_list, first, width))
-            )
-            for col in range(0, width, CHUNK):
-                x_codes[first + col] = codes[:, col : col + CHUNK]
-            first = first + width
+
+        def gather_words(codes, first):
+            width = codes.shape[1]
+            nc.vector.tensor_copy(codes[:], word_table[:].bitcast(U32).indirect(entries(token_list, first, width)))
+            for col in range(0, width, PIECE):
+                x_codes[first + col] = codes[:, col : col + PIECE]
 
         def picked_x(first, width):
-            return x_codes[first], x_bytes[:, first : first + width]
+            piece, col = divmod(first, PIECE)
+            return x_codes[piece * PIECE][:, col : col + width], x_bytes[:, first : first + width]
+
+        w1_codes = keep.tile([P, H], U32, name="w1_codes", align_bytes=64)
+        w1_scales = keep.tile([P, H], U8, name="w1_scales", align_bytes=64)
+
+        def round_w1(copy, rounded, half, pair):
+            copy(
+                rounded[:].rearrange("p (t m j) -> p m t j", t=PAIR, j=PACK),
+                w1_raw[half][:].rearrange("p j (m t) -> p m t j", t=PACK)[:, :, PAIR * pair : PAIR * (pair + 1), :],
+            )
+
+        def quantise_w1(rounded, half, pair):
+            for u in range(PAIR):
+                cols = slice((PAIR * pair + u) * P + half * SIDE, (PAIR * pair + u) * P + (half + 1) * SIDE)
+                nc.vector.quantize_mx(
+                    w1_codes[:, cols].bitcast(FP8X4), w1_scales[:, cols], rounded[:, u * HALF : (u + 1) * HALF]
+                )
+
+        w1_bf = {
+            (half, pair): keep.tile([P, PAIR * HALF], BF16, name=f"w1_bf{half}{pair}", align_bytes=64)
+            for half, pair in ((0, 0), (0, 1), (1, 0))
+        }
+        w1_bf[1, 1] = turns.tile([P, PAIR * HALF], BF16, name="w1_bf11", align_bytes=64, offset=0)
+
+        gather_words(keep.tile([P, 2 * PIECE], U32, name="x_codes0", align_bytes=64), 0)
+        gather_words(keep.tile([P, PIECE], U32, name="x_codes2", align_bytes=64), 2 * PIECE)
+        round_w1(nc.scalar.copy, w1_bf[0, 0], 0, 0)
+        round_w1(nc.scalar.copy, w1_bf[0, 1], 0, 1)
+        quantise_w1(w1_bf[0, 0], 0, 0)
+        round_w1(nc.vector.tensor_copy, w1_bf[1, 0], 1, 0)
+        round_w1(nc.scalar.copy, w1_bf[1, 1], 1, 1)
+        quantise_w1(w1_bf[0, 1], 0, 1)
+        quantise_w1(w1_bf[1, 0], 1, 0)
+        quantise_w1(w1_bf[1, 1], 1, 1)
+        gather_words(turns.tile([P, PIECE], U32, name="x_codes3", align_bytes=64, offset=0), 3 * PIECE)
 
         def product(target, stationary, moving):
             nc.tensor.matmul_mx(
@@ -164,53 +167,46 @@ def tile_picked_yvera_silu_p_kernel(
         def w1_plane(t):
             return w1_codes[:, t * P : (t + 1) * P], w1_scales[:, t * P : (t + 1) * P]
 
-        h_bf = {u: keep.tile([P, PIECE * PACK], BF16, name=f"h_bf{u}", align_bytes=64) for u in (0, 2)}
-        h_single = {c: keep.tile([P, CHUNK * PACK], BF16, name=f"h_single{c}", align_bytes=64) for c in (2, 3)}
-        h_bf[3] = turns.tile([P, PIECE * PACK], BF16, name="h_bf3", align_bytes=64, offset=18 * KIB)
+        order = (0, 2, 1, 4, 3, 6, 5, 7)
+        y = {c: bank(number, [P, PACK, CHUNK], f"y{c}") for number, c in enumerate(order)}
+
+        def plane_of_y(c, t):
+            product(y[c][:, t, :], w1_plane(t), picked_x(c * CHUNK, CHUNK))
+
+        for t in range(PAIR):
+            for c in order[:2]:
+                plane_of_y(c, t)
+        for c in order[:2]:
+            for t in range(PAIR, PACK):
+                plane_of_y(c, t)
+        for c in order[2:]:
+            for t in range(PACK):
+                plane_of_y(c, t)
+
+        h_bf = [keep.tile([P, PIECE * PACK], BF16, name=f"h_bf{u}", align_bytes=64) for u in range(S // PIECE)]
+
+        def in_pairs(planes):
+            return planes.rearrange("p t (c i) -> p c t i", i=PAIR)
 
         def h_of(c):
-            if c in h_single:
-                return h_single[c][:]
             piece, col = divmod(c * CHUNK, PIECE)
-            return h_bf[piece][:, col * PACK : (col + CHUNK) * PACK]
-
-        def planes_of_y(c, tag, bufs):
-            y = psum.tile([P, PACK, CHUNK], F32, name="y", tag=tag, bufs=bufs)
-            for t in range(PACK):
-                product(y[:, t, :], w1_plane(t), picked_x(c * CHUNK, CHUNK))
-            return y
-
-        def multiply(target, y, first, width):
-            nc.vector.tensor_tensor(
-                target.rearrange("p (c i t) -> p c t i", i=PAIR, t=PACK),
-                y.rearrange("p t (c i) -> p c t i", i=PAIR),
-                picked_planes(first, width).rearrange("p t (c i) -> p c t i", i=PAIR),
-                MULT,
-            )
+            target = h_bf[piece][:, col * PACK : (col + CHUNK) * PACK]
+            return target.rearrange("p (c i t) -> p c t i", i=PAIR, t=PACK)
 
         def hidden(c):
-            multiply(h_of(c), planes_of_y(c, "y", 3)[:], c * CHUNK, CHUNK)
+            nc.vector.tensor_tensor(h_of(c), in_pairs(y[c][:]), in_pairs(picked_planes(c * CHUNK, CHUNK)), MULT)
 
-        def copied_out(y, offset):
-            width = y.shape[2]
-            woven = turns.tile([P, width // STRETCH, PACK, STRETCH], F32, name=f"woven{offset}", offset=offset * KIB)
-            nc.scalar.copy(woven[:], y.rearrange("p t (c i) -> p c t i", i=STRETCH))
-            return woven
+        def hidden_aside(c, woven):
+            nc.scalar.copy(woven[:], in_pairs(y[c][:]))
+            nc.gpsimd.tensor_tensor(h_of(c), woven[:], in_pairs(picked_planes(c * CHUNK, CHUNK)), MULT)
 
-        def hidden_aside(target, woven, first, width):
-            nc.gpsimd.tensor_tensor(
-                target.rearrange("p (c i t) -> p c t i", i=STRETCH, t=PACK),
-                woven[:],
-                picked_planes(first, width).rearrange("p t (c i) -> p c t i", i=STRETCH),
-                MULT,
-            )
-
-        def rounded_weight(rounded, raw):
+        def rounded_weight(name, raw):
+            rounded = keep.tile([P, N * PACK], BF16, name=f"{name}_bf", align_bytes=64)
             nc.scalar.copy(
-                rounded.rearrange("p (c i j) -> p c j i", i=RUN, j=PACK),
+                rounded[:].rearrange("p (c i j) -> p c j i", i=RUN, j=PACK),
                 raw[:].rearrange("p j (c i) -> p c j i", i=RUN),
             )
-            return rounded
+            return rounded[:]
 
         def quantised(name, rounded, offset=None):
             width = rounded.shape[1] // PACK
@@ -222,92 +218,93 @@ def tile_picked_yvera_silu_p_kernel(
             nc.vector.quantize_mx(codes[:].bitcast(FP8X4), scales[:], rounded)
             return codes[:], scales[:]
 
-        ee_turned = [
-            turns.tile([P, per_bank, N], F32, name=f"ee_turned{half}", offset=offset * KIB)
-            for half, offset in enumerate((22, 32))
+        woven = [
+            turns.tile([P, CHUNK // PAIR, PACK, PAIR], F32, name=f"woven{u}", offset=offset * KIB)
+            for u, offset in enumerate((2, 20))
+        ]
+        lb_picked = [
+            turns.tile([P, PIECE], F32, name=f"lb_picked{u}", offset=offset * KIB)
+            for u, offset in enumerate((22, 23, 23, 2))
         ]
 
-        def frozen_layer(half, tag, w3_quantised):
-            bank = psum.tile([P, per_bank, N], F32, name="ee_bank", tag=tag, bufs=1)
-            for c in range(per_bank):
-                product(bank[:, c, :], picked_x((half * per_bank + c) * CHUNK, CHUNK), w3_quantised)
-            return bank
+        w3_quantised = quantised("w3", rounded_weight("w3", w3_raw))
+        w2_bf = rounded_weight("w2", w2_raw)
+        hidden(0)
+        w2_quantised = quantised("w2", w2_bf)
+        hidden_aside(2, woven[0])
+        on_scalar(lb_picked[0][:], lb_table[:], 0)
+        hidden(1)
+        hidden(4)
+        hidden_aside(3, woven[1])
+        on_scalar(lb_picked[2][:], lb_table[:], 2 * PIECE)
+        hidden(6)
+        hidden(5)
+        hidden(7)
 
-        def copy_ee(half, bank):
-            nc.scalar.copy(ee_turned[half][:], bank[:])
-
-        def second_product(rr, h_quantised, w2_quantised):
-            h_codes, h_scales = h_quantised
-            for c in range(rr.shape[1]):
-                cols = slice(c * CHUNK, (c + 1) * CHUNK)
-                product(rr[:, c, :], (h_codes[:, cols], h_scales[:, cols]), w2_quantised)
+        turned, plain = (0, 2), (3, 1)
+        ee_bank = bank(0, [P, 2, 2, N], "ee_bank")
+        for g, piece in enumerate(turned):
+            for c in range(2):
+                product(ee_bank[:, g, c, :], picked_x(piece * PIECE + c * CHUNK, CHUNK), w3_quantised)
+        lb_bank = bank(2, [P, 2, 2, N], "lb_bank")
+        for g, piece in enumerate(turned):
+            for c in range(2):
+                nc.tensor.transpose(lb_bank[:, g, c, :], lb_picked[piece][:, c * CHUNK : (c + 1) * CHUNK], identity[:])
+        ee_turned = keep.tile([P, 2, 2, N], F32, name="ee_turned")
+        nc.scalar.copy(ee_turned[:], ee_bank[:])
+        lb_turned = keep.tile([P, 2, 2, N], F32, name="lb_turned")
+        nc.scalar.copy(lb_turned[:], lb_bank[:])
+        for piece in plain:
+            on_scalar(lb_picked[piece][:], lb_table[:], piece * PIECE)
 
         def turned_back(total, addend, opens):
-            count = addend.shape[1]
-            for c in range(count):
+            for c in range(2):
                 nc.tensor.matmul(
                     total[:, c * CHUNK : (c + 1) * CHUNK],
                     lhsT=addend[:, c, :],
                     rhs=identity[:],
                     is_transpose=True,
                     start=opens and c == 0,
-                    stop=not opens and c == count - 1,
+                    stop=not opens and c == 1,
                 )
 
-        def opened(chunks, tag, bufs):
-            total = psum.tile([P, (chunks.stop - chunks.start) * CHUNK], F32, name="total", tag=tag, bufs=bufs)
-            half, c = divmod(chunks.start, per_bank)
-            turned_back(total, ee_turned[half][:, c : c + chunks.stop - chunks.start, :], True)
-            return total
+        h_quantised = {
+            piece: quantised(f"h{piece}", h_bf[piece][:], offset)
+            for piece, offset in ((0, 12 * KIB), (2, 12 * KIB + 256), (3, None), (1, None))
+        }
+        rr = {}
+        totals = {}
+        for g, piece in enumerate(turned):
+            rr[piece] = bank(3 + g, [P, 2, N], f"rr{piece}")
+            codes, scales = h_quantised[piece]
+            for c in range(2):
+                cols = slice(c * CHUNK, (c + 1) * CHUNK)
+                product(rr[piece][:, c, :], (codes[:, cols], scales[:, cols]), w2_quantised)
+        for g, piece in enumerate(plain):
+            rr[piece] = bank(5 + g, [P, PIECE], f"rr{piece}")
+            product(rr[piece][:], w2_quantised, h_quantised[piece])
+        for g, piece in enumerate(turned):
+            totals[piece] = bank(7 * g, [P, PIECE], f"total{piece}")
+            turned_back(totals[piece], ee_turned[:, g, :, :], True)
+        ee_plain = bank(1, [P, 2, PIECE], "ee_plain")
+        for g, piece in enumerate(plain):
+            product(ee_plain[:, g, :], w3_quantised, picked_x(piece * PIECE, PIECE))
 
-        def finish(chunks, rr, total, term, queue):
-            first, width = chunks.start * CHUNK, (chunks.stop - chunks.start) * CHUNK
-            half, c = divmod(chunks.start, per_bank)
-            nc.vector.tensor_tensor(term[:], rr, lb_turned[half][:, c : c + width // CHUNK, :], MULT)
-            turned_back(total, term[:], False)
-            result = keep.tile([P, width], F32, name=f"result{first}")
-            nc.scalar.activation(result[:], total[:], SILU)
-            queue.dma_start(out[:, first : first + width], result[:])
+        def finish(piece, total, queue):
+            result = keep.tile([P, PIECE], F32, name=f"result{piece}")
+            nc.scalar.activation(result[:], total, SILU)
+            queue.dma_start(out[:, piece * PIECE : (piece + 1) * PIECE], result[:])
 
-        look_up(on_scalar, 3, pieces[0])
-        look_up(on_scalar, 3, pieces[1])
-        w3_bf = rounded_weight(h_of(2), w3_raw)
-        hidden(0)
-        w3_quantised = quantised("w3", w3_bf)
-        hidden(1)
-        look_up(on_scalar, 3, pieces[2])
-        hidden_aside(h_of(2), copied_out(planes_of_y(2, "a", 1)[:], 32), 2 * CHUNK, CHUNK)
-        hidden(4)
-        look_up(on_scalar, 3, pieces[3])
-        y_shared = planes_of_y(3, "b", 1)
-        woven_shared = copied_out(y_shared[:, :, 0:SHARE], 34)
-        hidden(6)
-        multiply(h_of(3)[:, SHARE * PACK :], y_shared[:, :, SHARE:CHUNK], 3 * CHUNK + SHARE, CHUNK - SHARE)
-        hidden_aside(h_of(3)[:, 0 : SHARE * PACK], woven_shared, 3 * CHUNK, SHARE)
-        hidden(5)
-        hidden(7)
-        w2_bf = turns.tile([P, N * PACK], BF16, name="w2_bf", align_bytes=64, offset=21 * KIB)
-        rounded_weight(w2_bf[:], w2_raw)
-        copy_ee(0, frozen_layer(0, "c", w3_quantised))
-        copy_ee(1, frozen_layer(1, "e", w3_quantised))
-        w2_quantised = quantised("w2", w2_bf[:], 17 * KIB + 256)
-        h0 = quantised("h0", h_bf[0][:], 17 * KIB)
-        h2 = quantised("h2", h_bf[2][:], 17 * KIB + 512)
-        h3 = quantised("h3", h_bf[3][:])
-        h10 = quantised("h10", h_of(2), 17 * KIB + 768)
-        h11 = quantised("h11", h_of(3), 17 * KIB + 896)
-        groups = [slice(0, 2), slice(4, 6), slice(6, 8), slice(2, 4)]
-        totals = [opened(chunks, tag, bufs) for chunks, tag, bufs in zip(groups, "cedy", (1, 1, 1, 3))]
-        rrs = []
-        for h, tag, bufs in zip((h0, h2, h3), "ayy", (1, 3, 3)):
-            rr = psum.tile([P, 2, N], F32, name="rr", tag=tag, bufs=bufs)
-            second_product(rr[:], h, w2_quantised)
-            rrs.append(rr)
-        rr = psum.tile([P, 2, N], F32, name="rr", tag="b", bufs=1)
-        second_product(rr[:, 0:1, :], h10, w2_quantised)
-        second_product(rr[:, 1:2, :], h11, w2_quantised)
-        rrs.append(rr)
-        terms = [turns.tile([P, 2, N], F32, name=f"term{g}", offset=(18 + g) * KIB) for g in range(2)]
-        terms.extend(keep.tile([P, 2, N], F32, name=f"term{2 + g}") for g in range(2))
-        for g, rr in enumerate(rrs):
-            finish(groups[g], rr[:], totals[g], terms[g], nc.scalar if g == 3 else nc.sync)
+        for g, piece in enumerate(turned):
+            term = keep.tile([P, 2, N], F32, name=f"term{piece}")
+            nc.vector.tensor_tensor(term[:], rr[piece][:], lb_turned[:, g, :, :], MULT)
+            turned_back(totals[piece], term[:], False)
+            finish(piece, totals[piece][:], nc.sync)
+        terms = {}
+        for piece in plain:
+            terms[piece] = keep.tile([P, PIECE], F32, name=f"term{piece}")
+            nc.vector.tensor_tensor(terms[piece][:], rr[piece][:], lb_picked[piece][:], MULT)
+        for g, piece in enumerate(plain):
+            total = keep.tile([P, PIECE], F32, name=f"sum{piece}")
+            nc.vector.tensor_tensor(total[:], ee_plain[:, g, :], terms[piece][:], ADD)
+            finish(piece, total[:], nc.scalar if g == 1 else nc.sync)

@@ -101,9 +101,9 @@ def tile_picked_yvera_silu_p_kernel(
         for t, table in ((0, ld_first), (1, ld_middle), (3, ld_last)):
             for first in pieces:
                 on_scalar(picked_planes(first, PIECE)[:, t, :], table[:], first)
+        nc.sync.dma_start(w3_raw[:], w3.rearrange("(p j) c -> p j c", j=PACK))
         for r in range(4):
             nc.sync.dma_start(x_bytes[r:P:32, :].bitcast(I32), spread_bytes[8 * r : P : 32, :].bitcast(I32))
-        nc.sync.dma_start(w3_raw[:], w3.rearrange("(p j) c -> p j c", j=PACK))
         nc.sync.dma_start(w2_raw[:], w2.rearrange("(p j) c -> p j c", j=PACK))
         nc.sync.dma_start(lb_table[:], lb)
 
@@ -124,8 +124,8 @@ def tile_picked_yvera_silu_p_kernel(
 
         def round_w1(copy, rounded, half, pair):
             copy(
-                rounded[:].rearrange("p (t m j) -> p m t j", t=PAIR, j=PACK),
-                w1_raw[half][:].rearrange("p j (m t) -> p m t j", t=PACK)[:, :, PAIR * pair : PAIR * (pair + 1), :],
+                rounded[:].rearrange("p (t m j) -> p m j t", t=PAIR, j=PACK),
+                w1_raw[half][:].rearrange("p j (m t) -> p m j t", t=PACK)[:, :, :, PAIR * pair : PAIR * (pair + 1)],
             )
 
         def quantise_w1(rounded, half, pair):
@@ -167,7 +167,7 @@ def tile_picked_yvera_silu_p_kernel(
         def w1_plane(t):
             return w1_codes[:, t * P : (t + 1) * P], w1_scales[:, t * P : (t + 1) * P]
 
-        order = (0, 2, 1, 4, 3, 6, 5, 7)
+        order = (0, 2, 1, 3, 4, 6, 5, 7)
         y = {c: bank(number, [P, PACK, CHUNK], f"y{c}") for number, c in enumerate(order)}
 
         def plane_of_y(c, t):
@@ -183,7 +183,8 @@ def tile_picked_yvera_silu_p_kernel(
             for t in range(PACK):
                 plane_of_y(c, t)
 
-        h_bf = [keep.tile([P, PIECE * PACK], BF16, name=f"h_bf{u}", align_bytes=64) for u in range(S // PIECE)]
+        h_bf = {u: keep.tile([P, PIECE * PACK], BF16, name=f"h_bf{u}", align_bytes=64) for u in (0, 2, 3)}
+        h_bf[1] = turns.tile([P, PIECE * PACK], BF16, name="h_bf1", align_bytes=64, offset=26 * KIB)
 
         def in_pairs(planes):
             return planes.rearrange("p t (c i) -> p c t i", i=PAIR)
@@ -200,13 +201,12 @@ def tile_picked_yvera_silu_p_kernel(
             nc.scalar.copy(woven[:], in_pairs(y[c][:]))
             nc.gpsimd.tensor_tensor(h_of(c), woven[:], in_pairs(picked_planes(c * CHUNK, CHUNK)), MULT)
 
-        def rounded_weight(name, raw):
-            rounded = keep.tile([P, N * PACK], BF16, name=f"{name}_bf", align_bytes=64)
+        def rounded_weight(rounded, raw):
             nc.scalar.copy(
-                rounded[:].rearrange("p (c i j) -> p c j i", i=RUN, j=PACK),
+                rounded.rearrange("p (c i j) -> p c j i", i=RUN, j=PACK),
                 raw[:].rearrange("p j (c i) -> p c j i", i=RUN),
             )
-            return rounded[:]
+            return rounded
 
         def quantised(name, rounded, offset=None):
             width = rounded.shape[1] // PACK
@@ -224,19 +224,19 @@ def tile_picked_yvera_silu_p_kernel(
         ]
         lb_picked = [
             turns.tile([P, PIECE], F32, name=f"lb_picked{u}", offset=offset * KIB)
-            for u, offset in enumerate((22, 23, 23, 2))
+            for u, offset in enumerate((22, 23, 23, 22))
         ]
 
-        w3_quantised = quantised("w3", rounded_weight("w3", w3_raw))
-        w2_bf = rounded_weight("w2", w2_raw)
+        w3_quantised = quantised("w3", rounded_weight(h_bf[0][:, 0 : N * PACK], w3_raw))
+        w2_bf = keep.tile([P, N * PACK], BF16, name="w2_bf", align_bytes=64)
+        rounded_weight(w2_bf[:], w2_raw)
         hidden(0)
-        w2_quantised = quantised("w2", w2_bf)
         hidden_aside(2, woven[0])
         on_scalar(lb_picked[0][:], lb_table[:], 0)
         hidden(1)
-        hidden(4)
         hidden_aside(3, woven[1])
         on_scalar(lb_picked[2][:], lb_table[:], 2 * PIECE)
+        hidden(4)
         hidden(6)
         hidden(5)
         hidden(7)
@@ -268,6 +268,7 @@ def tile_picked_yvera_silu_p_kernel(
                     stop=not opens and c == 1,
                 )
 
+        w2_quantised = quantised("w2", w2_bf[:], 12 * KIB + 512)
         h_quantised = {
             piece: quantised(f"h{piece}", h_bf[piece][:], offset)
             for piece, offset in ((0, 12 * KIB), (2, 12 * KIB + 256), (3, None), (1, None))
@@ -295,14 +296,15 @@ def tile_picked_yvera_silu_p_kernel(
             nc.scalar.activation(result[:], total, SILU)
             queue.dma_start(out[:, piece * PIECE : (piece + 1) * PIECE], result[:])
 
+        term_offsets = {0: 25 * KIB + 32, 2: 26 * KIB + 512, 3: 28 * KIB - 32, 1: 30 * KIB}
         for g, piece in enumerate(turned):
-            term = keep.tile([P, 2, N], F32, name=f"term{piece}")
+            term = turns.tile([P, 2, N], F32, name=f"term{piece}", offset=term_offsets[piece])
             nc.vector.tensor_tensor(term[:], rr[piece][:], lb_turned[:, g, :, :], MULT)
             turned_back(totals[piece], term[:], False)
             finish(piece, totals[piece][:], nc.sync)
         terms = {}
         for piece in plain:
-            terms[piece] = keep.tile([P, PIECE], F32, name=f"term{piece}")
+            terms[piece] = turns.tile([P, PIECE], F32, name=f"term{piece}", offset=term_offsets[piece])
             nc.vector.tensor_tensor(terms[piece][:], rr[piece][:], lb_picked[piece][:], MULT)
         for g, piece in enumerate(plain):
             total = keep.tile([P, PIECE], F32, name=f"sum{piece}")

@@ -26,6 +26,7 @@ CHUNK = 128
 PIECE = 256
 RUN = 4
 PAIR = 2
+SHARE = 96
 HALF = H // 2
 SIDE = P // 2
 
@@ -184,22 +185,33 @@ def tile_picked_yvera_silu_p_kernel(
                 plane_of_y(c, t)
 
         h_bf = {u: keep.tile([P, PIECE * PACK], BF16, name=f"h_bf{u}", align_bytes=64) for u in (0, 2, 3)}
-        h_bf[1] = turns.tile([P, PIECE * PACK], BF16, name="h_bf1", align_bytes=64, offset=26 * KIB)
+        h_single = {
+            2: keep.tile([P, CHUNK * PACK], BF16, name="h_single2", align_bytes=64),
+            3: turns.tile([P, CHUNK * PACK], BF16, name="h_single3", align_bytes=64, offset=26 * KIB),
+        }
 
         def in_pairs(planes):
             return planes.rearrange("p t (c i) -> p c t i", i=PAIR)
 
-        def h_of(c):
-            piece, col = divmod(c * CHUNK, PIECE)
-            target = h_bf[piece][:, col * PACK : (col + CHUNK) * PACK]
-            return target.rearrange("p (c i t) -> p c t i", i=PAIR, t=PACK)
+        def h_of(c, cols):
+            if c in h_single:
+                rows = h_single[c][:]
+            else:
+                piece, col = divmod(c * CHUNK, PIECE)
+                rows = h_bf[piece][:, col * PACK : (col + CHUNK) * PACK]
+            return rows[:, cols.start * PACK : cols.stop * PACK].rearrange("p (c i t) -> p c t i", i=PAIR, t=PACK)
 
-        def hidden(c):
-            nc.vector.tensor_tensor(h_of(c), in_pairs(y[c][:]), in_pairs(picked_planes(c * CHUNK, CHUNK)), MULT)
+        def ld_of(c, cols):
+            return in_pairs(picked_planes(c * CHUNK + cols.start, cols.stop - cols.start))
 
-        def hidden_aside(c, woven):
-            nc.scalar.copy(woven[:], in_pairs(y[c][:]))
-            nc.gpsimd.tensor_tensor(h_of(c), woven[:], in_pairs(picked_planes(c * CHUNK, CHUNK)), MULT)
+        def hidden(c, cols=slice(0, CHUNK)):
+            nc.vector.tensor_tensor(h_of(c, cols), in_pairs(y[c][:, :, cols]), ld_of(c, cols), MULT)
+
+        def hidden_aside(c, cols, offset):
+            width = cols.stop - cols.start
+            woven = turns.tile([P, width // PAIR, PACK, PAIR], F32, name=f"woven{c}", offset=offset * KIB)
+            nc.scalar.copy(woven[:], in_pairs(y[c][:, :, cols]))
+            nc.gpsimd.tensor_tensor(h_of(c, cols), woven[:], ld_of(c, cols), MULT)
 
         def rounded_weight(rounded, raw):
             nc.scalar.copy(
@@ -218,10 +230,6 @@ def tile_picked_yvera_silu_p_kernel(
             nc.vector.quantize_mx(codes[:].bitcast(FP8X4), scales[:], rounded)
             return codes[:], scales[:]
 
-        woven = [
-            turns.tile([P, CHUNK // PAIR, PACK, PAIR], F32, name=f"woven{u}", offset=offset * KIB)
-            for u, offset in enumerate((2, 20))
-        ]
         lb_picked = [
             turns.tile([P, PIECE], F32, name=f"lb_picked{u}", offset=offset * KIB)
             for u, offset in enumerate((22, 23, 23, 22))
@@ -231,10 +239,11 @@ def tile_picked_yvera_silu_p_kernel(
         w2_bf = keep.tile([P, N * PACK], BF16, name="w2_bf", align_bytes=64)
         rounded_weight(w2_bf[:], w2_raw)
         hidden(0)
-        hidden_aside(2, woven[0])
+        hidden_aside(2, slice(0, CHUNK), 2)
         on_scalar(lb_picked[0][:], lb_table[:], 0)
         hidden(1)
-        hidden_aside(3, woven[1])
+        hidden(3, slice(SHARE, CHUNK))
+        hidden_aside(3, slice(0, SHARE), 20)
         on_scalar(lb_picked[2][:], lb_table[:], 2 * PIECE)
         hidden(4)
         hidden(6)
@@ -271,8 +280,11 @@ def tile_picked_yvera_silu_p_kernel(
         w2_quantised = quantised("w2", w2_bf[:], 12 * KIB + 512)
         h_quantised = {
             piece: quantised(f"h{piece}", h_bf[piece][:], offset)
-            for piece, offset in ((0, 12 * KIB), (2, 12 * KIB + 256), (3, None), (1, None))
+            for piece, offset in ((0, 12 * KIB), (2, 12 * KIB + 256), (3, None))
         }
+        h_singles = [
+            quantised(f"h_single{c}", h_single[c][:], offset) for c, offset in ((2, 12 * KIB + 768), (3, None))
+        ]
         rr = {}
         totals = {}
         for g, piece in enumerate(turned):
@@ -283,7 +295,10 @@ def tile_picked_yvera_silu_p_kernel(
                 product(rr[piece][:, c, :], (codes[:, cols], scales[:, cols]), w2_quantised)
         for g, piece in enumerate(plain):
             rr[piece] = bank(5 + g, [P, PIECE], f"rr{piece}")
-            product(rr[piece][:], w2_quantised, h_quantised[piece])
+            parts = h_singles if piece == 1 else [h_quantised[piece]]
+            width = PIECE // len(parts)
+            for c, part in enumerate(parts):
+                product(rr[piece][:, c * width : (c + 1) * width], w2_quantised, part)
         for g, piece in enumerate(turned):
             totals[piece] = bank(7 * g, [P, PIECE], f"total{piece}")
             turned_back(totals[piece], ee_turned[:, g, :, :], True)
@@ -296,17 +311,17 @@ def tile_picked_yvera_silu_p_kernel(
             nc.scalar.activation(result[:], total, SILU)
             queue.dma_start(out[:, piece * PIECE : (piece + 1) * PIECE], result[:])
 
-        term_offsets = {0: 25 * KIB + 32, 2: 26 * KIB + 512, 3: 28 * KIB - 32, 1: 30 * KIB}
+        held_terms = turns.tile([P, 3, PIECE], F32, name="held_terms", offset=26 * KIB)
+        last_term = keep.tile([P, PIECE], F32, name="last_term")
+        terms = {0: held_terms[:, 0, :], 2: held_terms[:, 1, :], 3: held_terms[:, 2, :], 1: last_term[:]}
         for g, piece in enumerate(turned):
-            term = turns.tile([P, 2, N], F32, name=f"term{piece}", offset=term_offsets[piece])
-            nc.vector.tensor_tensor(term[:], rr[piece][:], lb_turned[:, g, :, :], MULT)
-            turned_back(totals[piece], term[:], False)
+            term = terms[piece].rearrange("p (c m) -> p c m", c=2)
+            nc.vector.tensor_tensor(term, rr[piece][:], lb_turned[:, g, :, :], MULT)
+            turned_back(totals[piece], term, False)
             finish(piece, totals[piece][:], nc.sync)
-        terms = {}
         for piece in plain:
-            terms[piece] = turns.tile([P, PIECE], F32, name=f"term{piece}", offset=term_offsets[piece])
-            nc.vector.tensor_tensor(terms[piece][:], rr[piece][:], lb_picked[piece][:], MULT)
+            nc.vector.tensor_tensor(terms[piece], rr[piece][:], lb_picked[piece][:], MULT)
         for g, piece in enumerate(plain):
             total = keep.tile([P, PIECE], F32, name=f"sum{piece}")
-            nc.vector.tensor_tensor(total[:], ee_plain[:, g, :], terms[piece][:], ADD)
+            nc.vector.tensor_tensor(total[:], ee_plain[:, g, :], terms[piece], ADD)
             finish(piece, total[:], nc.scalar if g == 1 else nc.sync)

@@ -147,12 +147,6 @@ def tile_picked_yvera_silu_p_kernel(
         round_w1(nc.scalar.copy, w1_bf[0, 0], 0, 0)
         round_w1(nc.scalar.copy, w1_bf[0, 1], 0, 1)
         quantise_w1(w1_bf[0, 0], 0, 0)
-        round_w1(nc.vector.tensor_copy, w1_bf[1, 0], 1, 0)
-        round_w1(nc.scalar.copy, w1_bf[1, 1], 1, 1)
-        quantise_w1(w1_bf[0, 1], 0, 1)
-        quantise_w1(w1_bf[1, 0], 1, 0)
-        quantise_w1(w1_bf[1, 1], 1, 1)
-        gather_words(turns.tile([P, PIECE], U32, name="x_codes3", align_bytes=64, offset=0), 3 * PIECE)
 
         def product(target, stationary, moving):
             nc.tensor.matmul_mx(
@@ -167,6 +161,19 @@ def tile_picked_yvera_silu_p_kernel(
 
         def w1_plane(t):
             return w1_codes[:, t * P : (t + 1) * P], w1_scales[:, t * P : (t + 1) * P]
+
+        warm_codes = keep.tile([P, P], U32, name="warm_codes", align_bytes=64)
+        warm_scales = keep.tile([P, P], U8, name="warm_scales", align_bytes=64)
+        nc.vector.quantize_mx(warm_codes[:].bitcast(FP8X4), warm_scales[:], w1_bf[0, 0][:])
+        warm_bank = bank(7, [P, PACK, CHUNK], "warm_bank")
+        for u in range(PACK):
+            product(warm_bank[:, u, :], (warm_codes[:], warm_scales[:]), (warm_codes[:], warm_scales[:]))
+        round_w1(nc.vector.tensor_copy, w1_bf[1, 0], 1, 0)
+        round_w1(nc.scalar.copy, w1_bf[1, 1], 1, 1)
+        quantise_w1(w1_bf[0, 1], 0, 1)
+        quantise_w1(w1_bf[1, 0], 1, 0)
+        quantise_w1(w1_bf[1, 1], 1, 1)
+        gather_words(turns.tile([P, PIECE], U32, name="x_codes3", align_bytes=64, offset=0), 3 * PIECE)
 
         order = (0, 2, 1, 3, 4, 6, 5, 7)
         y = {c: bank(number, [P, PACK, CHUNK], f"y{c}") for number, c in enumerate(order)}

@@ -73,10 +73,10 @@ def tile_picked_yvera_silu_p_kernel(
         w1_rows = w1.rearrange("(p j) c -> p j c", j=PACK)
         nc.sync.dma_start(ld_first[:], ld_rows[:, 0:R])
         nc.sync.dma_start(ad_list[:], ad)
-        nc.sync.dma_start(ld_middle[:], ld_rows[:, R : 3 * R])
+        nc.sync.dma_start(ld_last[:], ld_rows[:, 3 * R : 4 * R])
         nc.sync.dma_start(token_list[:], offs)
         nc.sync.dma_start(scale_table[0:P:8, :].bitcast(I32), x_scales[0].bitcast(I32))
-        nc.sync.dma_start(ld_last[:], ld_rows[:, 3 * R : 4 * R])
+        nc.sync.dma_start(ld_middle[:], ld_rows[:, R : 3 * R])
         nc.sync.dma_start(word_table[:], x_words[0].rearrange("p c t -> p (c t)").bitcast(I32))
         for half in range(2):
             nc.sync.dma_start(w1_raw[half][:], w1_rows[:, :, half * HALF : (half + 1) * HALF])
@@ -90,17 +90,18 @@ def tile_picked_yvera_silu_p_kernel(
             return ld_picked[piece][:, :, col : col + width]
 
         def on_scalar(target, window, first):
-            nc.scalar.activation(target, window.indirect(entries(ad_list, first, PIECE)), COPY)
+            nc.scalar.activation(target, window.indirect(entries(ad_list, first, target.shape[1])), COPY)
 
         pieces = range(0, S, PIECE)
+        nc.vector.tensor_copy(picked_planes(0, PIECE)[:, 0, :], ld_first[:].indirect(entries(ad_list, 0, PIECE)))
         spread_bytes = keep.tile([P, S], U8, name="spread_bytes")
         nc.vector.tensor_copy(spread_bytes[:], scale_table[:].indirect(token_list[:]))
         for first in pieces:
             nc.vector.tensor_copy(
                 picked_planes(first, PIECE)[:, 2, :], ld_middle[:, R : 2 * R].indirect(entries(ad_list, first, PIECE))
             )
-        for t, table in ((0, ld_first), (1, ld_middle), (3, ld_last)):
-            for first in pieces:
+        for t, table, share in ((0, ld_first, pieces[1:]), (3, ld_last, pieces), (1, ld_middle, pieces)):
+            for first in share:
                 on_scalar(picked_planes(first, PIECE)[:, t, :], table[:], first)
         nc.sync.dma_start(w3_raw[:], w3.rearrange("(p j) c -> p j c", j=PACK))
         for r in range(4):

@@ -26,7 +26,6 @@ CHUNK = 128
 PIECE = 256
 RUN = 4
 PAIR = 2
-SHARE = 96
 HALF = H // 2
 SIDE = P // 2
 
@@ -100,9 +99,12 @@ def tile_picked_yvera_silu_p_kernel(
             nc.vector.tensor_copy(
                 picked_planes(first, PIECE)[:, 2, :], ld_middle[:, R : 2 * R].indirect(entries(ad_list, first, PIECE))
             )
-        for t, table, share in ((0, ld_first, pieces[1:]), (3, ld_last, pieces), (1, ld_middle, pieces)):
+        aside_first = (pieces[1], pieces[0], pieces[2], pieces[3])
+        for t, table, share in ((0, ld_first, pieces[1:]), (3, ld_last, pieces), (1, ld_middle, aside_first)):
             for first in share:
                 on_scalar(picked_planes(first, PIECE)[:, t, :], table[:], first)
+        ld_woven = keep.tile([P, PIECE, PACK], F32, name="ld_woven")
+        nc.vector.tensor_copy(ld_woven[:], ld_picked[1][:].rearrange("p t c -> p c t"))
         nc.sync.dma_start(w3_raw[:], w3.rearrange("(p j) c -> p j c", j=PACK))
         for r in range(4):
             nc.sync.dma_start(x_bytes[r:P:32, :].bitcast(I32), spread_bytes[8 * r : P : 32, :].bitcast(I32))
@@ -193,33 +195,33 @@ def tile_picked_yvera_silu_p_kernel(
                 plane_of_y(c, t)
 
         h_bf = {u: keep.tile([P, PIECE * PACK], BF16, name=f"h_bf{u}", align_bytes=64) for u in (0, 2, 3)}
-        h_single = {
-            2: keep.tile([P, CHUNK * PACK], BF16, name="h_single2", align_bytes=64),
-            3: turns.tile([P, CHUNK * PACK], BF16, name="h_single3", align_bytes=64, offset=26 * KIB),
-        }
+        h_bf[1] = turns.tile([P, PIECE * PACK], BF16, name="h_bf1", align_bytes=64, offset=26 * KIB)
 
         def in_pairs(planes):
             return planes.rearrange("p t (c i) -> p c t i", i=PAIR)
 
-        def h_of(c, cols):
-            if c in h_single:
-                rows = h_single[c][:]
-            else:
-                piece, col = divmod(c * CHUNK, PIECE)
-                rows = h_bf[piece][:, col * PACK : (col + CHUNK) * PACK]
-            return rows[:, cols.start * PACK : cols.stop * PACK].rearrange("p (c i t) -> p c t i", i=PAIR, t=PACK)
+        def h_of(c):
+            piece, col = divmod(c * CHUNK, PIECE)
+            return h_bf[piece][:, col * PACK : (col + CHUNK) * PACK]
 
-        def ld_of(c, cols):
-            return in_pairs(picked_planes(c * CHUNK + cols.start, cols.stop - cols.start))
+        def hidden(c):
+            nc.vector.tensor_tensor(
+                h_of(c).rearrange("p (c i t) -> p c t i", i=PAIR, t=PACK),
+                in_pairs(y[c][:]),
+                in_pairs(picked_planes(c * CHUNK, CHUNK)),
+                MULT,
+            )
 
-        def hidden(c, cols=slice(0, CHUNK)):
-            nc.vector.tensor_tensor(h_of(c, cols), in_pairs(y[c][:, :, cols]), ld_of(c, cols), MULT)
-
-        def hidden_aside(c, cols, offset):
-            width = cols.stop - cols.start
-            woven = turns.tile([P, width // PAIR, PACK, PAIR], F32, name=f"woven{c}", offset=offset * KIB)
-            nc.scalar.copy(woven[:], in_pairs(y[c][:, :, cols]))
-            nc.gpsimd.tensor_tensor(h_of(c, cols), woven[:], ld_of(c, cols), MULT)
+        def hidden_aside(c, offset):
+            y_woven = turns.tile([P, CHUNK, PACK], F32, name=f"y_woven{c}", offset=offset * KIB)
+            nc.scalar.copy(y_woven[:], y[c][:].rearrange("p t c -> p c t"))
+            col = c * CHUNK - PIECE
+            nc.gpsimd.tensor_tensor(
+                h_of(c),
+                y_woven[:].rearrange("p c t -> p (c t)"),
+                ld_woven[:, col : col + CHUNK, :].rearrange("p c t -> p (c t)"),
+                MULT,
+            )
 
         def rounded_weight(rounded, raw):
             nc.scalar.copy(
@@ -247,11 +249,10 @@ def tile_picked_yvera_silu_p_kernel(
         w2_bf = keep.tile([P, N * PACK], BF16, name="w2_bf", align_bytes=64)
         rounded_weight(w2_bf[:], w2_raw)
         hidden(0)
-        hidden_aside(2, slice(0, CHUNK), 2)
+        hidden_aside(2, 2)
         on_scalar(lb_picked[0][:], lb_table[:], 0)
         hidden(1)
-        hidden(3, slice(SHARE, CHUNK))
-        hidden_aside(3, slice(0, SHARE), 20)
+        hidden_aside(3, 20)
         on_scalar(lb_picked[2][:], lb_table[:], 2 * PIECE)
         hidden(4)
         hidden(6)
@@ -288,11 +289,8 @@ def tile_picked_yvera_silu_p_kernel(
         w2_quantised = quantised("w2", w2_bf[:], 12 * KIB + 512)
         h_quantised = {
             piece: quantised(f"h{piece}", h_bf[piece][:], offset)
-            for piece, offset in ((0, 12 * KIB), (2, 12 * KIB + 256), (3, None))
+            for piece, offset in ((0, 12 * KIB), (2, 12 * KIB + 256), (3, None), (1, None))
         }
-        h_singles = [
-            quantised(f"h_single{c}", h_single[c][:], offset) for c, offset in ((2, 12 * KIB + 768), (3, None))
-        ]
         rr = {}
         totals = {}
         for g, piece in enumerate(turned):
@@ -303,10 +301,7 @@ def tile_picked_yvera_silu_p_kernel(
                 product(rr[piece][:, c, :], (codes[:, cols], scales[:, cols]), w2_quantised)
         for g, piece in enumerate(plain):
             rr[piece] = bank(5 + g, [P, PIECE], f"rr{piece}")
-            parts = h_singles if piece == 1 else [h_quantised[piece]]
-            width = PIECE // len(parts)
-            for c, part in enumerate(parts):
-                product(rr[piece][:, c * width : (c + 1) * width], w2_quantised, part)
+            product(rr[piece][:], w2_quantised, h_quantised[piece])
         for g, piece in enumerate(turned):
             totals[piece] = bank(7 * g, [P, PIECE], f"total{piece}")
             turned_back(totals[piece], ee_turned[:, g, :, :], True)

@@ -245,9 +245,11 @@ def tile_picked_yvera_silu_p_kernel(
             for u, offset in enumerate((22, 23, 23, 22))
         ]
 
-        w3_quantised = quantised("w3", rounded_weight(h_bf[0][:, 0 : N * PACK], w3_raw))
-        w2_bf = keep.tile([P, N * PACK], BF16, name="w2_bf", align_bytes=64)
-        rounded_weight(w2_bf[:], w2_raw)
+        small_bf = keep.tile([P, N * PACK], BF16, name="small_bf", align_bytes=64)
+        w3_quantised = quantised("w3", rounded_weight(small_bf[:], w3_raw))
+        nc.gpsimd.tensor_scalar(
+            small_bf[:].rearrange("p (c j) -> p c j", j=PACK), w2_raw[:].rearrange("p j c -> p c j"), 1.0, 0.0, MULT, ADD
+        )
         hidden(0)
         hidden_aside(2, 2)
         on_scalar(lb_picked[0][:], lb_table[:], 0)
@@ -286,7 +288,7 @@ def tile_picked_yvera_silu_p_kernel(
                     stop=not opens and c == 1,
                 )
 
-        w2_quantised = quantised("w2", w2_bf[:], 12 * KIB + 512)
+        w2_quantised = quantised("w2", small_bf[:], 12 * KIB + 512)
         h_quantised = {
             piece: quantised(f"h{piece}", h_bf[piece][:], offset)
             for piece, offset in ((0, 12 * KIB), (2, 12 * KIB + 256), (3, None), (1, None))

from contextlib import ExitStack

import concourse.mybir as mybir
from concourse.masks import make_identity

K, T, S, H, N, R = 512, 4096, 1024, 512, 128, 512
FLOPS = 2 * S * (K * N + K * H + H * N)

F32 = mybir.dt.float32
BF16 = mybir.dt.bfloat16
I32 = mybir.dt.int32
U32 = mybir.dt.uint32
U16 = mybir.dt.uint16
U8 = mybir.dt.uint8
FP8X4 = mybir.dt.float8_e4m3fn_x4
MULT = mybir.AluOpType.mult
ADD = mybir.AluOpType.add
SILU = mybir.ActivationFunctionType.Silu
COPY = mybir.ActivationFunctionType.Copy

P = 128
KIB = 1024
PACK = 4
LIST = 16
CHUNK = 128
PIECE = 256
RUN = 4
PAIR = 2
HALF = H // 2
SIDE = P // 2


def tile_picked_yvera_silu_p_kernel(
    tc, x_words, x_scales, w1, w2, w3, ld, lb, offs, ad, out
):
    nc = tc.nc
    with ExitStack() as ctx:
        lists = ctx.enter_context(tc.tile_pool(name="lists", bufs=1))
        keep = ctx.enter_context(tc.tile_pool(name="keep", bufs=1))
        turns = ctx.enter_context(tc.tile_pool(name="turns", bufs=1))
        psum = ctx.enter_context(tc.psum_pool(name="psum", bufs=1))

        ad_list = lists.tile([P, S // LIST], U16, name="ad_list")
        token_list = lists.tile([P, S // LIST], U16, name="token_list")
        ld_first = keep.tile([P, R], F32, name="ld_first")
        ld_middle = keep.tile([P, 2 * R], F32, name="ld_middle")
        ld_last = keep.tile([P, R], F32, name="ld_last")
        word_table = keep.tile([P, T], I32, name="word_table")
        scale_table = keep.tile([P, T], U8, name="scale_table")
        lb_table = keep.tile([P, R], F32, name="lb_table")
        w1_raw = [keep.tile([P, PACK, HALF], F32, name=f"w1_raw{half}") for half in range(2)]
        w3_raw = keep.tile([P, PACK, N], F32, name="w3_raw")
        w2_raw = keep.tile([P, PACK, N], F32, name="w2_raw")
        x_bytes = keep.tile([P, S], U8, name="x_bytes", align_bytes=64)

        def entries(index_list, first, count):
            return index_list[:, first // LIST : (first + count) // LIST]

        def bank(number, shape, name):
            return psum.tile(shape, F32, name=name, tag=f"bank{number}", bufs=1)

        nc.vector.memset(scale_table[:].bitcast(I32), 0)
        nc.vector.memset(x_bytes[:].bitcast(I32), 0)
        warm_in = keep.tile([P, 1], F32, name="warm_in")
        warm_out = keep.tile([P, 1], F32, name="warm_out")
        nc.vector.memset(warm_in[:], 0.0)
        nc.scalar.activation(warm_out[:], warm_in[:], SILU)
        identity = keep.tile([P, P], F32, name="identity")
        make_identity(nc, identity[:])

        ld_rows = ld.rearrange("(p t) r -> p (t r)", t=PACK)
        w1_rows = w1.rearrange("(p j) c -> p j c", j=PACK)
        nc.sync.dma_start(ld_first[:], ld_rows[:, 0:R])
        nc.sync.dma_start(ad_list[:], ad)
        nc.sync.dma_start(ld_last[:], ld_rows[:, 3 * R : 4 * R])
        nc.sync.dma_start(token_list[:], offs)
        nc.sync.dma_start(scale_table[0:P:8, :].bitcast(I32), x_scales[0].bitcast(I32))
        nc.sync.dma_start(ld_middle[:], ld_rows[:, R : 3 * R])
        nc.sync.dma_start(word_table[:], x_words[0].rearrange("p c t -> p (c t)").bitcast(I32))
        for half in range(2):
            nc.sync.dma_start(w1_raw[half][:], w1_rows[:, :, half * HALF : (half + 1) * HALF])

        ld_picked = [
            turns.tile([P, PACK, PIECE], F32, name=f"ld_picked{u}", offset=(4 + 4 * u) * KIB) for u in range(S // PIECE)
        ]

        def picked_planes(first, width):
            piece, col = divmod(first, PIECE)
            return ld_picked[piece][:, :, col : col + width]

        def on_scalar(target, window, first):
            nc.scalar.activation(target, window.indirect(entries(ad_list, first, target.shape[1])), COPY)

        pieces = range(0, S, PIECE)
        nc.vector.tensor_copy(picked_planes(0, PIECE)[:, 0, :], ld_first[:].indirect(entries(ad_list, 0, PIECE)))
        spread_bytes = keep.tile([P, S], U8, name="spread_bytes")
        nc.vector.tensor_copy(spread_bytes[:], scale_table[:].indirect(token_list[:]))
        for first in pieces:
            nc.vector.tensor_copy(
                picked_planes(first, PIECE)[:, 2, :], ld_middle[:, R : 2 * R].indirect(entries(ad_list, first, PIECE))
            )
        aside_first = (pieces[1], pieces[0], pieces[2], pieces[3])
        for t, table, share in ((0, ld_first, pieces[1:]), (3, ld_last, pieces), (1, ld_middle, aside_first)):
            for first in share:
                on_scalar(picked_planes(first, PIECE)[:, t, :], table[:], first)
        ld_woven = keep.tile([P, PIECE, PACK], F32, name="ld_woven")
        nc.vector.tensor_copy(ld_woven[:], ld_picked[1][:].rearrange("p t c -> p c t"))
        nc.sync.dma_start(w3_raw[:], w3.rearrange("(p j) c -> p j c", j=PACK))
        for r in range(4):
            nc.sync.dma_start(x_bytes[r:P:32, :].bitcast(I32), spread_bytes[8 * r : P : 32, :].bitcast(I32))
        nc.sync.dma_start(w2_raw[:], w2.rearrange("(p j) c -> p j c", j=PACK))
        nc.sync.dma_start(lb_table[:], lb)

        x_codes = {}

        def gather_words(codes, first):
            width = codes.shape[1]
            nc.vector.tensor_copy(codes[:], word_table[:].bitcast(U32).indirect(entries(token_list, first, width)))
            for col in range(0, width, PIECE):
                x_codes[first + col] = codes[:, col : col + PIECE]

        def picked_x(first, width):
            piece, col = divmod(first, PIECE)
            return x_codes[piece * PIECE][:, col : col + width], x_bytes[:, first : first + width]

        w1_codes = keep.tile([P, H], U32, name="w1_codes", align_bytes=64)
        w1_scales = keep.tile([P, H], U8, name="w1_scales", align_bytes=64)

        def round_w1(copy, rounded, half, pair):
            copy(
                rounded[:].rearrange("p (t m j) -> p m j t", t=PAIR, j=PACK),
                w1_raw[half][:].rearrange("p j (m t) -> p m j t", t=PACK)[:, :, :, PAIR * pair : PAIR * (pair + 1)],
            )

        def quantise_w1(rounded, half, pair):
            for u in range(PAIR):
                cols = slice((PAIR * pair + u) * P + half * SIDE, (PAIR * pair + u) * P + (half + 1) * SIDE)
                nc.vector.quantize_mx(
                    w1_codes[:, cols].bitcast(FP8X4), w1_scales[:, cols], rounded[:, u * HALF : (u + 1) * HALF]
                )

        w1_bf = {
            (half, pair): keep.tile([P, PAIR * HALF], BF16, name=f"w1_bf{half}{pair}", align_bytes=64)
            for half, pair in ((0, 0), (0, 1), (1, 0))
        }
        w1_bf[1, 1] = turns.tile([P, PAIR * HALF], BF16, name="w1_bf11", align_bytes=64, offset=0)

        gather_words(keep.tile([P, 2 * PIECE], U32, name="x_codes0", align_bytes=64), 0)
        gather_words(keep.tile([P, PIECE], U32, name="x_codes2", align_bytes=64), 2 * PIECE)
        round_w1(nc.scalar.copy, w1_bf[0, 0], 0, 0)
        round_w1(nc.scalar.copy, w1_bf[0, 1], 0, 1)
        quantise_w1(w1_bf[0, 0], 0, 0)

        def product(target, stationary, moving):
            nc.tensor.matmul_mx(
                target,
                lhsT=stationary[0].bitcast(FP8X4),
                lhsT_scale=stationary[1],
                rhs=moving[0].bitcast(FP8X4),
                rhs_scale=moving[1],
                start=True,
                stop=True,
            )

        def w1_plane(t):
            return w1_codes[:, t * P : (t + 1) * P], w1_scales[:, t * P : (t + 1) * P]

        warm_codes = keep.tile([P, P], U32, name="warm_codes", align_bytes=64)
        warm_scales = keep.tile([P, P], U8, name="warm_scales", align_bytes=64)
        nc.vector.quantize_mx(warm_codes[:].bitcast(FP8X4), warm_scales[:], w1_bf[0, 0][:])
        warm_bank = bank(7, [P, PACK, CHUNK], "warm_bank")
        for u in range(PACK):
            product(warm_bank[:, u, :], (warm_codes[:], warm_scales[:]), (warm_codes[:], warm_scales[:]))
        round_w1(nc.vector.tensor_copy, w1_bf[1, 0], 1, 0)
        round_w1(nc.scalar.copy, w1_bf[1, 1], 1, 1)
        quantise_w1(w1_bf[0, 1], 0, 1)
        quantise_w1(w1_bf[1, 0], 1, 0)
        quantise_w1(w1_bf[1, 1], 1, 1)
        gather_words(turns.tile([P, PIECE], U32, name="x_codes3", align_bytes=64, offset=0), 3 * PIECE)

        order = (0, 2, 1, 3, 4, 6, 5, 7)
        y = {c: bank(number, [P, PACK, CHUNK], f"y{c}") for number, c in enumerate(order)}

        def plane_of_y(c, t):
            product(y[c][:, t, :], w1_plane(t), picked_x(c * CHUNK, CHUNK))

        for t in range(PAIR):
            for c in order[:2]:
                plane_of_y(c, t)
        for c in order[:2]:
            for t in range(PAIR, PACK):
                plane_of_y(c, t)
        for c in order[2:]:
            for t in range(PACK):
                plane_of_y(c, t)

        h_bf = {u: keep.tile([P, PIECE * PACK], BF16, name=f"h_bf{u}", align_bytes=64) for u in (0, 2, 3)}
        h_bf[1] = turns.tile([P, PIECE * PACK], BF16, name="h_bf1", align_bytes=64, offset=26 * KIB)

        def in_pairs(planes):
            return planes.rearrange("p t (c i) -> p c t i", i=PAIR)

        def h_of(c):
            piece, col = divmod(c * CHUNK, PIECE)
            return h_bf[piece][:, col * PACK : (col + CHUNK) * PACK]

        def hidden(c):
            nc.vector.tensor_tensor(
                h_of(c).rearrange("p (c i t) -> p c t i", i=PAIR, t=PACK),
                in_pairs(y[c][:]),
                in_pairs(picked_planes(c * CHUNK, CHUNK)),
                MULT,
            )

        def hidden_aside(c, offset):
            y_woven = turns.tile([P, CHUNK, PACK], F32, name=f"y_woven{c}", offset=offset * KIB)
            nc.scalar.copy(y_woven[:], y[c][:].rearrange("p t c -> p c t"))
            col = c * CHUNK - PIECE
            nc.gpsimd.tensor_tensor(
                h_of(c),
                y_woven[:].rearrange("p c t -> p (c t)"),
                ld_woven[:, col : col + CHUNK, :].rearrange("p c t -> p (c t)"),
                MULT,
            )

        def rounded_weight(rounded, raw):
            nc.scalar.copy(
                rounded.rearrange("p (c i j) -> p c j i", i=RUN, j=PACK),
                raw[:].rearrange("p j (c i) -> p c j i", i=RUN),
            )
            return rounded

        def quantised(name, rounded, offset=None):
            width = rounded.shape[1] // PACK
            codes = keep.tile([P, width], U32, name=f"{name}_codes", align_bytes=64)
            if offset is None:
                scales = keep.tile([P, width], U8, name=f"{name}_scales", align_bytes=64)
            else:
                scales = turns.tile([P, width], U8, name=f"{name}_scales", align_bytes=64, offset=offset)
            nc.vector.quantize_mx(codes[:].bitcast(FP8X4), scales[:], rounded)
            return codes[:], scales[:]

        lb_picked = [
            turns.tile([P, PIECE], F32, name=f"lb_picked{u}", offset=offset * KIB)
            for u, offset in enumerate((22, 23, 23, 22))
        ]

        small_bf = keep.tile([P, N * PACK], BF16, name="small_bf", align_bytes=64)
        w3_quantised = quantised("w3", rounded_weight(small_bf[:], w3_raw))
        nc.gpsimd.tensor_scalar(
            small_bf[:].rearrange("p (c j) -> p c j", j=PACK), w2_raw[:].rearrange("p j c -> p c j"), 1.0, 0.0, MULT, ADD
        )
        hidden(0)
        hidden_aside(2, 2)
        on_scalar(lb_picked[0][:], lb_table[:], 0)
        hidden(1)
        hidden_aside(3, 20)
        on_scalar(lb_picked[2][:], lb_table[:], 2 * PIECE)
        hidden(4)
        hidden(6)
        hidden(5)
        hidden(7)

        turned, plain = (0, 2), (3, 1)
        ee_bank = bank(0, [P, 2, 2, N], "ee_bank")
        for g, piece in enumerate(turned):
            for c in range(2):
                product(ee_bank[:, g, c, :], picked_x(piece * PIECE + c * CHUNK, CHUNK), w3_quantised)
        lb_bank = bank(2, [P, 2, 2, N], "lb_bank")
        for g, piece in enumerate(turned):
            for c in range(2):
                nc.tensor.transpose(lb_bank[:, g, c, :], lb_picked[piece][:, c * CHUNK : (c + 1) * CHUNK], identity[:])
        ee_turned = keep.tile([P, 2, 2, N], F32, name="ee_turned")
        nc.scalar.copy(ee_turned[:], ee_bank[:])
        lb_turned = keep.tile([P, 2, 2, N], F32, name="lb_turned")
        nc.scalar.copy(lb_turned[:], lb_bank[:])
        for piece in plain:
            on_scalar(lb_picked[piece][:], lb_table[:], piece * PIECE)

        def turned_back(total, addend, opens):
            for c in range(2):
                nc.tensor.matmul(
                    total[:, c * CHUNK : (c + 1) * CHUNK],
                    lhsT=addend[:, c, :],
                    rhs=identity[:],
                    is_transpose=True,
                    start=opens and c == 0,
                    stop=not opens and c == 1,
                )

        w2_quantised = quantised("w2", small_bf[:], 12 * KIB + 512)
        h_quantised = {
            piece: quantised(f"h{piece}", h_bf[piece][:], offset)
            for piece, offset in ((0, 12 * KIB), (2, 12 * KIB + 256), (3, None), (1, None))
        }
        rr = {}
        totals = {}
        for g, piece in enumerate(turned):
            rr[piece] = bank(3 + g, [P, 2, N], f"rr{piece}")
            codes, scales = h_quantised[piece]
            for c in range(2):
                cols = slice(c * CHUNK, (c + 1) * CHUNK)
                product(rr[piece][:, c, :], (codes[:, cols], scales[:, cols]), w2_quantised)
        for g, piece in enumerate(plain):
            rr[piece] = bank(5 + g, [P, PIECE], f"rr{piece}")
            product(rr[piece][:], w2_quantised, h_quantised[piece])
        for g, piece in enumerate(turned):
            totals[piece] = bank(7 * g, [P, PIECE], f"total{piece}")
            turned_back(totals[piece], ee_turned[:, g, :, :], True)
        ee_plain = bank(1, [P, 2, PIECE], "ee_plain")
        for g, piece in enumerate(plain):
            product(ee_plain[:, g, :], w3_quantised, picked_x(piece * PIECE, PIECE))

        def finish(piece, total, queue):
            result = keep.tile([P, PIECE], F32, name=f"result{piece}")
            nc.scalar.activation(result[:], total, SILU)
            queue.dma_start(out[:, piece * PIECE : (piece + 1) * PIECE], result[:])

        held_terms = turns.tile([P, 3, PIECE], F32, name="held_terms", offset=26 * KIB)
        last_term = keep.tile([P, PIECE], F32, name="last_term")
        terms = {0: held_terms[:, 0, :], 2: held_terms[:, 1, :], 3: held_terms[:, 2, :], 1: last_term[:]}
        for g, piece in enumerate(turned):
            term = terms[piece].rearrange("p (c m) -> p c m", c=2)
            nc.vector.tensor_tensor(term, rr[piece][:], lb_turned[:, g, :, :], MULT)
            turned_back(totals[piece], term, False)
            finish(piece, totals[piece][:], nc.sync)
        for piece in plain:
            nc.vector.tensor_tensor(terms[piece], rr[piece][:], lb_picked[piece][:], MULT)
        for g, piece in enumerate(plain):
            total = keep.tile([P, PIECE], F32, name=f"sum{piece}")
            nc.vector.tensor_tensor(total[:], ee_plain[:, g, :], terms[piece], ADD)
            finish(piece, total[:], nc.scalar if g == 1 else nc.sync)
